import numpy as np
import ml_dtypes


def mxq(x, axis, fmt="e4m3"):
    dtype, down = {"e4m3": (ml_dtypes.float8_e4m3fn, 7), "e5m2": (ml_dtypes.float8_e5m2, 14)}[fmt]
    v = np.moveaxis(np.asarray(x, np.float32).astype(ml_dtypes.bfloat16).astype(np.float64), axis, -1)
    blocks = v.reshape(v.shape[:-1] + (-1, 32))
    amax = np.abs(blocks).max(-1, keepdims=True)
    byte = np.maximum(np.where(amax > 0, np.frexp(amax)[1] - 1 + 127, 0) - down, 1)
    scale = np.exp2(byte - 127.0)
    codes = (blocks / scale).astype(np.float32).astype(dtype).astype(np.float64)
    return np.moveaxis((codes * scale).reshape(v.shape), -1, axis)


WIDE = False


def mx_kscale(k):
    if not WIDE:
        return np.ones(k)
    levels = np.array([10, -10, 5, -5, 0])
    if k % 512:
        return np.exp2(np.random.permutation(np.resize(levels, k // 32))).repeat(32)
    a = np.empty((k // 512, 16))
    for p in range(k // 512):
        a[p, :8] = np.random.permutation(np.resize(levels, 8))
        for g in range(8):
            far = levels[np.abs(levels - a[p, g]) >= 10]
            a[p, g + 8] = far[np.random.randint(len(far))]
    return np.exp2(a.ravel()).repeat(32)


BF16 = ml_dtypes.bfloat16


def bf(x):
    return np.asarray(x, np.float32).astype(BF16)


def f64(x):
    return np.asarray(x).astype(np.float64)


T, S, Z, A = 2048, 2048, 512, 1024


def draw0():
    s = mx_kscale(S)
    t = mx_kscale(T)
    slopes = np.random.standard_normal((T, S)) * s
    recon = np.random.standard_normal((S, Z)) / np.sqrt(S) / s[:, None]
    gain = 1 + 0.1 * np.random.standard_normal(Z)
    frame_weight = (1 + 0.1 * np.random.standard_normal(T)) * t
    commands = np.random.standard_normal((T, A)) / np.sqrt(T) / t[:, None]
    return {"slopes": bf(slopes),
            "recon": bf(recon),
            "gain": bf(gain),
            "frame_weight": bf(frame_weight),
            "commands": bf(commands)}


def core(slopes, recon, gain, frame_weight, commands):
    modes = mxq(f64(slopes), 1, "e4m3") @ mxq(f64(recon), 0, "e4m3")
    h = np.tanh(modes * f64(gain)[None, :]) * f64(frame_weight)[:, None]
    return mxq(h, 0, "e4m3").T @ mxq(f64(commands), 0, "e4m3")


def e4m3fn_bytes(y):
    return np.clip(np.asarray(y, np.float64), -448.0, 448.0).astype(np.float32).astype(ml_dtypes.float8_e4m3fn).view(np.uint8)


def e4m3fn_values(b):
    return np.asarray(b, np.uint8).view(ml_dtypes.float8_e4m3fn).astype(np.float64)


def setup_inputs():
    d = draw0()
    x0 = np.asarray(d['slopes']).astype(np.float64)
    s = (np.max(np.abs(x0), axis=(0,), keepdims=True) / 448.0).astype(np.float32)
    out = {}
    for k, v in d.items():
        if k == 'slopes':
            out['slopes_bytes'] = e4m3fn_bytes(x0 / s.astype(np.float64))
            out['slopes_scale'] = s
        else:
            out[k] = v
    return out


def reference(slopes_bytes, slopes_scale, recon, gain, frame_weight, commands):
    return core(e4m3fn_values(slopes_bytes) * slopes_scale.astype(np.float64), recon, gain, frame_weight, commands)

@@ -1,0 +1,436 @@
+from contextlib import ExitStack
+
+import concourse.mybir as mybir
+from concourse.masks import make_identity
+
+F32 = mybir.dt.float32
+BF16 = mybir.dt.bfloat16
+U32 = mybir.dt.uint32
+U8 = mybir.dt.uint8
+E4M3 = mybir.dt.float8_e4m3fn
+E4M3X4 = mybir.dt.float8_e4m3fn_x4
+ADD = mybir.AluOpType.add
+MULT = mybir.AluOpType.mult
+TANH = mybir.ActivationFunctionType.Tanh
+
+T, S, Z, A = 2048, 2048, 512, 1024
+FLOPS = 2 * T * S * Z + 2 * T * Z * A
+
+P = 128
+J = 4
+PASSES = S // (P * J)
+HALF = S // 2
+UNIT = 2 * P
+UNITS = T // UNIT
+STEPS = 2 * UNITS
+LAST = UNITS - 1
+MODE_BLOCKS = Z // P
+COLS = 512
+PIECE = 256
+
+COMMAND_STEPS = (3, 3, 5, 6, 6, 7, 8, 8, 9, 9, 10, 11, 12, 13, 14, 15)
+COMMAND_BLOCKS_IN_STEPS = 5
+OPEN_STEPS = {9: 0, 13: 1}
+PARTIAL_STEPS = {12: ((2, 0), (2, 1)), 13: ((3, 0),), 15: ((3, 1),)}
+
+
+def stage1_steps():
+    steps = {}
+    for i in range(LAST * MODE_BLOCKS):
+        step = min(max(i // 2 + 3, i // MODE_BLOCKS + 4), STEPS - 1)
+        steps.setdefault(step, []).append(divmod(i, MODE_BLOCKS))
+    return steps
+
+
+def tile_modal_response_estimate_s7_kernel(
+    tc, slopes_bytes, slopes_scale, recon, gain, frame_weight, commands, out
+):
+    nc = tc.nc
+    scalar_copy = nc.scalar.copy
+    vector_copy = nc.vector.tensor_copy
+
+    bytes_view = slopes_bytes.rearrange("(g p t) s -> g p t s", p=P, t=J)
+    recon_view = recon.rearrange("(g p j) z -> g p j z", p=P, j=J)
+    commands_view = commands.rearrange("(g p j) a -> g p j a", p=P, j=J)
+
+    with ExitStack() as ctx:
+        once = ctx.enter_context(tc.tile_pool(name="once", bufs=1))
+        work = ctx.enter_context(tc.tile_pool(name="work", bufs=2))
+        psum = ctx.enter_context(tc.psum_pool(name="psum", bufs=1))
+        ctx.enter_context(tc.manual_schedule())
+
+        scale = once.tile([P, S], F32, name="scale")
+        ident = once.tile([P, P], F32, name="ident")
+        scale_rows = once.tile([P, P], F32, name="scale_rows")
+        scale_cols = once.tile([P, S // P], F32, name="scale_cols")
+        gain_rows = once.tile([P, P], BF16, name="gain_rows")
+        gain_rows32 = once.tile([P, P], F32, name="gain_rows32")
+        gain_cols = once.tile([P, MODE_BLOCKS], F32, name="gain_cols")
+        weight = once.tile([P, PASSES, J], BF16, name="weight")
+        warm = once.tile([P, 1], F32, name="warm")
+
+        recon_codes = once.tile([P, PASSES * Z], U32, name="recon_codes", align_bytes=64)
+        recon_sbytes = once.tile([P, PASSES * Z], U8, name="recon_sbytes", align_bytes=64)
+        com_codes = once.tile([P, PASSES * A], U32, name="com_codes", align_bytes=64)
+        com_sbytes = once.tile([P, PASSES * A], U8, name="com_sbytes", align_bytes=64)
+        h_codes = once.tile([P, PASSES * Z], U32, name="h_codes", align_bytes=64)
+        h_sbytes = once.tile([P, PASSES * Z], U8, name="h_sbytes", align_bytes=64)
+
+        byte_rows = {}
+        recon_raw = {}
+        recon_grouped = {}
+        com_raw = {}
+        com_grouped = {}
+        widened = {}
+        turned = {}
+        slopes_grouped = {}
+        slope_codes = {}
+        acc = {}
+        h_raw = {}
+        h_turned = {}
+        h_grouped = {}
+        resp = {}
+        partial = {}
+
+        def load_bytes(unit, halves=(0, 1), rows=(0, 1)):
+            g, pair = divmod(unit, 2)
+            k0 = halves[0] * HALF
+            k1 = k0 + len(halves) * HALF
+            t0 = 2 * pair + rows[0]
+            label = "bytes%d_%d_%d" % (unit, halves[0], rows[0])
+            row_bytes = once.tile([P, len(rows), k1 - k0], U8, name=label)
+            nc.sync.dma_start(out=row_bytes[:], in_=bytes_view[g][:, t0 : t0 + len(rows), k0:k1])
+            for i, row in enumerate(rows):
+                for half in halves:
+                    byte_rows[unit, half, row] = row_bytes[:, i, half * HALF - k0 : (half + 1) * HALF - k0]
+
+        def load_recon(g):
+            raw = work.tile([P, J, Z], BF16, name="recon_raw", bufs=4)
+            nc.sync.dma_start(out=raw[:], in_=recon_view[g])
+            recon_raw[g] = raw
+
+        def load_commands(g):
+            raw = work.tile([P, J, A], BF16, name="com_raw", bufs=2)
+            nc.sync.dma_start(out=raw[:], in_=commands_view[g])
+            com_raw[g] = raw
+
+        def turn_scales():
+            bank = psum.tile([P, P], F32, name="hturn0")
+            nc.tensor.transpose(bank[:], scale_rows[:], ident[:])
+            nc.vector.tensor_copy(out=scale_cols[:], in_=bank[:, 0 : S // P])
+
+        def spread_scales(bank_index, copy):
+            bank = psum.tile([P, 512], F32, name=("resp0", "resp1", "acc0", "acc1")[bank_index])
+            for i in range(4):
+                m = 4 * bank_index + i
+                nc.tensor.transpose(
+                    bank[:, i * P : (i + 1) * P], scale_cols[:, m : m + 1].to_broadcast([P, P]), ident[:]
+                )
+            copy(out=scale[:, bank_index * 512 : (bank_index + 1) * 512], in_=bank[:])
+
+        def interleave(copy, grouped, raw):
+            copy(
+                out=grouped.rearrange("p (c i j) -> p c j i", i=4, j=J),
+                in_=raw.rearrange("p j (c i) -> p c j i", i=4),
+            )
+
+        def interleave_recon(g, copy):
+            grouped = work.tile([P, J * Z], BF16, name="recon_grouped", bufs=2, align_bytes=64)
+            interleave(copy, grouped[:], recon_raw[g][:])
+            recon_grouped[g] = grouped
+
+        def quantize_recon(g):
+            nc.vector.quantize_mx(
+                out=recon_codes[:, g * Z : (g + 1) * Z].bitcast(E4M3X4),
+                scales=recon_sbytes[:, g * Z : (g + 1) * Z],
+                in_=recon_grouped[g][:],
+            )
+
+        def interleave_commands(piece):
+            block, part = divmod(piece, 2)
+            if part == 0:
+                com_grouped[block] = work.tile([P, J * COLS], BF16, name="com_grouped", bufs=4, align_bytes=64)
+            a0 = (piece % 4) * PIECE
+            interleave(
+                scalar_copy,
+                com_grouped[block][:, part * J * PIECE : (part + 1) * J * PIECE],
+                com_raw[block // 2][:, :, a0 : a0 + PIECE],
+            )
+
+        def quantize_commands(block):
+            nc.vector.quantize_mx(
+                out=com_codes[:, block * COLS : (block + 1) * COLS].bitcast(E4M3X4),
+                scales=com_sbytes[:, block * COLS : (block + 1) * COLS],
+                in_=com_grouped[block][:],
+            )
+
+        def widen(step):
+            unit, half = divmod(step, 2)
+            for row in range(2):
+                wide = work.tile([P, HALF], BF16, name="wide", bufs=5)
+                widened[step, row] = wide
+            pieces = 2 if step == 0 else 1
+            width = HALF // pieces
+            for i in range(pieces):
+                for row in range(2):
+                    k0 = half * HALF + i * width
+                    nc.vector.tensor_tensor(
+                        out=widened[step, row][:, i * width : (i + 1) * width],
+                        in0=byte_rows[unit, half, row][:, i * width : (i + 1) * width].bitcast(E4M3),
+                        in1=scale[:, k0 : k0 + width],
+                        op=MULT,
+                    )
+
+        def turn_slopes(step, row):
+            if row == 0:
+                turned[step] = [psum.tile([P, 2, UNIT], F32, name="turn%d" % b) for b in range(2)]
+            words = widened[step, row][:].bitcast(F32)
+            for b in range(2):
+                for w in range(2):
+                    nc.tensor.transpose(
+                        turned[step][b][:, w, row * P : (row + 1) * P],
+                        words[:, 256 * b + w : 256 * (b + 1) : 2],
+                        ident[:],
+                    )
+
+        def group_slopes(step, copies):
+            grouped = work.tile([P, 2 * UNIT * J], BF16, name="slopes_grouped", bufs=3, align_bytes=64)
+            words = grouped[:].bitcast(F32)
+            for b in range(2):
+                copies[b](
+                    out=words[:, 512 * b : 512 * (b + 1)].rearrange("p (r w) -> p r w", w=2),
+                    in_=turned[step][b][:].rearrange("p w r -> p r w"),
+                )
+            slopes_grouped[step] = grouped
+
+        def quantize_slopes(step):
+            unit, half = divmod(step, 2)
+            if half == 0:
+                slope_codes[unit] = (
+                    work.tile([P, PASSES * UNIT], U32, name="slope_codes", bufs=4, align_bytes=64),
+                    work.tile([P, PASSES * UNIT], U8, name="slope_sbytes", bufs=4, align_bytes=64),
+                )
+            codes, sbytes = slope_codes[unit]
+            cols = slice(half * 2 * UNIT, (half + 1) * 2 * UNIT)
+            nc.vector.quantize_mx(
+                out=codes[:, cols].bitcast(E4M3X4), scales=sbytes[:, cols], in_=slopes_grouped[step][:]
+            )
+
+        def stage1(unit, mb, bank_name):
+            bank = psum.tile([P, 2, UNIT], F32, name=bank_name)
+            codes, sbytes = slope_codes[unit]
+            for g in range(PASSES):
+                z0 = g * Z + mb * P
+                r0 = g * UNIT
+                nc.tensor.matmul_mx(
+                    out=bank[:, 0, :],
+                    lhsT=recon_codes[:, z0 : z0 + P].bitcast(E4M3X4),
+                    lhsT_scale=recon_sbytes[:, z0 : z0 + P],
+                    rhs=codes[:, r0 : r0 + UNIT].bitcast(E4M3X4),
+                    rhs_scale=sbytes[:, r0 : r0 + UNIT],
+                    start=(g == 0),
+                    stop=(g == PASSES - 1),
+                )
+            acc[unit, mb] = bank[:, 0, :]
+
+        def limit(unit, mb):
+            g, pair = divmod(unit, 2)
+            if pair == 0 and mb == 0:
+                h_raw[g] = work.tile([P, MODE_BLOCKS, J * P], F32, name="h_raw", bufs=2)
+            nc.scalar.activation(
+                out=h_raw[g][:, mb, pair * UNIT : (pair + 1) * UNIT],
+                in_=acc[unit, mb],
+                func=TANH,
+                scale=gain_cols[:, mb : mb + 1],
+            )
+
+        def turn_h(g, mb, bank_name):
+            bank = psum.tile([P, J * P], F32, name=bank_name)
+            for t in range(J):
+                nc.tensor.transpose(bank[:, t * P : (t + 1) * P], h_raw[g][:, mb, t * P : (t + 1) * P], ident[:])
+            h_turned[g, mb] = bank
+
+        def weigh_h(g, mb):
+            if mb == 0:
+                h_grouped[g] = work.tile([P, J * Z], BF16, name="h_grouped", bufs=2, align_bytes=64)
+            nc.vector.tensor_tensor(
+                out=h_grouped[g][:, mb * J * P : (mb + 1) * J * P].rearrange("p (z t) -> p z t", t=J),
+                in0=h_turned[g, mb][:].rearrange("p (t z) -> p z t", t=J),
+                in1=weight[:, g, :].unsqueeze(1).to_broadcast([P, P, J]),
+                op=MULT,
+            )
+
+        def quantize_h(g, mb, count):
+            cols = slice(g * Z + mb * P, g * Z + (mb + count) * P)
+            nc.vector.quantize_mx(
+                out=h_codes[:, cols].bitcast(E4M3X4),
+                scales=h_sbytes[:, cols],
+                in_=h_grouped[g][:, mb * J * P : (mb + count) * J * P],
+            )
+
+        def stage2(mb, half, groups, bank_name=None, last=PASSES - 1):
+            if bank_name:
+                resp[mb, half] = psum.tile([P, COLS], F32, name=bank_name)
+            for g in groups:
+                z0 = g * Z + mb * P
+                a0 = g * A + half * COLS
+                nc.tensor.matmul_mx(
+                    out=resp[mb, half][:],
+                    lhsT=h_codes[:, z0 : z0 + P].bitcast(E4M3X4),
+                    lhsT_scale=h_sbytes[:, z0 : z0 + P],
+                    rhs=com_codes[:, a0 : a0 + COLS].bitcast(E4M3X4),
+                    rhs_scale=com_sbytes[:, a0 : a0 + COLS],
+                    start=(bank_name is not None and g == groups[0]),
+                    stop=(g == last),
+                )
+
+        def keep_partial(mb, half):
+            part = once.tile([P, COLS], F32, name="partial%d_%d" % (mb, half))
+            nc.scalar.copy(out=part[:], in_=resp[mb, half][:])
+            partial[mb, half] = part
+
+        def store(mb, half):
+            result = work.tile([P, COLS], F32, name="result", bufs=8)
+            if (mb, half) in partial:
+                nc.vector.tensor_tensor(
+                    out=result[:], in0=resp[mb, half][:], in1=partial[mb, half][:], op=ADD
+                )
+            else:
+                nc.scalar.copy(out=result[:], in_=resp[mb, half][:])
+            nc.sync.dma_start(
+                out=out[mb * P : (mb + 1) * P, half * COLS : (half + 1) * COLS], in_=result[:]
+            )
+
+        nc.gpsimd.memset(scale_rows[:], 0.0)
+        nc.vector.memset(gain_rows[:], 0.0)
+        nc.gpsimd.memset(warm[:], 0.0)
+        make_identity(nc, ident[:])
+        nc.sync.dma_start(out=scale_rows[0 : S // P, :], in_=slopes_scale.rearrange("o (m n) -> (o m) n", n=P))
+        load_recon(0)
+        nc.sync.dma_start(out=gain_rows[0:MODE_BLOCKS, :], in_=gain.rearrange("(c p) -> c p", p=P))
+        load_bytes(0, (0,), (0,))
+        load_bytes(0, (0,), (1,))
+        load_bytes(0, (1,))
+        load_recon(1)
+        load_bytes(1)
+        load_recon(2)
+        load_recon(3)
+        nc.sync.dma_start(out=weight[:], in_=frame_weight.rearrange("(g p t) -> p g t", p=P, t=J))
+        load_bytes(2)
+        load_bytes(3)
+        load_commands(0)
+        load_bytes(4)
+        load_bytes(5)
+        load_commands(1)
+        load_bytes(6)
+        load_bytes(7)
+
+        nc.scalar.activation(out=warm[:], in_=warm[:], func=TANH)
+        turn_scales()
+        interleave_recon(0, vector_copy)
+        for bank_index in range(3):
+            spread_scales(bank_index, scalar_copy)
+        nc.scalar.copy(out=gain_rows32[:], in_=gain_rows[:])
+
+        stage1_blocks = stage1_steps()
+        h_blocks = {}
+        for step, blocks in stage1_blocks.items():
+            for unit, mb in blocks:
+                if unit % 2 == 1:
+                    h_blocks.setdefault(step + 1, []).append((unit // 2, mb))
+
+        for step in range(STEPS):
+            if step >= 1:
+                group_slopes(step - 1, (scalar_copy, scalar_copy))
+            for g, mb in h_blocks.get(step, []):
+                turn_h(g, mb, "hturn%d" % (mb % 2))
+            for piece, piece_step in enumerate(COMMAND_STEPS):
+                if piece_step == step:
+                    interleave_commands(piece)
+
+            blocks = stage1_blocks.get(step, [])
+            before = len(blocks) // 2
+            for unit, mb in blocks[:before]:
+                stage1(unit, mb, "acc%d" % (mb % 2))
+                limit(unit, mb)
+            if step in OPEN_STEPS:
+                g = OPEN_STEPS[step]
+                for half in range(2):
+                    stage2(0, half, (g,), "resp%d" % half if g == 0 else None)
+            for mb, half in PARTIAL_STEPS.get(step, ()):
+                stage2(mb, half, (0, 1), "hturn%d" % ((mb + half) % 2), last=1)
+                keep_partial(mb, half)
+            if step < PASSES - 1:
+                interleave_recon(step + 1, scalar_copy)
+
+            widen(step)
+            if step == 0:
+                spread_scales(3, vector_copy)
+            turn_slopes(step, 0)
+            for unit, mb in blocks[before:]:
+                stage1(unit, mb, "acc%d" % (mb % 2))
+                limit(unit, mb)
+            turn_slopes(step, 1)
+
+            for g, mb in h_blocks.get(step, []):
+                weigh_h(g, mb)
+            if step >= 1:
+                quantize_slopes(step - 1)
+            if step < PASSES:
+                quantize_recon(step)
+            for block in range(COMMAND_BLOCKS_IN_STEPS):
+                if COMMAND_STEPS[2 * block + 1] == step - 1:
+                    quantize_commands(block)
+            for g, mb in h_blocks.get(step, []):
+                if mb == MODE_BLOCKS - 1:
+                    quantize_h(g, 0, MODE_BLOCKS)
+
+            if step == 2:
+                gain_bank = psum.tile([P, P], F32, name="hturn0")
+                nc.tensor.transpose(gain_bank[:], gain_rows32[:], ident[:])
+            if step == 3:
+                nc.vector.tensor_copy(out=gain_cols[:], in_=gain_bank[:, 0:MODE_BLOCKS])
+            for g in (0, 1):
+                if step == COMMAND_STEPS[4 * g + 3]:
+                    load_commands(g + 2)
+
+        group_slopes(STEPS - 1, (scalar_copy, vector_copy))
+        quantize_slopes(STEPS - 1)
+        stage2(0, 0, (2,))
+        stage2(1, 0, (0, 1, 2), "hturn0")
+        for mb in range(3):
+            stage1(LAST, mb, "acc%d" % (mb % 2))
+            limit(LAST, mb)
+        for block in (6, 5, 7):
+            quantize_commands(block)
+        turn_h(3, 0, "turn0")
+        turn_h(3, 1, "turn1")
+        stage1(LAST, 3, "acc1")
+        limit(LAST, 3)
+        turn_h(3, 2, "acc0")
+        weigh_h(3, 0)
+
+        weigh_h(3, 1)
+        quantize_h(3, 0, 1)
+        stage2(0, 0, (3,))
+        stage2(0, 1, (2, 3))
+        turn_h(3, 3, "acc1")
+
+        weigh_h(3, 2)
+        quantize_h(3, 1, 1)
+        stage2(1, 1, (0, 1, 2), "hturn1")
+        for half in range(2):
+            stage2(1, half, (3,))
+
+        weigh_h(3, 3)
+        quantize_h(3, 2, 1)
+        for half in range(2):
+            stage2(2, half, (2, 3), "turn%d" % half)
+
+        quantize_h(3, 3, 1)
+        for half in range(2):
+            stage2(3, half, (2, 3), "acc%d" % half)
+
+        for mb in range(MODE_BLOCKS):
+            for half in range(2):
+                store(mb, half)

@@ -12,13 +12,14 @@ E4M3X4 = mybir.dt.float8_e4m3fn_x4
 ADD = mybir.AluOpType.add
 MULT = mybir.AluOpType.mult
 TANH = mybir.ActivationFunctionType.Tanh
+COPY = mybir.ActivationFunctionType.Copy
 
 T, S, Z, A = 2048, 2048, 512, 1024
 FLOPS = 2 * T * S * Z + 2 * T * Z * A
 
 P = 128
 J = 4
-PASSES = S // (P * J)
+PASSES = 4
 HALF = S // 2
 UNIT = 2 * P
 UNITS = T // UNIT
@@ -28,26 +29,13 @@ MODE_BLOCKS = Z // P
 COLS = 512
 PIECE = 256
 
-COMMAND_STEPS = (3, 3, 5, 6, 6, 7, 8, 8, 9, 9, 10, 11, 12, 13, 14, 15)
-COMMAND_BLOCKS_IN_STEPS = 5
-OPEN_STEPS = {9: 0, 13: 1}
-PARTIAL_STEPS = {12: ((2, 0), (2, 1)), 13: ((3, 0),), 15: ((3, 1),)}
-
-
-def stage1_steps():
-    steps = {}
-    for i in range(LAST * MODE_BLOCKS):
-        step = min(max(i // 2 + 3, i // MODE_BLOCKS + 4), STEPS - 1)
-        steps.setdefault(step, []).append(divmod(i, MODE_BLOCKS))
-    return steps
+TURN_BANKS = 4
 
 
 def tile_modal_response_estimate_s7_kernel(
     tc, slopes_bytes, slopes_scale, recon, gain, frame_weight, commands, out
 ):
     nc = tc.nc
-    scalar_copy = nc.scalar.copy
-    vector_copy = nc.vector.tensor_copy
 
     bytes_view = slopes_bytes.rearrange("(g p t) s -> g p t s", p=P, t=J)
     recon_view = recon.rearrange("(g p j) z -> g p j z", p=P, j=J)
@@ -59,15 +47,12 @@ def tile_modal_response_estimate_s7_kernel(
         psum = ctx.enter_context(tc.psum_pool(name="psum", bufs=1))
         ctx.enter_context(tc.manual_schedule())
 
-        scale = once.tile([P, S], F32, name="scale")
+        scale = once.tile([P, PASSES, J], F32, name="scale")
         ident = once.tile([P, P], F32, name="ident")
-        scale_rows = once.tile([P, P], F32, name="scale_rows")
-        scale_cols = once.tile([P, S // P], F32, name="scale_cols")
         gain_rows = once.tile([P, P], BF16, name="gain_rows")
         gain_rows32 = once.tile([P, P], F32, name="gain_rows32")
         gain_cols = once.tile([P, MODE_BLOCKS], F32, name="gain_cols")
         weight = once.tile([P, PASSES, J], BF16, name="weight")
-        warm = once.tile([P, 1], F32, name="warm")
 
         recon_codes = once.tile([P, PASSES * Z], U32, name="recon_codes", align_bytes=64)
         recon_sbytes = once.tile([P, PASSES * Z], U8, name="recon_sbytes", align_bytes=64)
@@ -90,155 +75,137 @@ def tile_modal_response_estimate_s7_kernel(
         h_turned = {}
         h_grouped = {}
         resp = {}
-        partial = {}
 
-        def load_bytes(unit, halves=(0, 1), rows=(0, 1)):
+        def scalar_move(out, in_):
+            nc.scalar.copy(out=out, in_=in_)
+
+        def gpsimd_move(out, in_):
+            nc.gpsimd.tensor_scalar(out=out, in0=in_, scalar1=1.0, scalar2=0.0, op0=MULT, op1=ADD)
+
+        def vector_move(out, in_):
+            nc.vector.tensor_copy(out=out, in_=in_)
+
+        def load_bytes(unit, halves):
             g, pair = divmod(unit, 2)
             k0 = halves[0] * HALF
             k1 = k0 + len(halves) * HALF
-            t0 = 2 * pair + rows[0]
-            label = "bytes%d_%d_%d" % (unit, halves[0], rows[0])
-            row_bytes = once.tile([P, len(rows), k1 - k0], U8, name=label)
-            nc.sync.dma_start(out=row_bytes[:], in_=bytes_view[g][:, t0 : t0 + len(rows), k0:k1])
-            for i, row in enumerate(rows):
-                for half in halves:
-                    byte_rows[unit, half, row] = row_bytes[:, i, half * HALF - k0 : (half + 1) * HALF - k0]
-
-        def load_recon(g):
-            raw = work.tile([P, J, Z], BF16, name="recon_raw", bufs=4)
-            nc.sync.dma_start(out=raw[:], in_=recon_view[g])
-            recon_raw[g] = raw
-
-        def load_commands(g):
-            raw = work.tile([P, J, A], BF16, name="com_raw", bufs=2)
-            nc.sync.dma_start(out=raw[:], in_=commands_view[g])
-            com_raw[g] = raw
-
-        def turn_scales():
-            bank = psum.tile([P, P], F32, name="hturn0")
-            nc.tensor.transpose(bank[:], scale_rows[:], ident[:])
-            nc.vector.tensor_copy(out=scale_cols[:], in_=bank[:, 0 : S // P])
-
-        def spread_scales(bank_index, copy):
-            bank = psum.tile([P, 512], F32, name=("resp0", "resp1", "acc0", "acc1")[bank_index])
-            for i in range(4):
-                m = 4 * bank_index + i
-                nc.tensor.transpose(
-                    bank[:, i * P : (i + 1) * P], scale_cols[:, m : m + 1].to_broadcast([P, P]), ident[:]
-                )
-            copy(out=scale[:, bank_index * 512 : (bank_index + 1) * 512], in_=bank[:])
-
-        def interleave(copy, grouped, raw):
-            copy(
-                out=grouped.rearrange("p (c i j) -> p c j i", i=4, j=J),
-                in_=raw.rearrange("p j (c i) -> p c j i", i=4),
-            )
-
-        def interleave_recon(g, copy):
-            grouped = work.tile([P, J * Z], BF16, name="recon_grouped", bufs=2, align_bytes=64)
-            interleave(copy, grouped[:], recon_raw[g][:])
-            recon_grouped[g] = grouped
-
-        def quantize_recon(g):
-            nc.vector.quantize_mx(
-                out=recon_codes[:, g * Z : (g + 1) * Z].bitcast(E4M3X4),
-                scales=recon_sbytes[:, g * Z : (g + 1) * Z],
-                in_=recon_grouped[g][:],
-            )
-
-        def interleave_commands(piece):
-            block, part = divmod(piece, 2)
-            if part == 0:
-                com_grouped[block] = work.tile([P, J * COLS], BF16, name="com_grouped", bufs=4, align_bytes=64)
-            a0 = (piece % 4) * PIECE
-            interleave(
-                scalar_copy,
-                com_grouped[block][:, part * J * PIECE : (part + 1) * J * PIECE],
-                com_raw[block // 2][:, :, a0 : a0 + PIECE],
-            )
-
-        def quantize_commands(block):
-            nc.vector.quantize_mx(
-                out=com_codes[:, block * COLS : (block + 1) * COLS].bitcast(E4M3X4),
-                scales=com_sbytes[:, block * COLS : (block + 1) * COLS],
-                in_=com_grouped[block][:],
-            )
-
-        def widen(step):
-            unit, half = divmod(step, 2)
+            row_bytes = work.tile([P, 2, k1 - k0], U8, name="row_bytes", bufs=5)
+            nc.sync.dma_start(out=row_bytes[:], in_=bytes_view[g][:, 2 * pair : 2 * pair + 2, k0:k1])
             for row in range(2):
-                wide = work.tile([P, HALF], BF16, name="wide", bufs=5)
-                widened[step, row] = wide
-            pieces = 2 if step == 0 else 1
-            width = HALF // pieces
-            for i in range(pieces):
-                for row in range(2):
-                    k0 = half * HALF + i * width
-                    nc.vector.tensor_tensor(
-                        out=widened[step, row][:, i * width : (i + 1) * width],
-                        in0=byte_rows[unit, half, row][:, i * width : (i + 1) * width].bitcast(E4M3),
-                        in1=scale[:, k0 : k0 + width],
-                        op=MULT,
-                    )
+                for half in halves:
+                    byte_rows[unit, half, row] = row_bytes[:, row, half * HALF - k0 : (half + 1) * HALF - k0]
 
-        def turn_slopes(step, row):
-            if row == 0:
-                turned[step] = [psum.tile([P, 2, UNIT], F32, name="turn%d" % b) for b in range(2)]
-            words = widened[step, row][:].bitcast(F32)
-            for b in range(2):
+        def load_recon(g, parts):
+            z0 = parts[0] * PIECE
+            raw = once.tile([P, J, len(parts) * PIECE], BF16, name="recon_raw%d_%d" % (g, parts[0]))
+            nc.sync.dma_start(out=raw[:], in_=recon_view[g][:, :, z0 : z0 + len(parts) * PIECE])
+            for i, part in enumerate(parts):
+                recon_raw[g, part] = raw[:, :, i * PIECE : (i + 1) * PIECE]
+
+        def load_commands(g, half):
+            raw = work.tile([P, J, COLS], BF16, name="com_raw", bufs=4)
+            nc.sync.dma_start(out=raw[:], in_=commands_view[g][:, :, half * COLS : (half + 1) * COLS])
+            com_raw[g, half] = raw
+
+        def interleave(move, grouped, raw):
+            move(
+                grouped.rearrange("p (c i j) -> p c j i", i=4, j=J),
+                raw.rearrange("p j (c i) -> p c j i", i=4),
+            )
+
+        def interleave_recon(g, part, move, name):
+            grouped = once.tile([P, J * PIECE], BF16, name=name, align_bytes=64)
+            interleave(move, grouped[:], recon_raw[g, part])
+            recon_grouped[g, part] = grouped
+
+        def quantize_recon(g, part):
+            cols = slice(g * Z + part * PIECE, g * Z + (part + 1) * PIECE)
+            nc.vector.quantize_mx(
+                out=recon_codes[:, cols].bitcast(E4M3X4), scales=recon_sbytes[:, cols], in_=recon_grouped[g, part][:]
+            )
+
+        def interleave_commands(g, half, part, move, name):
+            grouped = once.tile([P, J * PIECE], BF16, name=name, align_bytes=64)
+            interleave(move, grouped[:], com_raw[g, half][:, :, part * PIECE : (part + 1) * PIECE])
+            com_grouped[g, half, part] = grouped
+
+        def quantize_commands(g, half):
+            for part in range(2):
+                a0 = g * A + half * COLS + part * PIECE
+                nc.vector.quantize_mx(
+                    out=com_codes[:, a0 : a0 + PIECE].bitcast(E4M3X4),
+                    scales=com_sbytes[:, a0 : a0 + PIECE],
+                    in_=com_grouped[g, half, part][:],
+                )
+
+        def widen(step, row):
+            unit, half = divmod(step, 2)
+            wide = work.tile([P, HALF], BF16, name="wide", bufs=8)
+            widened[step, row] = wide
+            nc.scalar.copy(out=wide[:], in_=byte_rows[unit, half, row].bitcast(E4M3))
+
+        def turn_slopes(step, b):
+            bank = psum.tile([P, 2, UNIT], F32, name="turn%d" % ((2 * step + b) % TURN_BANKS))
+            turned[step, b] = bank
+            for row in range(2):
+                words = widened[step, row][:].bitcast(F32)
                 for w in range(2):
                     nc.tensor.transpose(
-                        turned[step][b][:, w, row * P : (row + 1) * P],
-                        words[:, 256 * b + w : 256 * (b + 1) : 2],
-                        ident[:],
+                        bank[:, w, row * P : (row + 1) * P], words[:, 256 * b + w : 256 * (b + 1) : 2], ident[:]
                     )
 
-        def group_slopes(step, copies):
-            grouped = work.tile([P, 2 * UNIT * J], BF16, name="slopes_grouped", bufs=3, align_bytes=64)
-            words = grouped[:].bitcast(F32)
-            for b in range(2):
-                copies[b](
-                    out=words[:, 512 * b : 512 * (b + 1)].rearrange("p (r w) -> p r w", w=2),
-                    in_=turned[step][b][:].rearrange("p w r -> p r w"),
-                )
-            slopes_grouped[step] = grouped
-
-        def quantize_slopes(step):
-            unit, half = divmod(step, 2)
-            if half == 0:
-                slope_codes[unit] = (
-                    work.tile([P, PASSES * UNIT], U32, name="slope_codes", bufs=4, align_bytes=64),
-                    work.tile([P, PASSES * UNIT], U8, name="slope_sbytes", bufs=4, align_bytes=64),
-                )
-            codes, sbytes = slope_codes[unit]
-            cols = slice(half * 2 * UNIT, (half + 1) * 2 * UNIT)
-            nc.vector.quantize_mx(
-                out=codes[:, cols].bitcast(E4M3X4), scales=sbytes[:, cols], in_=slopes_grouped[step][:]
+        def scale_slopes(step, b):
+            if b == 0:
+                grouped = work.tile([P, UNIT * J], BF16, name="slopes_grouped", bufs=2, align_bytes=64)
+            else:
+                grouped = once.tile([P, UNIT * J], BF16, name="shared%d" % step, align_bytes=64)
+            slopes_grouped[step, b] = grouped
+            g = 2 * (step % 2) + b
+            values = turned[step, b][:].rearrange("p w r -> p (w r)").bitcast(BF16)
+            nc.vector.tensor_tensor(
+                out=grouped[:].rearrange("p (r w e) -> p r w e", w=2, e=2),
+                in0=values.rearrange("p (w r e) -> p r w e", w=2, e=2),
+                in1=scale[:, g, :].rearrange("p (w e) -> p w e", e=2).unsqueeze(1).to_broadcast([P, UNIT, 2, 2]),
+                op=MULT,
             )
 
-        def stage1(unit, mb, bank_name):
+        def quantize_slopes(step, b):
+            unit, half = divmod(step, 2)
+            if half == 0 and b == 0:
+                slope_codes[unit] = (
+                    work.tile([P, PASSES * UNIT], U32, name="slope_codes", bufs=3, align_bytes=64),
+                    work.tile([P, PASSES * UNIT], U8, name="slope_sbytes", bufs=3, align_bytes=64),
+                )
+            codes, sbytes = slope_codes[unit]
+            cols = slice((2 * half + b) * UNIT, (2 * half + b + 1) * UNIT)
+            nc.vector.quantize_mx(
+                out=codes[:, cols].bitcast(E4M3X4), scales=sbytes[:, cols], in_=slopes_grouped[step, b][:]
+            )
+
+        def stage1(unit, blocks, bank_name):
             bank = psum.tile([P, 2, UNIT], F32, name=bank_name)
             codes, sbytes = slope_codes[unit]
-            for g in range(PASSES):
-                z0 = g * Z + mb * P
-                r0 = g * UNIT
-                nc.tensor.matmul_mx(
-                    out=bank[:, 0, :],
-                    lhsT=recon_codes[:, z0 : z0 + P].bitcast(E4M3X4),
-                    lhsT_scale=recon_sbytes[:, z0 : z0 + P],
-                    rhs=codes[:, r0 : r0 + UNIT].bitcast(E4M3X4),
-                    rhs_scale=sbytes[:, r0 : r0 + UNIT],
-                    start=(g == 0),
-                    stop=(g == PASSES - 1),
-                )
-            acc[unit, mb] = bank[:, 0, :]
+            for i, mb in enumerate(blocks):
+                for g in range(PASSES):
+                    z0 = g * Z + mb * P
+                    r0 = g * UNIT
+                    nc.tensor.matmul_mx(
+                        out=bank[:, i, :],
+                        lhsT=recon_codes[:, z0 : z0 + P].bitcast(E4M3X4),
+                        lhsT_scale=recon_sbytes[:, z0 : z0 + P],
+                        rhs=codes[:, r0 : r0 + UNIT].bitcast(E4M3X4),
+                        rhs_scale=sbytes[:, r0 : r0 + UNIT],
+                        start=(g == 0),
+                        stop=(g == PASSES - 1),
+                    )
+                acc[unit, mb] = bank[:, i, :]
 
         def limit(unit, mb):
             g, pair = divmod(unit, 2)
-            if pair == 0 and mb == 0:
-                h_raw[g] = work.tile([P, MODE_BLOCKS, J * P], F32, name="h_raw", bufs=2)
+            if pair == 0:
+                h_raw[g, mb] = once.tile([P, J * P], F32, name="h_raw%d_%d" % (g, mb))
             nc.scalar.activation(
-                out=h_raw[g][:, mb, pair * UNIT : (pair + 1) * UNIT],
+                out=h_raw[g, mb][:, pair * UNIT : (pair + 1) * UNIT],
                 in_=acc[unit, mb],
                 func=TANH,
                 scale=gain_cols[:, mb : mb + 1],
@@ -247,28 +214,25 @@ def tile_modal_response_estimate_s7_kernel(
         def turn_h(g, mb, bank_name):
             bank = psum.tile([P, J * P], F32, name=bank_name)
             for t in range(J):
-                nc.tensor.transpose(bank[:, t * P : (t + 1) * P], h_raw[g][:, mb, t * P : (t + 1) * P], ident[:])
+                nc.tensor.transpose(bank[:, t * P : (t + 1) * P], h_raw[g, mb][:, t * P : (t + 1) * P], ident[:])
             h_turned[g, mb] = bank
 
         def weigh_h(g, mb):
-            if mb == 0:
-                h_grouped[g] = work.tile([P, J * Z], BF16, name="h_grouped", bufs=2, align_bytes=64)
+            h_grouped[g, mb] = work.tile([P, J * P], BF16, name="h_grouped", bufs=6, align_bytes=64)
             nc.vector.tensor_tensor(
-                out=h_grouped[g][:, mb * J * P : (mb + 1) * J * P].rearrange("p (z t) -> p z t", t=J),
+                out=h_grouped[g, mb][:].rearrange("p (z t) -> p z t", t=J),
                 in0=h_turned[g, mb][:].rearrange("p (t z) -> p z t", t=J),
                 in1=weight[:, g, :].unsqueeze(1).to_broadcast([P, P, J]),
                 op=MULT,
             )
 
-        def quantize_h(g, mb, count):
-            cols = slice(g * Z + mb * P, g * Z + (mb + count) * P)
+        def quantize_h(g, mb):
+            cols = slice(g * Z + mb * P, g * Z + (mb + 1) * P)
             nc.vector.quantize_mx(
-                out=h_codes[:, cols].bitcast(E4M3X4),
-                scales=h_sbytes[:, cols],
-                in_=h_grouped[g][:, mb * J * P : (mb + count) * J * P],
+                out=h_codes[:, cols].bitcast(E4M3X4), scales=h_sbytes[:, cols], in_=h_grouped[g, mb][:]
             )
 
-        def stage2(mb, half, groups, bank_name=None, last=PASSES - 1):
+        def stage2(mb, half, groups, bank_name=None):
             if bank_name:
                 resp[mb, half] = psum.tile([P, COLS], F32, name=bank_name)
             for g in groups:
@@ -280,157 +244,172 @@ def tile_modal_response_estimate_s7_kernel(
                     lhsT_scale=h_sbytes[:, z0 : z0 + P],
                     rhs=com_codes[:, a0 : a0 + COLS].bitcast(E4M3X4),
                     rhs_scale=com_sbytes[:, a0 : a0 + COLS],
-                    start=(bank_name is not None and g == groups[0]),
-                    stop=(g == last),
+                    start=(g == 0),
+                    stop=(g == PASSES - 1),
                 )
 
-        def keep_partial(mb, half):
-            part = once.tile([P, COLS], F32, name="partial%d_%d" % (mb, half))
-            nc.scalar.copy(out=part[:], in_=resp[mb, half][:])
-            partial[mb, half] = part
+        def store(mb, half, move):
+            result = work.tile([P, COLS], F32, name="result", bufs=6)
+            move(result[:], resp[mb, half][:])
+            nc.sync.dma_start(out=out[mb * P : (mb + 1) * P, half * COLS : (half + 1) * COLS], in_=result[:])
 
-        def store(mb, half):
-            result = work.tile([P, COLS], F32, name="result", bufs=8)
-            if (mb, half) in partial:
-                nc.vector.tensor_tensor(
-                    out=result[:], in0=resp[mb, half][:], in1=partial[mb, half][:], op=ADD
-                )
-            else:
-                nc.scalar.copy(out=result[:], in_=resp[mb, half][:])
-            nc.sync.dma_start(
-                out=out[mb * P : (mb + 1) * P, half * COLS : (half + 1) * COLS], in_=result[:]
-            )
-
-        nc.gpsimd.memset(scale_rows[:], 0.0)
-        nc.vector.memset(gain_rows[:], 0.0)
-        nc.gpsimd.memset(warm[:], 0.0)
+        nc.gpsimd.memset(gain_rows[:], 0.0)
         make_identity(nc, ident[:])
-        nc.sync.dma_start(out=scale_rows[0 : S // P, :], in_=slopes_scale.rearrange("o (m n) -> (o m) n", n=P))
-        load_recon(0)
-        nc.sync.dma_start(out=gain_rows[0:MODE_BLOCKS, :], in_=gain.rearrange("(c p) -> c p", p=P))
-        load_bytes(0, (0,), (0,))
-        load_bytes(0, (0,), (1,))
+        nc.scalar.dma_start(out=scale[:], in_=slopes_scale.rearrange("o (g p j) -> p (o g) j", p=P, j=J))
+        load_bytes(0, (0,))
+        load_recon(0, (0,))
+        load_recon(0, (1,))
         load_bytes(0, (1,))
-        load_recon(1)
-        load_bytes(1)
-        load_recon(2)
-        load_recon(3)
+        load_recon(1, (0, 1))
+        load_bytes(1, (0,))
+        load_recon(2, (0, 1))
+        load_recon(3, (0, 1))
+        load_bytes(1, (1,))
+        nc.sync.dma_start(out=gain_rows[0:MODE_BLOCKS, :], in_=gain.rearrange("(c p) -> c p", p=P))
+        load_commands(0, 0)
+        load_bytes(2, (0, 1))
         nc.sync.dma_start(out=weight[:], in_=frame_weight.rearrange("(g p t) -> p g t", p=P, t=J))
-        load_bytes(2)
-        load_bytes(3)
-        load_commands(0)
-        load_bytes(4)
-        load_bytes(5)
-        load_commands(1)
-        load_bytes(6)
-        load_bytes(7)
+        load_commands(0, 1)
+        load_commands(1, 0)
+        load_commands(1, 1)
 
-        nc.scalar.activation(out=warm[:], in_=warm[:], func=TANH)
-        turn_scales()
-        interleave_recon(0, vector_copy)
-        for bank_index in range(3):
-            spread_scales(bank_index, scalar_copy)
-        nc.scalar.copy(out=gain_rows32[:], in_=gain_rows[:])
+        widen(0, 0)
+        widen(0, 1)
+        turn_slopes(0, 0)
+        turn_slopes(0, 1)
+        interleave_recon(0, 0, vector_move, "shared2")
+        interleave_recon(0, 1, vector_move, "shared3")
+        quantize_recon(0, 0)
+        widen(1, 0)
+        widen(1, 1)
+        turn_slopes(1, 0)
+        turn_slopes(1, 1)
+        interleave_recon(1, 0, gpsimd_move, "shared4")
+        interleave_recon(1, 1, scalar_move, "shared5")
+        widen(2, 0)
+        widen(2, 1)
+        interleave_recon(2, 1, scalar_move, "shared6")
+        interleave_recon(3, 0, scalar_move, "shared7")
+        interleave_recon(3, 1, scalar_move, "shared8")
 
-        stage1_blocks = stage1_steps()
-        h_blocks = {}
-        for step, blocks in stage1_blocks.items():
-            for unit, mb in blocks:
-                if unit % 2 == 1:
-                    h_blocks.setdefault(step + 1, []).append((unit // 2, mb))
+        pairs = [(u, mb) for u in range(UNITS) for mb in (0, 2)]
+        stage1_steps = {i + 2: pair for i, pair in enumerate(pairs)}
+        pieces = [(g, half, part) for g in range(PASSES) for half in range(2) for part in range(2)]
+        FIRST_PIECE = 1
+
+        def stage1_step(step):
+            unit, mb = stage1_steps[step]
+            stage1(unit, (mb, mb + 1), "acc%d" % (step % 2))
+            limit(unit, mb)
+            limit(unit, mb + 1)
+
+        def piece_done(g, half, part):
+            if part == 1 and g < 2:
+                load_commands(g + 2, half)
 
         for step in range(STEPS):
-            if step >= 1:
-                group_slopes(step - 1, (scalar_copy, scalar_copy))
-            for g, mb in h_blocks.get(step, []):
-                turn_h(g, mb, "hturn%d" % (mb % 2))
-            for piece, piece_step in enumerate(COMMAND_STEPS):
-                if piece_step == step:
-                    interleave_commands(piece)
-
-            blocks = stage1_blocks.get(step, [])
-            before = len(blocks) // 2
-            for unit, mb in blocks[:before]:
-                stage1(unit, mb, "acc%d" % (mb % 2))
-                limit(unit, mb)
-            if step in OPEN_STEPS:
-                g = OPEN_STEPS[step]
-                for half in range(2):
-                    stage2(0, half, (g,), "resp%d" % half if g == 0 else None)
-            for mb, half in PARTIAL_STEPS.get(step, ()):
-                stage2(mb, half, (0, 1), "hturn%d" % ((mb + half) % 2), last=1)
-                keep_partial(mb, half)
-            if step < PASSES - 1:
-                interleave_recon(step + 1, scalar_copy)
-
-            widen(step)
-            if step == 0:
-                spread_scales(3, vector_copy)
-            turn_slopes(step, 0)
-            for unit, mb in blocks[before:]:
-                stage1(unit, mb, "acc%d" % (mb % 2))
-                limit(unit, mb)
-            turn_slopes(step, 1)
-
-            for g, mb in h_blocks.get(step, []):
-                weigh_h(g, mb)
-            if step >= 1:
-                quantize_slopes(step - 1)
-            if step < PASSES:
-                quantize_recon(step)
-            for block in range(COMMAND_BLOCKS_IN_STEPS):
-                if COMMAND_STEPS[2 * block + 1] == step - 1:
-                    quantize_commands(block)
-            for g, mb in h_blocks.get(step, []):
-                if mb == MODE_BLOCKS - 1:
-                    quantize_h(g, 0, MODE_BLOCKS)
-
-            if step == 2:
-                gain_bank = psum.tile([P, P], F32, name="hturn0")
+            if step % 2 == 0 and step // 2 + 3 < UNITS:
+                load_bytes(step // 2 + 3, (0, 1))
+            scale_slopes(step, 0)
+            scale_slopes(step, 1)
+            if step == 1:
+                nc.scalar.copy(out=gain_rows32[:], in_=gain_rows[:])
+                gain_bank = psum.tile([P, P], F32, name="h0")
                 nc.tensor.transpose(gain_bank[:], gain_rows32[:], ident[:])
-            if step == 3:
-                nc.vector.tensor_copy(out=gain_cols[:], in_=gain_bank[:, 0:MODE_BLOCKS])
-            for g in (0, 1):
-                if step == COMMAND_STEPS[4 * g + 3]:
-                    load_commands(g + 2)
+            if step + 3 < STEPS:
+                widen(step + 3, 0)
+                widen(step + 3, 1)
+            if step == 1:
+                nc.scalar.copy(out=gain_cols[:], in_=gain_bank[:, 0:MODE_BLOCKS])
+            if step in stage1_steps:
+                stage1_step(step)
+            if step < STEPS - 2:
+                turn_slopes(step + 2, 0)
+                turn_slopes(step + 2, 1)
+            if step == STEPS - 2:
+                turn_h(0, 0, "h0")
+                turn_h(0, 1, "h1")
+            if step == STEPS - 1:
+                turn_h(1, 0, "turn0")
+                turn_h(1, 1, "turn1")
+            quantize_slopes(step, 0)
+            if step == 0:
+                quantize_recon(0, 1)
+            if step == 1:
+                for g in (1, 2, 3):
+                    quantize_recon(g, 0)
+                    quantize_recon(g, 1)
+            quantize_slopes(step, 1)
+            if step == 0:
+                interleave_recon(2, 0, gpsimd_move, "shared0")
+            if step >= FIRST_PIECE:
+                piece = pieces[step - FIRST_PIECE]
+                interleave_commands(*piece, gpsimd_move, "shared%d" % step)
+                piece_done(*piece)
+            if step == 13:
+                interleave_commands(*pieces[15], scalar_move, "shared0")
 
-        group_slopes(STEPS - 1, (scalar_copy, vector_copy))
-        quantize_slopes(STEPS - 1)
-        stage2(0, 0, (2,))
-        stage2(1, 0, (0, 1, 2), "hturn0")
-        for mb in range(3):
-            stage1(LAST, mb, "acc%d" % (mb % 2))
-            limit(LAST, mb)
-        for block in (6, 5, 7):
-            quantize_commands(block)
-        turn_h(3, 0, "turn0")
-        turn_h(3, 1, "turn1")
-        stage1(LAST, 3, "acc1")
-        limit(LAST, 3)
-        turn_h(3, 2, "acc0")
-        weigh_h(3, 0)
+        banks = {0: ("turn2", "turn3"), 1: ("turn0", "turn1"), 2: ("h0", "h1"), 3: ("turn0", "turn1")}
 
-        weigh_h(3, 1)
-        quantize_h(3, 0, 1)
-        stage2(0, 0, (3,))
-        stage2(0, 1, (2, 3))
-        turn_h(3, 3, "acc1")
-
-        weigh_h(3, 2)
-        quantize_h(3, 1, 1)
-        stage2(1, 1, (0, 1, 2), "hturn1")
-        for half in range(2):
-            stage2(1, half, (3,))
-
-        weigh_h(3, 3)
-        quantize_h(3, 2, 1)
-        for half in range(2):
-            stage2(2, half, (2, 3), "turn%d" % half)
-
-        quantize_h(3, 3, 1)
-        for half in range(2):
-            stage2(3, half, (2, 3), "acc%d" % half)
-
-        for mb in range(MODE_BLOCKS):
+        def passes(g, mb):
             for half in range(2):
-                store(mb, half)
+                stage2(mb, half, (g,), banks[mb][half] if g == 0 else None)
+
+        stage1_step(16)
+        stage1_step(17)
+        weigh_h(0, 0)
+        weigh_h(0, 1)
+        weigh_h(1, 0)
+        weigh_h(1, 1)
+        turn_h(2, 0, "h0")
+        turn_h(2, 1, "h1")
+        ahead = {
+            1: ((3, 0, "acc0"), (3, 1, "acc1")),
+            2: ((0, 2, "h0"), (1, 2, "h1")),
+            3: ((2, 2, "acc0"), (3, 2, "acc1")),
+        }
+        for g in range(PASSES):
+            if g >= 2:
+                weigh_h(g, 0)
+                weigh_h(g, 1)
+            quantize_h(g, 0)
+            quantize_commands(g, 0)
+            quantize_h(g, 1)
+            quantize_commands(g, 1)
+            for block in ahead.get(g, ()):
+                turn_h(*block)
+            passes(g, 0)
+            passes(g, 1)
+        for mb in range(2):
+            store(mb, 0, scalar_move)
+            store(mb, 1, scalar_move)
+        weigh_h(0, 2)
+        weigh_h(1, 2)
+        quantize_h(0, 2)
+        weigh_h(2, 2)
+        quantize_h(1, 2)
+        weigh_h(3, 2)
+        quantize_h(2, 2)
+        turn_h(0, 3, "turn2")
+        turn_h(1, 3, "turn3")
+        passes(0, 2)
+        passes(1, 2)
+        weigh_h(0, 3)
+        quantize_h(3, 2)
+        turn_h(2, 3, "acc0")
+        turn_h(3, 3, "acc1")
+        passes(2, 2)
+        passes(3, 2)
+        store(2, 0, scalar_move)
+        store(2, 1, scalar_move)
+        weigh_h(1, 3)
+        quantize_h(0, 3)
+        weigh_h(2, 3)
+        quantize_h(1, 3)
+        weigh_h(3, 3)
+        quantize_h(2, 3)
+        quantize_h(3, 3)
+        for g in range(PASSES):
+            passes(g, 3)
+        store(3, 0, scalar_move)
+        store(3, 1, vector_move)

@@ -30,6 +30,10 @@ COLS = 512
 PIECE = 256
 
 TURN_BANKS = 4
+WIDE_BUFS = 14
+ROWS = (0, 0, 5, 3, 3, 3, 3, 2, 2, 2, 1, 0, 0, 0, 0, 0)
+S_PIECES = {4: 2, 5: 3}
+G_PIECES = {2: 0, 3: 1, 4: 4, 5: 5, 6: 6, 7: 7, 8: 8, 9: 9, 10: 10, 11: 11, 12: 12, 13: 13, 14: 14, 15: 15}
 
 
 def tile_modal_response_estimate_s7_kernel(
@@ -53,6 +57,7 @@ def tile_modal_response_estimate_s7_kernel(
         gain_rows32 = once.tile([P, P], F32, name="gain_rows32")
         gain_cols = once.tile([P, MODE_BLOCKS], F32, name="gain_cols")
         weight = once.tile([P, PASSES, J], BF16, name="weight")
+        weight32 = once.tile([P, PASSES, J], F32, name="weight32")
 
         recon_codes = once.tile([P, PASSES * Z], U32, name="recon_codes", align_bytes=64)
         recon_sbytes = once.tile([P, PASSES * Z], U8, name="recon_sbytes", align_bytes=64)
@@ -74,6 +79,8 @@ def tile_modal_response_estimate_s7_kernel(
         h_raw = {}
         h_turned = {}
         h_grouped = {}
+        h_planes = {}
+        h_group = {}
         resp = {}
 
         def scalar_move(out, in_):
@@ -140,7 +147,7 @@ def tile_modal_response_estimate_s7_kernel(
 
         def widen(step, row):
             unit, half = divmod(step, 2)
-            wide = work.tile([P, HALF], BF16, name="wide", bufs=8)
+            wide = work.tile([P, HALF], BF16, name="wide", bufs=WIDE_BUFS)
             widened[step, row] = wide
             nc.scalar.copy(out=wide[:], in_=byte_rows[unit, half, row].bitcast(E4M3))
 
@@ -203,7 +210,7 @@ def tile_modal_response_estimate_s7_kernel(
         def limit(unit, mb):
             g, pair = divmod(unit, 2)
             if pair == 0:
-                h_raw[g, mb] = once.tile([P, J * P], F32, name="h_raw%d_%d" % (g, mb))
+                h_raw[g, mb] = work.tile([P, J * P], F32, name="h_raw", bufs=8)
             nc.scalar.activation(
                 out=h_raw[g, mb][:, pair * UNIT : (pair + 1) * UNIT],
                 in_=acc[unit, mb],
@@ -217,8 +224,34 @@ def tile_modal_response_estimate_s7_kernel(
                 nc.tensor.transpose(bank[:, t * P : (t + 1) * P], h_raw[g, mb][:, t * P : (t + 1) * P], ident[:])
             h_turned[g, mb] = bank
 
+        def turn_h_plane(g, t, bank_name):
+            bank = psum.tile([P, Z], F32, name=bank_name)
+            for mb in range(MODE_BLOCKS):
+                nc.tensor.transpose(bank[:, mb * P : (mb + 1) * P], h_raw[g, mb][:, t * P : (t + 1) * P], ident[:])
+            h_turned[g, t] = bank
+
+        def weigh_h_plane(g, t):
+            if t == 0:
+                h_planes[g] = work.tile([P, J, Z], BF16, name="h_planes", bufs=2)
+            nc.scalar.activation(
+                out=h_planes[g][:, t, :], in_=h_turned[g, t][:], func=COPY, scale=weight32[:, g, t : t + 1]
+            )
+
+        def interleave_h(g, part):
+            if part == 0:
+                h_group[g] = once.tile([P, J * Z], BF16, name="h_group%d" % g, align_bytes=64)
+            interleave(
+                scalar_move,
+                h_group[g][:, part * J * PIECE : (part + 1) * J * PIECE],
+                h_planes[g][:, :, part * PIECE : (part + 1) * PIECE],
+            )
+
+        def quantize_h_group(g):
+            cols = slice(g * Z, (g + 1) * Z)
+            nc.vector.quantize_mx(out=h_codes[:, cols].bitcast(E4M3X4), scales=h_sbytes[:, cols], in_=h_group[g][:])
+
         def weigh_h(g, mb):
-            h_grouped[g, mb] = work.tile([P, J * P], BF16, name="h_grouped", bufs=6, align_bytes=64)
+            h_grouped[g, mb] = work.tile([P, J * P], BF16, name="h_grouped", bufs=8, align_bytes=64)
             nc.vector.tensor_tensor(
                 out=h_grouped[g, mb][:].rearrange("p (z t) -> p z t", t=J),
                 in0=h_turned[g, mb][:].rearrange("p (t z) -> p z t", t=J),
@@ -258,18 +291,20 @@ def tile_modal_response_estimate_s7_kernel(
         nc.scalar.dma_start(out=scale[:], in_=slopes_scale.rearrange("o (g p j) -> p (o g) j", p=P, j=J))
         load_bytes(0, (0,))
         load_recon(0, (0,))
-        load_recon(0, (1,))
+        load_recon(1, (0,))
         load_bytes(0, (1,))
-        load_recon(1, (0, 1))
-        load_bytes(1, (0,))
-        load_recon(2, (0, 1))
-        load_recon(3, (0, 1))
-        load_bytes(1, (1,))
+        load_recon(2, (0,))
+        load_recon(3, (0,))
+        load_bytes(1, (0, 1))
         nc.sync.dma_start(out=gain_rows[0:MODE_BLOCKS, :], in_=gain.rearrange("(c p) -> c p", p=P))
-        load_commands(0, 0)
+        for g in range(PASSES):
+            load_recon(g, (1,))
         load_bytes(2, (0, 1))
-        nc.sync.dma_start(out=weight[:], in_=frame_weight.rearrange("(g p t) -> p g t", p=P, t=J))
+        load_commands(0, 0)
         load_commands(0, 1)
+        load_bytes(3, (0, 1))
+        nc.sync.dma_start(out=weight[:], in_=frame_weight.rearrange("(g p t) -> p g t", p=P, t=J))
+        load_bytes(4, (0, 1))
         load_commands(1, 0)
         load_commands(1, 1)
 
@@ -278,24 +313,22 @@ def tile_modal_response_estimate_s7_kernel(
         turn_slopes(0, 0)
         turn_slopes(0, 1)
         interleave_recon(0, 0, vector_move, "shared2")
-        interleave_recon(0, 1, vector_move, "shared3")
-        quantize_recon(0, 0)
+        interleave_recon(1, 0, gpsimd_move, "shared3")
         widen(1, 0)
         widen(1, 1)
         turn_slopes(1, 0)
         turn_slopes(1, 1)
-        interleave_recon(1, 0, gpsimd_move, "shared4")
-        interleave_recon(1, 1, scalar_move, "shared5")
+        interleave_recon(2, 0, scalar_move, "shared4")
         widen(2, 0)
         widen(2, 1)
-        interleave_recon(2, 1, scalar_move, "shared6")
-        interleave_recon(3, 0, scalar_move, "shared7")
-        interleave_recon(3, 1, scalar_move, "shared8")
+        widen(3, 0)
+        widen(3, 1)
+        nc.scalar.copy(out=gain_rows32[:], in_=gain_rows[:])
+        interleave_recon(0, 1, scalar_move, "shared5")
 
         pairs = [(u, mb) for u in range(UNITS) for mb in (0, 2)]
         stage1_steps = {i + 2: pair for i, pair in enumerate(pairs)}
         pieces = [(g, half, part) for g in range(PASSES) for half in range(2) for part in range(2)]
-        FIRST_PIECE = 1
 
         def stage1_step(step):
             unit, mb = stage1_steps[step]
@@ -303,53 +336,72 @@ def tile_modal_response_estimate_s7_kernel(
             limit(unit, mb)
             limit(unit, mb + 1)
 
-        def piece_done(g, half, part):
+        rows = [divmod(i, 2) for i in range(8, 2 * STEPS)]
+        rows_in_step = {}
+        for step in range(STEPS):
+            count = ROWS[step]
+            rows_in_step[step] = rows[:count]
+            rows = rows[count:]
+        plane_steps = {6 + i: [(i // J, i % J, "h%d" % (i % 2))] for i in range(2 * J)}
+        h_piece_steps = {11: (0, 0), 12: (0, 1), 14: (1, 0), 15: (1, 1)}
+        block_steps = {14: ((2, 0, "h0"), (2, 1, "turn0")), 15: ((2, 2, "h1"), (2, 3, "turn1"))}
+
+        def commands_piece(i, move, name):
+            g, half, part = pieces[i]
+            interleave_commands(g, half, part, move, name)
             if part == 1 and g < 2:
                 load_commands(g + 2, half)
 
         for step in range(STEPS):
-            if step % 2 == 0 and step // 2 + 3 < UNITS:
-                load_bytes(step // 2 + 3, (0, 1))
+            if step in (1, 2, 3):
+                load_bytes(step + 4, (0, 1))
             scale_slopes(step, 0)
             scale_slopes(step, 1)
             if step == 1:
-                nc.scalar.copy(out=gain_rows32[:], in_=gain_rows[:])
                 gain_bank = psum.tile([P, P], F32, name="h0")
                 nc.tensor.transpose(gain_bank[:], gain_rows32[:], ident[:])
-            if step + 3 < STEPS:
-                widen(step + 3, 0)
-                widen(step + 3, 1)
-            if step == 1:
                 nc.scalar.copy(out=gain_cols[:], in_=gain_bank[:, 0:MODE_BLOCKS])
+                interleave_recon(2, 1, scalar_move, "shared6")
+                interleave_recon(3, 1, scalar_move, "shared7")
+            for plane in plane_steps.get(step - 1, ()):
+                weigh_h_plane(*plane[:2])
+            if step == 2:
+                widen(4, 0)
+                widen(4, 1)
+                rows_in_step[2] = rows_in_step[2][2:]
             if step in stage1_steps:
                 stage1_step(step)
+            for row in rows_in_step[step]:
+                widen(*row)
+            if step == 3:
+                nc.scalar.copy(out=weight32[:], in_=weight[:])
+            if step in S_PIECES:
+                commands_piece(S_PIECES[step], scalar_move, ("shared0", "shared1", "extra")[(S_PIECES[step] % 2) if step < 10 else 2])
+            if step in h_piece_steps:
+                interleave_h(*h_piece_steps[step])
             if step < STEPS - 2:
                 turn_slopes(step + 2, 0)
                 turn_slopes(step + 2, 1)
-            if step == STEPS - 2:
-                turn_h(0, 0, "h0")
-                turn_h(0, 1, "h1")
-            if step == STEPS - 1:
-                turn_h(1, 0, "turn0")
-                turn_h(1, 1, "turn1")
+            for plane in plane_steps.get(step, ()):
+                turn_h_plane(*plane)
+            for block in block_steps.get(step, ()):
+                turn_h(*block)
             quantize_slopes(step, 0)
-            if step == 0:
-                quantize_recon(0, 1)
             if step == 1:
-                for g in (1, 2, 3):
+                for g in range(PASSES):
                     quantize_recon(g, 0)
+            if step == 2:
+                for g in range(PASSES):
                     quantize_recon(g, 1)
             quantize_slopes(step, 1)
             if step == 0:
-                interleave_recon(2, 0, gpsimd_move, "shared0")
-            if step >= FIRST_PIECE:
-                piece = pieces[step - FIRST_PIECE]
-                interleave_commands(*piece, gpsimd_move, "shared%d" % step)
-                piece_done(*piece)
-            if step == 13:
-                interleave_commands(*pieces[15], scalar_move, "shared0")
+                interleave_recon(3, 0, gpsimd_move, "shared0")
+            if step == 1:
+                interleave_recon(1, 1, gpsimd_move, "shared1")
+            if step in G_PIECES:
+                commands_piece(G_PIECES[step], gpsimd_move, "shared%d" % step)
 
-        banks = {0: ("turn2", "turn3"), 1: ("turn0", "turn1"), 2: ("h0", "h1"), 3: ("turn0", "turn1")}
+        banks = {0: ("turn2", "turn3"), 1: ("h0", "turn0"), 2: ("h1", "turn1"), 3: ("turn2", "turn3")}
 
         def passes(g, mb):
             for half in range(2):
@@ -357,59 +409,45 @@ def tile_modal_response_estimate_s7_kernel(
 
         stage1_step(16)
         stage1_step(17)
-        weigh_h(0, 0)
-        weigh_h(0, 1)
-        weigh_h(1, 0)
-        weigh_h(1, 1)
-        turn_h(2, 0, "h0")
-        turn_h(2, 1, "h1")
-        ahead = {
-            1: ((3, 0, "acc0"), (3, 1, "acc1")),
-            2: ((0, 2, "h0"), (1, 2, "h1")),
-            3: ((2, 2, "acc0"), (3, 2, "acc1")),
-        }
-        for g in range(PASSES):
-            if g >= 2:
-                weigh_h(g, 0)
-                weigh_h(g, 1)
-            quantize_h(g, 0)
-            quantize_commands(g, 0)
-            quantize_h(g, 1)
-            quantize_commands(g, 1)
-            for block in ahead.get(g, ()):
-                turn_h(*block)
-            passes(g, 0)
-            passes(g, 1)
+        for mb in range(MODE_BLOCKS):
+            weigh_h(2, mb)
+        quantize_commands(0, 0)
+        quantize_h_group(0)
+        quantize_commands(0, 1)
         for mb in range(2):
-            store(mb, 0, scalar_move)
-            store(mb, 1, scalar_move)
-        weigh_h(0, 2)
-        weigh_h(1, 2)
-        quantize_h(0, 2)
-        weigh_h(2, 2)
-        quantize_h(1, 2)
-        weigh_h(3, 2)
-        quantize_h(2, 2)
-        turn_h(0, 3, "turn2")
-        turn_h(1, 3, "turn3")
+            passes(0, mb)
+        turn_h(3, 0, "acc0")
+        turn_h(3, 1, "acc1")
         passes(0, 2)
-        passes(1, 2)
-        weigh_h(0, 3)
-        quantize_h(3, 2)
-        turn_h(2, 3, "acc0")
+        quantize_commands(1, 0)
+        quantize_h_group(1)
+        quantize_commands(1, 1)
+        weigh_h(3, 0)
+        weigh_h(3, 1)
+        for mb in range(3):
+            passes(1, mb)
+        turn_h(3, 2, "acc0")
         turn_h(3, 3, "acc1")
-        passes(2, 2)
-        passes(3, 2)
-        store(2, 0, scalar_move)
-        store(2, 1, scalar_move)
-        weigh_h(1, 3)
-        quantize_h(0, 3)
-        weigh_h(2, 3)
-        quantize_h(1, 3)
+        quantize_h(2, 0)
+        quantize_commands(2, 0)
+        quantize_commands(2, 1)
+        quantize_h(3, 0)
+        quantize_commands(3, 0)
+        quantize_commands(3, 1)
+        quantize_h(2, 1)
+        quantize_h(3, 1)
+        quantize_h(2, 2)
+        weigh_h(3, 2)
         weigh_h(3, 3)
+        quantize_h(3, 2)
         quantize_h(2, 3)
         quantize_h(3, 3)
-        for g in range(PASSES):
-            passes(g, 3)
+        for mb in range(3):
+            passes(2, mb)
+            passes(3, mb)
+            store(mb, 0, scalar_move)
+            store(mb, 1, scalar_move)
+        stage2(3, 0, (0, 1, 2, 3), "turn2")
         store(3, 0, scalar_move)
+        stage2(3, 1, (0, 1, 2, 3), "turn3")
         store(3, 1, vector_move)

@@ -30,10 +30,15 @@ COLS = 512
 PIECE = 256
 
 TURN_BANKS = 4
-WIDE_BUFS = 14
-ROWS = (0, 0, 5, 3, 3, 3, 3, 2, 2, 2, 1, 0, 0, 0, 0, 0)
-S_PIECES = {4: 2, 5: 3}
-G_PIECES = {2: 0, 3: 1, 4: 4, 5: 5, 6: 6, 7: 7, 8: 8, 9: 9, 10: 10, 11: 11, 12: 12, 13: 13, 14: 14, 15: 15}
+WIDE_BUFS = 10
+FIRST_PLANE = 4
+SORTED = range(6, 16)
+H_PIECES = {12: (0, 0), 13: (0, 1), 14: (1, 0), 15: (1, 1)}
+ROWS = (0, 0, 5, 3, 3, 2, 2, 2, 2, 2, 2, 1, 0, 0, 0, 0)
+WINDOWS = {0: 0, 1: 0, 2: 256, 3: 640, 5: 640, 7: 640, 9: 640, 11: 640, 13: 256, 14: 256, 15: 0}
+LAST_PLANES = {14: [(2, 2, "h0"), (2, 3, "h1")]}
+LATE_H = (0, 1)
+RECON_STEPS = {0: ((0, 0), (1, 0)), 1: ((2, 0), (3, 0)), 2: ((0, 1), (1, 1), (2, 1), (3, 1))}
 
 
 def tile_modal_response_estimate_s7_kernel(
@@ -67,11 +72,15 @@ def tile_modal_response_estimate_s7_kernel(
         h_sbytes = once.tile([P, PASSES * Z], U8, name="h_sbytes", align_bytes=64)
 
         byte_rows = {}
+        first_bytes = {}
         recon_raw = {}
         recon_grouped = {}
+        recon_banks = {}
+        acc_bank = {}
         com_raw = {}
-        com_grouped = {}
+        com_grouped = []
         widened = {}
+        sorted_words = {}
         turned = {}
         slopes_grouped = {}
         slope_codes = {}
@@ -102,6 +111,11 @@ def tile_modal_response_estimate_s7_kernel(
                 for half in halves:
                     byte_rows[unit, half, row] = row_bytes[:, row, half * HALF - k0 : (half + 1) * HALF - k0]
 
+        def load_first_bytes(b):
+            row_bytes = once.tile([P, 2, 512], U8, name="first_bytes%d" % b)
+            nc.sync.dma_start(out=row_bytes[:], in_=bytes_view[0][:, 0:2, 512 * b : 512 * (b + 1)])
+            first_bytes[b] = row_bytes
+
         def load_recon(g, parts):
             z0 = parts[0] * PIECE
             raw = once.tile([P, J, len(parts) * PIECE], BF16, name="recon_raw%d_%d" % (g, parts[0]))
@@ -109,10 +123,10 @@ def tile_modal_response_estimate_s7_kernel(
             for i, part in enumerate(parts):
                 recon_raw[g, part] = raw[:, :, i * PIECE : (i + 1) * PIECE]
 
-        def load_commands(g, half):
-            raw = work.tile([P, J, COLS], BF16, name="com_raw", bufs=4)
-            nc.sync.dma_start(out=raw[:], in_=commands_view[g][:, :, half * COLS : (half + 1) * COLS])
-            com_raw[g, half] = raw
+        def load_commands(g):
+            raw = work.tile([P, J, A], BF16, name="com_raw", bufs=3)
+            nc.sync.dma_start(out=raw[:], in_=commands_view[g])
+            com_raw[g] = raw
 
         def interleave(move, grouped, raw):
             move(
@@ -131,19 +145,28 @@ def tile_modal_response_estimate_s7_kernel(
                 out=recon_codes[:, cols].bitcast(E4M3X4), scales=recon_sbytes[:, cols], in_=recon_grouped[g, part][:]
             )
 
-        def interleave_commands(g, half, part, move, name):
-            grouped = once.tile([P, J * PIECE], BF16, name=name, align_bytes=64)
-            interleave(move, grouped[:], com_raw[g, half][:, :, part * PIECE : (part + 1) * PIECE])
-            com_grouped[g, half, part] = grouped
+        def interleave_commands(first, count, move, name):
+            grouped = once.tile([P, J * count], BF16, name=name, align_bytes=64)
+            done = 0
+            while done < count:
+                g, a0 = divmod(first + done, A)
+                width = min(count - done, A - a0)
+                interleave(move, grouped[:, J * done : J * (done + width)], com_raw[g][:, :, a0 : a0 + width])
+                done += width
+            com_grouped.append((first, count, grouped))
 
         def quantize_commands(g, half):
-            for part in range(2):
-                a0 = g * A + half * COLS + part * PIECE
-                nc.vector.quantize_mx(
-                    out=com_codes[:, a0 : a0 + PIECE].bitcast(E4M3X4),
-                    scales=com_sbytes[:, a0 : a0 + PIECE],
-                    in_=com_grouped[g, half, part][:],
-                )
+            lo = g * A + half * COLS
+            hi = lo + COLS
+            for first, count, grouped in com_grouped:
+                c0 = max(lo, first)
+                c1 = min(hi, first + count)
+                if c0 < c1:
+                    nc.vector.quantize_mx(
+                        out=com_codes[:, c0:c1].bitcast(E4M3X4),
+                        scales=com_sbytes[:, c0:c1],
+                        in_=grouped[:, J * (c0 - first) : J * (c1 - first)],
+                    )
 
         def widen(step, row):
             unit, half = divmod(step, 2)
@@ -151,43 +174,74 @@ def tile_modal_response_estimate_s7_kernel(
             widened[step, row] = wide
             nc.scalar.copy(out=wide[:], in_=byte_rows[unit, half, row].bitcast(E4M3))
 
+        def first_step(b):
+            wide = work.tile([P, 2, 512], BF16, name="wide", bufs=WIDE_BUFS)
+            nc.scalar.copy(
+                out=wide[:].rearrange("p r k -> p (r k)"),
+                in_=first_bytes[b][:].rearrange("p r k -> p (r k)").bitcast(E4M3),
+            )
+            bank = psum.tile([P, 2, UNIT], F32, name="turn%d" % b)
+            turned[0, b] = bank
+            for row in range(2):
+                words = wide[:, row, :].bitcast(F32)
+                for w in range(2):
+                    nc.tensor.transpose(bank[:, w, row * P : (row + 1) * P], words[:, w:256:2], ident[:])
+
+        def sort_words(step, row):
+            ordered = work.tile([P, 2, 2, P], F32, name="ordered", bufs=3)
+            nc.scalar.copy(
+                out=ordered[:], in_=widened[step, row][:].bitcast(F32).rearrange("p (b m w) -> p b w m", b=2, w=2)
+            )
+            sorted_words[step, row] = ordered
+
         def turn_slopes(step, b):
             bank = psum.tile([P, 2, UNIT], F32, name="turn%d" % ((2 * step + b) % TURN_BANKS))
             turned[step, b] = bank
             for row in range(2):
                 words = widened[step, row][:].bitcast(F32)
                 for w in range(2):
-                    nc.tensor.transpose(
-                        bank[:, w, row * P : (row + 1) * P], words[:, 256 * b + w : 256 * (b + 1) : 2], ident[:]
-                    )
+                    if (step, row) in sorted_words:
+                        source = sorted_words[step, row][:, b, w, :]
+                    else:
+                        source = words[:, 256 * b + w : 256 * (b + 1) : 2]
+                    nc.tensor.transpose(bank[:, w, row * P : (row + 1) * P], source, ident[:])
 
         def scale_slopes(step, b):
-            if b == 0:
-                grouped = work.tile([P, UNIT * J], BF16, name="slopes_grouped", bufs=2, align_bytes=64)
+            if step not in WINDOWS:
+                if b == 0:
+                    slopes_grouped[step] = work.tile([P, 2 * UNIT * J], BF16, name="step_grouped", bufs=2, align_bytes=64)
+                grouped = slopes_grouped[step][:, b * UNIT * J : (b + 1) * UNIT * J]
             else:
-                grouped = once.tile([P, UNIT * J], BF16, name="shared%d" % step, align_bytes=64)
-            slopes_grouped[step, b] = grouped
+                if b == 0:
+                    tile = work.tile([P, UNIT * J], BF16, name="bank_grouped", bufs=2, align_bytes=64)
+                else:
+                    tile = once.tile([P, UNIT * J], BF16, name="shared%d" % step, align_bytes=64)
+                slopes_grouped[step, b] = tile
+                grouped = tile[:]
             g = 2 * (step % 2) + b
             values = turned[step, b][:].rearrange("p w r -> p (w r)").bitcast(BF16)
             nc.vector.tensor_tensor(
-                out=grouped[:].rearrange("p (r w e) -> p r w e", w=2, e=2),
+                out=grouped.rearrange("p (r w e) -> p r w e", w=2, e=2),
                 in0=values.rearrange("p (w r e) -> p r w e", w=2, e=2),
                 in1=scale[:, g, :].rearrange("p (w e) -> p w e", e=2).unsqueeze(1).to_broadcast([P, UNIT, 2, 2]),
                 op=MULT,
             )
 
-        def quantize_slopes(step, b):
+        def quantize_slopes(step, b=None):
             unit, half = divmod(step, 2)
-            if half == 0 and b == 0:
+            if half == 0 and not b:
                 slope_codes[unit] = (
                     work.tile([P, PASSES * UNIT], U32, name="slope_codes", bufs=3, align_bytes=64),
                     work.tile([P, PASSES * UNIT], U8, name="slope_sbytes", bufs=3, align_bytes=64),
                 )
             codes, sbytes = slope_codes[unit]
-            cols = slice((2 * half + b) * UNIT, (2 * half + b + 1) * UNIT)
-            nc.vector.quantize_mx(
-                out=codes[:, cols].bitcast(E4M3X4), scales=sbytes[:, cols], in_=slopes_grouped[step, b][:]
-            )
+            if b is None:
+                cols = slice(2 * half * UNIT, (2 * half + 2) * UNIT)
+                grouped = slopes_grouped[step]
+            else:
+                cols = slice((2 * half + b) * UNIT, (2 * half + b + 1) * UNIT)
+                grouped = slopes_grouped[step, b]
+            nc.vector.quantize_mx(out=codes[:, cols].bitcast(E4M3X4), scales=sbytes[:, cols], in_=grouped[:])
 
         def stage1(unit, blocks, bank_name):
             bank = psum.tile([P, 2, UNIT], F32, name=bank_name)
@@ -206,6 +260,26 @@ def tile_modal_response_estimate_s7_kernel(
                         stop=(g == PASSES - 1),
                     )
                 acc[unit, mb] = bank[:, i, :]
+
+        def stage1_passes(unit, mb0, groups, bank_name):
+            if groups[0] == 0:
+                acc_bank[unit, mb0] = psum.tile([P, 2, UNIT], F32, name=bank_name)
+            bank = acc_bank[unit, mb0]
+            codes, sbytes = slope_codes[unit]
+            for g in groups:
+                for i in range(2):
+                    z0 = g * Z + (mb0 + i) * P
+                    r0 = g * UNIT
+                    nc.tensor.matmul_mx(
+                        out=bank[:, i, :],
+                        lhsT=recon_codes[:, z0 : z0 + P].bitcast(E4M3X4),
+                        lhsT_scale=recon_sbytes[:, z0 : z0 + P],
+                        rhs=codes[:, r0 : r0 + UNIT].bitcast(E4M3X4),
+                        rhs_scale=sbytes[:, r0 : r0 + UNIT],
+                        start=(g == 0 and i == 0),
+                        stop=(g == PASSES - 1 and i == 1),
+                    )
+                    acc[unit, mb0 + i] = bank[:, i, :]
 
         def limit(unit, mb):
             g, pair = divmod(unit, 2)
@@ -251,7 +325,7 @@ def tile_modal_response_estimate_s7_kernel(
             nc.vector.quantize_mx(out=h_codes[:, cols].bitcast(E4M3X4), scales=h_sbytes[:, cols], in_=h_group[g][:])
 
         def weigh_h(g, mb):
-            h_grouped[g, mb] = work.tile([P, J * P], BF16, name="h_grouped", bufs=8, align_bytes=64)
+            h_grouped[g, mb] = work.tile([P, J * P], BF16, name="h_grouped", bufs=4, align_bytes=64)
             nc.vector.tensor_tensor(
                 out=h_grouped[g, mb][:].rearrange("p (z t) -> p z t", t=J),
                 in0=h_turned[g, mb][:].rearrange("p (t z) -> p z t", t=J),
@@ -281,18 +355,38 @@ def tile_modal_response_estimate_s7_kernel(
                     stop=(g == PASSES - 1),
                 )
 
+        def last_tile(part, bank_name, move):
+            bank = psum.tile([P, PIECE], F32, name=bank_name)
+            a0 = COLS + part * PIECE
+            for g in range(PASSES):
+                z0 = g * Z + 3 * P
+                nc.tensor.matmul_mx(
+                    out=bank[:],
+                    lhsT=h_codes[:, z0 : z0 + P].bitcast(E4M3X4),
+                    lhsT_scale=h_sbytes[:, z0 : z0 + P],
+                    rhs=com_codes[:, g * A + a0 : g * A + a0 + PIECE].bitcast(E4M3X4),
+                    rhs_scale=com_sbytes[:, g * A + a0 : g * A + a0 + PIECE],
+                    start=(g == 0),
+                    stop=(g == PASSES - 1),
+                )
+            result = work.tile([P, PIECE], F32, name="wide", bufs=WIDE_BUFS)
+            move(result[:], bank[:])
+            nc.sync.dma_start(out=out[3 * P : 4 * P, a0 : a0 + PIECE], in_=result[:])
+
         def store(mb, half, move):
-            result = work.tile([P, COLS], F32, name="result", bufs=6)
+            result = work.tile([P, COLS], F32, name="wide", bufs=WIDE_BUFS)
             move(result[:], resp[mb, half][:])
             nc.sync.dma_start(out=out[mb * P : (mb + 1) * P, half * COLS : (half + 1) * COLS], in_=result[:])
 
         nc.gpsimd.memset(gain_rows[:], 0.0)
         make_identity(nc, ident[:])
+        nc.scalar.dma_start(out=weight[:], in_=frame_weight.rearrange("(g p t) -> p g t", p=P, t=J))
         nc.scalar.dma_start(out=scale[:], in_=slopes_scale.rearrange("o (g p j) -> p (o g) j", p=P, j=J))
-        load_bytes(0, (0,))
+        load_first_bytes(0)
+        load_first_bytes(1)
         load_recon(0, (0,))
-        load_recon(1, (0,))
         load_bytes(0, (1,))
+        load_recon(1, (0,))
         load_recon(2, (0,))
         load_recon(3, (0,))
         load_bytes(1, (0, 1))
@@ -300,39 +394,37 @@ def tile_modal_response_estimate_s7_kernel(
         for g in range(PASSES):
             load_recon(g, (1,))
         load_bytes(2, (0, 1))
-        load_commands(0, 0)
-        load_commands(0, 1)
+        load_commands(0)
         load_bytes(3, (0, 1))
-        nc.sync.dma_start(out=weight[:], in_=frame_weight.rearrange("(g p t) -> p g t", p=P, t=J))
         load_bytes(4, (0, 1))
-        load_commands(1, 0)
-        load_commands(1, 1)
+        load_commands(1)
 
-        widen(0, 0)
-        widen(0, 1)
-        turn_slopes(0, 0)
-        turn_slopes(0, 1)
+        nc.scalar.activation(out=weight32[:], in_=weight[:], func=COPY)
+        first_step(0)
+        first_step(1)
         interleave_recon(0, 0, vector_move, "shared2")
         interleave_recon(1, 0, gpsimd_move, "shared3")
         widen(1, 0)
         widen(1, 1)
         turn_slopes(1, 0)
         turn_slopes(1, 1)
-        interleave_recon(2, 0, scalar_move, "shared4")
+        interleave_recon(2, 0, scalar_move, "shared7")
         widen(2, 0)
         widen(2, 1)
         widen(3, 0)
         widen(3, 1)
         nc.scalar.copy(out=gain_rows32[:], in_=gain_rows[:])
-        interleave_recon(0, 1, scalar_move, "shared5")
+        interleave_recon(0, 1, scalar_move, "shared9")
 
-        pairs = [(u, mb) for u in range(UNITS) for mb in (0, 2)]
+        pairs = [(u, mb) for u in range(LAST) for mb in (0, 2)]
         stage1_steps = {i + 2: pair for i, pair in enumerate(pairs)}
-        pieces = [(g, half, part) for g in range(PASSES) for half in range(2) for part in range(2)]
 
         def stage1_step(step):
             unit, mb = stage1_steps[step]
-            stage1(unit, (mb, mb + 1), "acc%d" % (step % 2))
+            if step == 2:
+                stage1_passes(0, 0, (2, 3), None)
+            else:
+                stage1(unit, (mb, mb + 1), "acc%d" % (step % 2))
             limit(unit, mb)
             limit(unit, mb + 1)
 
@@ -342,15 +434,11 @@ def tile_modal_response_estimate_s7_kernel(
             count = ROWS[step]
             rows_in_step[step] = rows[:count]
             rows = rows[count:]
-        plane_steps = {6 + i: [(i // J, i % J, "h%d" % (i % 2))] for i in range(2 * J)}
-        h_piece_steps = {11: (0, 0), 12: (0, 1), 14: (1, 0), 15: (1, 1)}
-        block_steps = {14: ((2, 0, "h0"), (2, 1, "turn0")), 15: ((2, 2, "h1"), (2, 3, "turn1"))}
+        plane_steps = {FIRST_PLANE + i: [(i // J, i % J, "h%d" % (i % 2))] for i in range(10)}
+        h_piece_steps = dict(H_PIECES)
+        plane_steps.update(LAST_PLANES)
 
-        def commands_piece(i, move, name):
-            g, half, part = pieces[i]
-            interleave_commands(g, half, part, move, name)
-            if part == 1 and g < 2:
-                load_commands(g + 2, half)
+        first_actuator = 0
 
         for step in range(STEPS):
             if step in (1, 2, 3):
@@ -361,93 +449,111 @@ def tile_modal_response_estimate_s7_kernel(
                 gain_bank = psum.tile([P, P], F32, name="h0")
                 nc.tensor.transpose(gain_bank[:], gain_rows32[:], ident[:])
                 nc.scalar.copy(out=gain_cols[:], in_=gain_bank[:, 0:MODE_BLOCKS])
-                interleave_recon(2, 1, scalar_move, "shared6")
-                interleave_recon(3, 1, scalar_move, "shared7")
+                interleave_recon(2, 1, scalar_move, "shared11")
+                interleave_recon(3, 1, scalar_move, "shared13")
+            if step == STEPS - 1:
+                stage1_step(step)
+            if step == 13:
+                interleave_h(*h_piece_steps.pop(step))
             for plane in plane_steps.get(step - 1, ()):
                 weigh_h_plane(*plane[:2])
             if step == 2:
                 widen(4, 0)
                 widen(4, 1)
                 rows_in_step[2] = rows_in_step[2][2:]
-            if step in stage1_steps:
+            if step in stage1_steps and step < STEPS - 1:
                 stage1_step(step)
             for row in rows_in_step[step]:
                 widen(*row)
-            if step == 3:
-                nc.scalar.copy(out=weight32[:], in_=weight[:])
-            if step in S_PIECES:
-                commands_piece(S_PIECES[step], scalar_move, ("shared0", "shared1", "extra")[(S_PIECES[step] % 2) if step < 10 else 2])
+            if step + 3 in SORTED:
+                sort_words(step + 3, 1)
             if step in h_piece_steps:
                 interleave_h(*h_piece_steps[step])
-            if step < STEPS - 2:
+            if 0 < step < STEPS - 2:
                 turn_slopes(step + 2, 0)
                 turn_slopes(step + 2, 1)
             for plane in plane_steps.get(step, ()):
                 turn_h_plane(*plane)
-            for block in block_steps.get(step, ()):
-                turn_h(*block)
-            quantize_slopes(step, 0)
-            if step == 1:
-                for g in range(PASSES):
-                    quantize_recon(g, 0)
-            if step == 2:
-                for g in range(PASSES):
-                    quantize_recon(g, 1)
-            quantize_slopes(step, 1)
-            if step == 0:
-                interleave_recon(3, 0, gpsimd_move, "shared0")
-            if step == 1:
-                interleave_recon(1, 1, gpsimd_move, "shared1")
-            if step in G_PIECES:
-                commands_piece(G_PIECES[step], gpsimd_move, "shared%d" % step)
+            if step == STEPS - 1:
+                stage1_passes(LAST, 0, (0, 1), "acc0")
+                stage1_passes(LAST, 2, (0, 1), "acc1")
+            if step in WINDOWS:
+                if step > 0 and step - 1 not in WINDOWS:
+                    quantize_slopes(step - 1)
+                quantize_slopes(step, 0)
+                for g, part in RECON_STEPS.get(step, ()):
+                    quantize_recon(g, part)
+                quantize_slopes(step, 1)
+                if step == 0:
+                    interleave_recon(3, 0, gpsimd_move, "shared0")
+                    stage1_passes(0, 0, (0, 1), "acc0")
+                    turn_slopes(2, 0)
+                    turn_slopes(2, 1)
+                elif step == 1:
+                    interleave_recon(1, 1, gpsimd_move, "shared1")
+                elif WINDOWS[step]:
+                    interleave_commands(first_actuator, WINDOWS[step], gpsimd_move, "shared%d" % step)
+                    first_actuator += WINDOWS[step]
+            if step == 3:
+                load_commands(2)
+            if step == 6:
+                load_commands(3)
 
-        banks = {0: ("turn2", "turn3"), 1: ("h0", "turn0"), 2: ("h1", "turn1"), 3: ("turn2", "turn3")}
+        banks = {0: ("turn2", "turn3"), 1: ("h0", "h1"), 2: ("turn0", "turn1"), 3: ("turn2", "turn3")}
+
+        def one_pass(g, mb, half):
+            stage2(mb, half, (g,), banks[mb][half] if g == 0 else None)
 
         def passes(g, mb):
-            for half in range(2):
-                stage2(mb, half, (g,), banks[mb][half] if g == 0 else None)
+            one_pass(g, mb, 0)
+            one_pass(g, mb, 1)
 
-        stage1_step(16)
-        stage1_step(17)
-        for mb in range(MODE_BLOCKS):
-            weigh_h(2, mb)
+        for plane in plane_steps.get(STEPS - 1, ()):
+            weigh_h_plane(*plane[:2])
+        for mb in (0, 2):
+            stage1_passes(LAST, mb, (2, 3), None)
+            limit(LAST, mb)
+            limit(LAST, mb + 1)
+        for part in LATE_H:
+            interleave_h(2, part)
+        interleave_commands(first_actuator, PASSES * A - first_actuator, scalar_move, "shared15")
         quantize_commands(0, 0)
         quantize_h_group(0)
         quantize_commands(0, 1)
-        for mb in range(2):
-            passes(0, mb)
+        for half in range(2):
+            for mb in range(3):
+                one_pass(0, mb, half)
         turn_h(3, 0, "acc0")
         turn_h(3, 1, "acc1")
-        passes(0, 2)
         quantize_commands(1, 0)
         quantize_h_group(1)
         quantize_commands(1, 1)
         weigh_h(3, 0)
         weigh_h(3, 1)
-        for mb in range(3):
-            passes(1, mb)
+        for half in range(2):
+            for mb in range(3):
+                one_pass(1, mb, half)
         turn_h(3, 2, "acc0")
         turn_h(3, 3, "acc1")
-        quantize_h(2, 0)
         quantize_commands(2, 0)
+        quantize_h_group(2)
         quantize_commands(2, 1)
         quantize_h(3, 0)
         quantize_commands(3, 0)
-        quantize_commands(3, 1)
-        quantize_h(2, 1)
         quantize_h(3, 1)
-        quantize_h(2, 2)
+        quantize_commands(3, 1)
         weigh_h(3, 2)
         weigh_h(3, 3)
         quantize_h(3, 2)
-        quantize_h(2, 3)
         quantize_h(3, 3)
+        for half in range(2):
+            for mb in range(3):
+                one_pass(2, mb, half)
         for mb in range(3):
-            passes(2, mb)
             passes(3, mb)
             store(mb, 0, scalar_move)
-            store(mb, 1, scalar_move)
+            store(mb, 1, scalar_move if mb == 0 else vector_move)
         stage2(3, 0, (0, 1, 2, 3), "turn2")
         store(3, 0, scalar_move)
-        stage2(3, 1, (0, 1, 2, 3), "turn3")
-        store(3, 1, vector_move)
+        last_tile(0, "turn3", vector_move)
+        last_tile(1, "acc0", scalar_move)

@@ -30,15 +30,18 @@ COLS = 512
 PIECE = 256
 
 TURN_BANKS = 4
-WIDE_BUFS = 10
+WIDE_BUFS = 8
 FIRST_PLANE = 4
+HPB = 3
+CUT_A = 6
+CUT_B = 3
 SORTED = range(6, 16)
-H_PIECES = {12: (0, 0), 13: (0, 1), 14: (1, 0), 15: (1, 1)}
-ROWS = (0, 0, 5, 3, 3, 2, 2, 2, 2, 2, 2, 1, 0, 0, 0, 0)
+H_PIECES = {12: (0, 0), 13: (0, 1), 14: (1, 0)}
+ROWS = (0, 0, 3, 3, 3, 2, 2, 2, 2, 2, 2, 1, 0, 0, 0, 0)
 WINDOWS = {0: 0, 1: 0, 2: 256, 3: 640, 5: 640, 7: 640, 9: 640, 11: 640, 13: 256, 14: 256, 15: 0}
 LAST_PLANES = {14: [(2, 2, "h0"), (2, 3, "h1")]}
 LATE_H = (0, 1)
-RECON_STEPS = {0: ((0, 0), (1, 0)), 1: ((2, 0), (3, 0)), 2: ((0, 1), (1, 1), (2, 1), (3, 1))}
+RECON_STEPS = {0: ((0, 0), (0, 1)), 1: ((1, 0), (2, 0), (1, 1)), 2: ((2, 1), (3, 0), (3, 1))}
 
 
 def tile_modal_response_estimate_s7_kernel(
@@ -261,6 +264,32 @@ def tile_modal_response_estimate_s7_kernel(
                     )
                 acc[unit, mb] = bank[:, i, :]
 
+        def stage1_run(step, first, last):
+            unit, mb0 = stage1_steps[step]
+            if first == 0:
+                acc_bank[unit, mb0] = psum.tile([P, 2, UNIT], F32, name="acc%d" % (step % 2))
+            bank = acc_bank[unit, mb0]
+            codes, sbytes = slope_codes[unit]
+            for n in range(first, last):
+                i, g = divmod(n, PASSES)
+                z0 = g * Z + (mb0 + i) * P
+                r0 = g * UNIT
+                nc.tensor.matmul_mx(
+                    out=bank[:, i, :],
+                    lhsT=recon_codes[:, z0 : z0 + P].bitcast(E4M3X4),
+                    lhsT_scale=recon_sbytes[:, z0 : z0 + P],
+                    rhs=codes[:, r0 : r0 + UNIT].bitcast(E4M3X4),
+                    rhs_scale=sbytes[:, r0 : r0 + UNIT],
+                    start=(g == 0),
+                    stop=(g == PASSES - 1),
+                )
+                acc[unit, mb0 + i] = bank[:, i, :]
+
+        def limit_pair(step):
+            unit, mb0 = stage1_steps[step]
+            limit(unit, mb0)
+            limit(unit, mb0 + 1)
+
         def stage1_passes(unit, mb0, groups, bank_name):
             if groups[0] == 0:
                 acc_bank[unit, mb0] = psum.tile([P, 2, UNIT], F32, name=bank_name)
@@ -306,16 +335,16 @@ def tile_modal_response_estimate_s7_kernel(
 
         def weigh_h_plane(g, t):
             if t == 0:
-                h_planes[g] = work.tile([P, J, Z], BF16, name="h_planes", bufs=2)
+                h_planes[g] = work.tile([P, J, Z], BF16, name="h_planes", bufs=HPB)
             nc.scalar.activation(
                 out=h_planes[g][:, t, :], in_=h_turned[g, t][:], func=COPY, scale=weight32[:, g, t : t + 1]
             )
 
-        def interleave_h(g, part):
+        def interleave_h(g, part, move=scalar_move):
             if part == 0:
                 h_group[g] = once.tile([P, J * Z], BF16, name="h_group%d" % g, align_bytes=64)
             interleave(
-                scalar_move,
+                move,
                 h_group[g][:, part * J * PIECE : (part + 1) * J * PIECE],
                 h_planes[g][:, :, part * PIECE : (part + 1) * PIECE],
             )
@@ -378,57 +407,54 @@ def tile_modal_response_estimate_s7_kernel(
             move(result[:], resp[mb, half][:])
             nc.sync.dma_start(out=out[mb * P : (mb + 1) * P, half * COLS : (half + 1) * COLS], in_=result[:])
 
-        nc.gpsimd.memset(gain_rows[:], 0.0)
         make_identity(nc, ident[:])
-        nc.scalar.dma_start(out=weight[:], in_=frame_weight.rearrange("(g p t) -> p g t", p=P, t=J))
         nc.scalar.dma_start(out=scale[:], in_=slopes_scale.rearrange("o (g p j) -> p (o g) j", p=P, j=J))
+        nc.scalar.activation(out=gain_rows[:], in_=ident[:], func=COPY, scale=0.0)
         load_first_bytes(0)
         load_first_bytes(1)
-        load_recon(0, (0,))
+        load_recon(0, (0, 1))
         load_bytes(0, (1,))
-        load_recon(1, (0,))
-        load_recon(2, (0,))
-        load_recon(3, (0,))
-        load_bytes(1, (0, 1))
-        nc.sync.dma_start(out=gain_rows[0:MODE_BLOCKS, :], in_=gain.rearrange("(c p) -> c p", p=P))
-        for g in range(PASSES):
-            load_recon(g, (1,))
+        load_recon(1, (0, 1))
+        load_bytes(1, (0,))
+        load_recon(2, (0, 1))
+        load_recon(3, (0, 1))
+        load_bytes(1, (1,))
         load_bytes(2, (0, 1))
+        nc.sync.dma_start(out=gain_rows[0:MODE_BLOCKS, :], in_=gain.rearrange("(c p) -> c p", p=P))
         load_commands(0)
         load_bytes(3, (0, 1))
+        nc.sync.dma_start(out=weight[:], in_=frame_weight.rearrange("(g p t) -> p g t", p=P, t=J))
         load_bytes(4, (0, 1))
         load_commands(1)
 
-        nc.scalar.activation(out=weight32[:], in_=weight[:], func=COPY)
         first_step(0)
         first_step(1)
-        interleave_recon(0, 0, vector_move, "shared2")
-        interleave_recon(1, 0, gpsimd_move, "shared3")
+        interleave_recon(0, 0, gpsimd_move, "shared2")
+        interleave_recon(0, 1, scalar_move, "shared3")
         widen(1, 0)
         widen(1, 1)
         turn_slopes(1, 0)
         turn_slopes(1, 1)
-        interleave_recon(2, 0, scalar_move, "shared7")
+        interleave_recon(1, 0, scalar_move, "shared5")
         widen(2, 0)
         widen(2, 1)
+        interleave_recon(1, 1, scalar_move, "shared7")
+        interleave_recon(2, 1, scalar_move, "shared9")
         widen(3, 0)
         widen(3, 1)
         nc.scalar.copy(out=gain_rows32[:], in_=gain_rows[:])
-        interleave_recon(0, 1, scalar_move, "shared9")
+        interleave_recon(3, 0, scalar_move, "shared11")
 
         pairs = [(u, mb) for u in range(LAST) for mb in (0, 2)]
         stage1_steps = {i + 2: pair for i, pair in enumerate(pairs)}
 
         def stage1_step(step):
             unit, mb = stage1_steps[step]
-            if step == 2:
-                stage1_passes(0, 0, (2, 3), None)
-            else:
-                stage1(unit, (mb, mb + 1), "acc%d" % (step % 2))
+            stage1(unit, (mb, mb + 1), "acc%d" % (step % 2))
             limit(unit, mb)
             limit(unit, mb + 1)
 
-        rows = [divmod(i, 2) for i in range(8, 2 * STEPS)]
+        rows = [divmod(i, 2) for i in range(10, 2 * STEPS)]
         rows_in_step = {}
         for step in range(STEPS):
             count = ROWS[step]
@@ -440,43 +466,75 @@ def tile_modal_response_estimate_s7_kernel(
 
         first_actuator = 0
 
+        def side_work(step):
+            for row in rows_in_step.pop(step):
+                widen(*row)
+            if step + 3 in SORTED:
+                sort_words(step + 3, 1)
+
+        def middle_step(step):
+            if step % 2 == 0:
+                side_work(step)
+                stage1_run(step, 0, CUT_A)
+                turn_slopes(step + 2, 0)
+                turn_h_plane(*plane_steps[step][0])
+                stage1_run(step, CUT_A, 8)
+                stage1_run(step + 1, 0, CUT_B)
+                weigh_h_plane(*plane_steps[step][0][:2])
+                limit_pair(step)
+                turn_slopes(step + 2, 1)
+                turn_h_plane(*plane_steps[step + 1][0])
+            else:
+                side_work(step)
+                stage1_run(step, CUT_B, 8)
+                weigh_h_plane(*plane_steps[step][0][:2])
+                limit_pair(step)
+                turn_slopes(step + 2, 0)
+                turn_slopes(step + 2, 1)
+            if step in h_piece_steps:
+                interleave_h(*h_piece_steps[step])
+
         for step in range(STEPS):
+            middle = 4 <= step < 14
             if step in (1, 2, 3):
                 load_bytes(step + 4, (0, 1))
             scale_slopes(step, 0)
             scale_slopes(step, 1)
-            if step == 1:
-                gain_bank = psum.tile([P, P], F32, name="h0")
-                nc.tensor.transpose(gain_bank[:], gain_rows32[:], ident[:])
-                nc.scalar.copy(out=gain_cols[:], in_=gain_bank[:, 0:MODE_BLOCKS])
-                interleave_recon(2, 1, scalar_move, "shared11")
-                interleave_recon(3, 1, scalar_move, "shared13")
+            if step == 4:
+                side_work(step)
+                limit_pair(4)
+                turn_slopes(6, 0)
+                turn_h_plane(0, 0, "acc0")
+                turn_slopes(6, 1)
+                stage1_passes(1, 2, (2, 3), None)
+                weigh_h_plane(0, 0)
+                limit_pair(5)
+            if step == 5:
+                side_work(step)
+                turn_h_plane(0, 1, "acc1")
+                turn_slopes(7, 0)
+                turn_slopes(7, 1)
+                weigh_h_plane(0, 1)
+            if 6 <= step < 14:
+                middle_step(step)
             if step == STEPS - 1:
                 stage1_step(step)
-            if step == 13:
-                interleave_h(*h_piece_steps.pop(step))
-            for plane in plane_steps.get(step - 1, ()):
-                weigh_h_plane(*plane[:2])
-            if step == 2:
-                widen(4, 0)
-                widen(4, 1)
-                rows_in_step[2] = rows_in_step[2][2:]
-            if step in stage1_steps and step < STEPS - 1:
+            if step == STEPS - 1:
+                for plane in plane_steps[step - 1]:
+                    weigh_h_plane(*plane[:2])
+            if step == 14:
                 stage1_step(step)
-            for row in rows_in_step[step]:
-                widen(*row)
-            if step + 3 in SORTED:
-                sort_words(step + 3, 1)
-            if step in h_piece_steps:
-                interleave_h(*h_piece_steps[step])
-            if 0 < step < STEPS - 2:
-                turn_slopes(step + 2, 0)
-                turn_slopes(step + 2, 1)
-            for plane in plane_steps.get(step, ()):
-                turn_h_plane(*plane)
+            if not middle:
+                side_work(step)
+                if step in h_piece_steps:
+                    interleave_h(*h_piece_steps[step])
+
+            if step == 14:
+                for plane in plane_steps[step]:
+                    turn_h_plane(*plane)
             if step == STEPS - 1:
                 stage1_passes(LAST, 0, (0, 1), "acc0")
-                stage1_passes(LAST, 2, (0, 1), "acc1")
+                stage1_passes(LAST, 2, (0, 1), "turn1")
             if step in WINDOWS:
                 if step > 0 and step - 1 not in WINDOWS:
                     quantize_slopes(step - 1)
@@ -485,15 +543,39 @@ def tile_modal_response_estimate_s7_kernel(
                     quantize_recon(g, part)
                 quantize_slopes(step, 1)
                 if step == 0:
-                    interleave_recon(3, 0, gpsimd_move, "shared0")
-                    stage1_passes(0, 0, (0, 1), "acc0")
+                    interleave_recon(2, 0, gpsimd_move, "shared0")
+                    stage1_passes(0, 0, (0,), "acc0")
+                    stage1_passes(0, 2, (0,), "acc1")
                     turn_slopes(2, 0)
                     turn_slopes(2, 1)
                 elif step == 1:
-                    interleave_recon(1, 1, gpsimd_move, "shared1")
+                    interleave_recon(3, 1, gpsimd_move, "shared1")
+                    stage1_passes(0, 0, (1, 2), None)
+                    stage1_passes(0, 2, (1,), None)
+                    gain_bank = psum.tile([P, P], F32, name="h0")
+                    nc.tensor.transpose(gain_bank[:], gain_rows32[:], ident[:])
+                    nc.scalar.copy(out=gain_cols[:], in_=gain_bank[:, 0:MODE_BLOCKS])
+                    widen(4, 0)
+                    widen(4, 1)
+                    turn_slopes(3, 0)
+                    turn_slopes(3, 1)
                 elif WINDOWS[step]:
                     interleave_commands(first_actuator, WINDOWS[step], gpsimd_move, "shared%d" % step)
                     first_actuator += WINDOWS[step]
+            if step == 2:
+                stage1_passes(1, 0, (0, 1), "h0")
+                stage1_passes(0, 0, (3,), None)
+                stage1_passes(0, 2, (2, 3), None)
+                turn_slopes(4, 0)
+                turn_slopes(4, 1)
+                stage1_passes(1, 2, (0, 1), "h1")
+                limit_pair(2)
+                limit_pair(3)
+                nc.scalar.copy(out=weight32[:], in_=weight[:])
+            if step == 3:
+                turn_slopes(5, 0)
+                turn_slopes(5, 1)
+                stage1_passes(1, 0, (2, 3), None)
             if step == 3:
                 load_commands(2)
             if step == 6:
@@ -525,35 +607,42 @@ def tile_modal_response_estimate_s7_kernel(
                 one_pass(0, mb, half)
         turn_h(3, 0, "acc0")
         turn_h(3, 1, "acc1")
+        interleave_h(1, 1, vector_move)
         quantize_commands(1, 0)
         quantize_h_group(1)
         quantize_commands(1, 1)
         weigh_h(3, 0)
-        weigh_h(3, 1)
         for half in range(2):
             for mb in range(3):
                 one_pass(1, mb, half)
         turn_h(3, 2, "acc0")
-        turn_h(3, 3, "acc1")
         quantize_commands(2, 0)
         quantize_h_group(2)
-        quantize_commands(2, 1)
         quantize_h(3, 0)
         quantize_commands(3, 0)
+        weigh_h(3, 1)
+        quantize_commands(2, 1)
         quantize_h(3, 1)
-        quantize_commands(3, 1)
         weigh_h(3, 2)
-        weigh_h(3, 3)
+        quantize_commands(3, 1)
         quantize_h(3, 2)
-        quantize_h(3, 3)
-        for half in range(2):
-            for mb in range(3):
-                one_pass(2, mb, half)
         for mb in range(3):
-            passes(3, mb)
-            store(mb, 0, scalar_move)
-            store(mb, 1, scalar_move if mb == 0 else vector_move)
+            one_pass(2, mb, 0)
+        one_pass(3, 0, 0)
+        store(0, 0, scalar_move)
+        turn_h(3, 3, "acc1")
+        weigh_h(3, 3)
+        quantize_h(3, 3)
+        one_pass(3, 1, 0)
+        store(1, 0, scalar_move)
+        for mb in range(3):
+            one_pass(2, mb, 1)
+        one_pass(3, 2, 0)
+        store(2, 0, scalar_move)
+        for mb in range(3):
+            one_pass(3, mb, 1)
+            store(mb, 1, vector_move if mb == 1 else scalar_move)
         stage2(3, 0, (0, 1, 2, 3), "turn2")
-        store(3, 0, scalar_move)
-        last_tile(0, "turn3", vector_move)
-        last_tile(1, "acc0", scalar_move)
+        store(3, 0, vector_move)
+        last_tile(0, "h0", scalar_move)
+        last_tile(1, "acc0", vector_move)

@@ -34,11 +34,12 @@ WIDE_BUFS = 8
 FIRST_PLANE = 4
 HPB = 3
 CUT_A = 6
+TWO_RUNS_FROM = 6
 CUT_B = 3
 SORTED = range(6, 16)
 H_PIECES = {12: (0, 0), 13: (0, 1), 14: (1, 0)}
-ROWS = (0, 0, 3, 3, 3, 2, 2, 2, 2, 2, 2, 1, 0, 0, 0, 0)
-WINDOWS = {0: 0, 1: 0, 2: 256, 3: 640, 5: 640, 7: 640, 9: 640, 11: 640, 13: 256, 14: 256, 15: 0}
+ROWS = (0, 0, 3, 3, 2, 2, 2, 2, 2, 2, 2, 2, 0, 0, 0, 0)
+WINDOWS = {0: 0, 1: 0, 2: 256, 3: 640, 5: 512, 7: 640, 9: 640, 11: 512, 13: 256, 14: 256, 15: 0}
 LAST_PLANES = {14: [(2, 2, "h0"), (2, 3, "h1")]}
 LATE_H = (0, 1)
 RECON_STEPS = {0: ((0, 0), (0, 1)), 1: ((1, 0), (2, 0), (1, 1)), 2: ((2, 1), (3, 0), (3, 1))}
@@ -473,7 +474,18 @@ def tile_modal_response_estimate_s7_kernel(
                 sort_words(step + 3, 1)
 
         def middle_step(step):
-            if step % 2 == 0:
+            if step >= TWO_RUNS_FROM:
+                side_work(step)
+                stage1_run(step, 0, 8)
+                if step > TWO_RUNS_FROM:
+                    weigh_h_plane(*plane_steps[step - 1][0][:2])
+                limit_pair(step)
+                turn_slopes(step + 2, 0)
+                turn_slopes(step + 2, 1)
+                turn_h_plane(*plane_steps[step][0])
+                if step == 13:
+                    weigh_h_plane(*plane_steps[step][0][:2])
+            elif step % 2 == 0:
                 side_work(step)
                 stage1_run(step, 0, CUT_A)
                 turn_slopes(step + 2, 0)
@@ -563,9 +575,11 @@ def tile_modal_response_estimate_s7_kernel(
                     interleave_commands(first_actuator, WINDOWS[step], gpsimd_move, "shared%d" % step)
                     first_actuator += WINDOWS[step]
             if step == 2:
-                stage1_passes(1, 0, (0, 1), "h0")
+                stage1_passes(1, 0, (0,), "h0")
+                stage1_passes(0, 2, (2,), None)
                 stage1_passes(0, 0, (3,), None)
-                stage1_passes(0, 2, (2, 3), None)
+                stage1_passes(0, 2, (3,), None)
+                stage1_passes(1, 0, (1,), None)
                 turn_slopes(4, 0)
                 turn_slopes(4, 1)
                 stage1_passes(1, 2, (0, 1), "h1")

@@ -37,12 +37,12 @@ CUT_A = 6
 TWO_RUNS_FROM = 6
 CUT_B = 3
 SORTED = range(6, 16)
-H_PIECES = {12: (0, 0), 13: (0, 1), 14: (1, 0)}
+H_PIECES = {12: (0, 0), 13: (0, 1), 14: (1, 0), 15: (1, 1)}
 ROWS = (0, 0, 3, 3, 2, 2, 2, 2, 2, 2, 2, 2, 0, 0, 0, 0)
 WINDOWS = {0: 0, 1: 0, 2: 256, 3: 640, 5: 512, 7: 640, 9: 640, 11: 512, 13: 256, 14: 256, 15: 0}
 LAST_PLANES = {14: [(2, 2, "h0"), (2, 3, "h1")]}
 LATE_H = (0, 1)
-RECON_STEPS = {0: ((0, 0), (0, 1)), 1: ((1, 0), (2, 0), (1, 1)), 2: ((2, 1), (3, 0), (3, 1))}
+RECON_STEPS = {0: ((0, 0),), 1: ((0, 1), (1, 0), (1, 1)), 2: ((2, 0), (2, 1), (3, 1), (3, 0))}
 
 
 def tile_modal_response_estimate_s7_kernel(
@@ -60,7 +60,7 @@ def tile_modal_response_estimate_s7_kernel(
         psum = ctx.enter_context(tc.psum_pool(name="psum", bufs=1))
         ctx.enter_context(tc.manual_schedule())
 
-        scale = once.tile([P, PASSES, J], F32, name="scale")
+        scale = [once.tile([P, 2, J], F32, name="scale%d" % half) for half in range(2)]
         ident = once.tile([P, P], F32, name="ident")
         gain_rows = once.tile([P, P], BF16, name="gain_rows")
         gain_rows32 = once.tile([P, P], F32, name="gain_rows32")
@@ -115,10 +115,10 @@ def tile_modal_response_estimate_s7_kernel(
                 for half in halves:
                     byte_rows[unit, half, row] = row_bytes[:, row, half * HALF - k0 : (half + 1) * HALF - k0]
 
-        def load_first_bytes(b):
-            row_bytes = once.tile([P, 2, 512], U8, name="first_bytes%d" % b)
-            nc.sync.dma_start(out=row_bytes[:], in_=bytes_view[0][:, 0:2, 512 * b : 512 * (b + 1)])
-            first_bytes[b] = row_bytes
+        def load_first_bytes(b, row):
+            row_bytes = once.tile([P, 512], U8, name="first_bytes%d_%d" % (b, row))
+            nc.sync.dma_start(out=row_bytes[:], in_=bytes_view[0][:, row, 512 * b : 512 * (b + 1)])
+            first_bytes[b, row] = row_bytes
 
         def load_recon(g, parts):
             z0 = parts[0] * PIECE
@@ -178,18 +178,14 @@ def tile_modal_response_estimate_s7_kernel(
             widened[step, row] = wide
             nc.scalar.copy(out=wide[:], in_=byte_rows[unit, half, row].bitcast(E4M3))
 
-        def first_step(b):
-            wide = work.tile([P, 2, 512], BF16, name="wide", bufs=WIDE_BUFS)
-            nc.scalar.copy(
-                out=wide[:].rearrange("p r k -> p (r k)"),
-                in_=first_bytes[b][:].rearrange("p r k -> p (r k)").bitcast(E4M3),
-            )
-            bank = psum.tile([P, 2, UNIT], F32, name="turn%d" % b)
-            turned[0, b] = bank
-            for row in range(2):
-                words = wide[:, row, :].bitcast(F32)
-                for w in range(2):
-                    nc.tensor.transpose(bank[:, w, row * P : (row + 1) * P], words[:, w:256:2], ident[:])
+        def first_step(b, row):
+            wide = work.tile([P, 512], BF16, name="wide", bufs=WIDE_BUFS)
+            nc.scalar.copy(out=wide[:], in_=first_bytes[b, row][:].bitcast(E4M3))
+            bank = psum.tile([P, 2, P], F32, name=("turn%d", "h%d")[row] % b)
+            turned[0, b, row] = bank
+            words = wide[:].bitcast(F32)
+            for w in range(2):
+                nc.tensor.transpose(bank[:, w, :], words[:, w:256:2], ident[:])
 
         def sort_words(step, row):
             ordered = work.tile([P, 2, 2, P], F32, name="ordered", bufs=3)
@@ -223,13 +219,18 @@ def tile_modal_response_estimate_s7_kernel(
                 slopes_grouped[step, b] = tile
                 grouped = tile[:]
             g = 2 * (step % 2) + b
-            values = turned[step, b][:].rearrange("p w r -> p (w r)").bitcast(BF16)
-            nc.vector.tensor_tensor(
-                out=grouped.rearrange("p (r w e) -> p r w e", w=2, e=2),
-                in0=values.rearrange("p (w r e) -> p r w e", w=2, e=2),
-                in1=scale[:, g, :].rearrange("p (w e) -> p w e", e=2).unsqueeze(1).to_broadcast([P, UNIT, 2, 2]),
-                op=MULT,
-            )
+            if step == 0:
+                parts = [(turned[0, b, row], grouped[:, row * P * J : (row + 1) * P * J], P) for row in range(2)]
+            else:
+                parts = [(turned[step, b], grouped, UNIT)]
+            for bank, target, frames in parts:
+                values = bank[:].rearrange("p w r -> p (w r)").bitcast(BF16)
+                nc.vector.tensor_tensor(
+                    out=target.rearrange("p (r w e) -> p r w e", w=2, e=2),
+                    in0=values.rearrange("p (w r e) -> p r w e", w=2, e=2),
+                    in1=scale[g // 2][:, g % 2, :].rearrange("p (w e) -> p w e", e=2).unsqueeze(1).to_broadcast([P, frames, 2, 2]),
+                    op=MULT,
+                )
 
         def quantize_slopes(step, b=None):
             unit, half = divmod(step, 2)
@@ -350,9 +351,13 @@ def tile_modal_response_estimate_s7_kernel(
                 h_planes[g][:, :, part * PIECE : (part + 1) * PIECE],
             )
 
-        def quantize_h_group(g):
-            cols = slice(g * Z, (g + 1) * Z)
-            nc.vector.quantize_mx(out=h_codes[:, cols].bitcast(E4M3X4), scales=h_sbytes[:, cols], in_=h_group[g][:])
+        def quantize_h_group(g, first=0, count=MODE_BLOCKS):
+            cols = slice(g * Z + first * P, g * Z + (first + count) * P)
+            nc.vector.quantize_mx(
+                out=h_codes[:, cols].bitcast(E4M3X4),
+                scales=h_sbytes[:, cols],
+                in_=h_group[g][:, first * J * P : (first + count) * J * P],
+            )
 
         def weigh_h(g, mb):
             h_grouped[g, mb] = work.tile([P, J * P], BF16, name="h_grouped", bufs=4, align_bytes=64)
@@ -369,7 +374,7 @@ def tile_modal_response_estimate_s7_kernel(
                 out=h_codes[:, cols].bitcast(E4M3X4), scales=h_sbytes[:, cols], in_=h_grouped[g, mb][:]
             )
 
-        def stage2(mb, half, groups, bank_name=None):
+        def stage2(mb, half, groups, bank_name=None, last=PASSES - 1):
             if bank_name:
                 resp[mb, half] = psum.tile([P, COLS], F32, name=bank_name)
             for g in groups:
@@ -382,7 +387,7 @@ def tile_modal_response_estimate_s7_kernel(
                     rhs=com_codes[:, a0 : a0 + COLS].bitcast(E4M3X4),
                     rhs_scale=com_sbytes[:, a0 : a0 + COLS],
                     start=(g == 0),
-                    stop=(g == PASSES - 1),
+                    stop=(g == last),
                 )
 
         def last_tile(part, bank_name, move):
@@ -409,12 +414,16 @@ def tile_modal_response_estimate_s7_kernel(
             nc.sync.dma_start(out=out[mb * P : (mb + 1) * P, half * COLS : (half + 1) * COLS], in_=result[:])
 
         make_identity(nc, ident[:])
-        nc.scalar.dma_start(out=scale[:], in_=slopes_scale.rearrange("o (g p j) -> p (o g) j", p=P, j=J))
+        scale_view = slopes_scale.rearrange("o (g p j) -> p (o g) j", p=P, j=J)
+        nc.scalar.dma_start(out=scale[0][:], in_=scale_view[:, 0:2, :])
         nc.scalar.activation(out=gain_rows[:], in_=ident[:], func=COPY, scale=0.0)
-        load_first_bytes(0)
-        load_first_bytes(1)
+        load_first_bytes(0, 0)
+        load_first_bytes(0, 1)
+        load_first_bytes(1, 0)
+        load_first_bytes(1, 1)
         load_recon(0, (0, 1))
         load_bytes(0, (1,))
+        nc.sync.dma_start(out=scale[1][:], in_=scale_view[:, 2:4, :])
         load_recon(1, (0, 1))
         load_bytes(1, (0,))
         load_recon(2, (0, 1))
@@ -428,23 +437,23 @@ def tile_modal_response_estimate_s7_kernel(
         load_bytes(4, (0, 1))
         load_commands(1)
 
-        first_step(0)
-        first_step(1)
+        for b in range(2):
+            for row in range(2):
+                first_step(b, row)
         interleave_recon(0, 0, gpsimd_move, "shared2")
-        interleave_recon(0, 1, scalar_move, "shared3")
         widen(1, 0)
         widen(1, 1)
         turn_slopes(1, 0)
         turn_slopes(1, 1)
+        interleave_recon(0, 1, scalar_move, "shared3")
         interleave_recon(1, 0, scalar_move, "shared5")
         widen(2, 0)
         widen(2, 1)
-        interleave_recon(1, 1, scalar_move, "shared7")
-        interleave_recon(2, 1, scalar_move, "shared9")
+        interleave_recon(2, 0, scalar_move, "shared7")
         widen(3, 0)
         widen(3, 1)
         nc.scalar.copy(out=gain_rows32[:], in_=gain_rows[:])
-        interleave_recon(3, 0, scalar_move, "shared11")
+        interleave_recon(2, 1, scalar_move, "shared9")
 
         pairs = [(u, mb) for u in range(LAST) for mb in (0, 2)]
         stage1_steps = {i + 2: pair for i, pair in enumerate(pairs)}
@@ -551,18 +560,20 @@ def tile_modal_response_estimate_s7_kernel(
                 if step > 0 and step - 1 not in WINDOWS:
                     quantize_slopes(step - 1)
                 quantize_slopes(step, 0)
+                if step == 2:
+                    interleave_recon(3, 0, vector_move, "shared11")
                 for g, part in RECON_STEPS.get(step, ()):
                     quantize_recon(g, part)
                 quantize_slopes(step, 1)
                 if step == 0:
-                    interleave_recon(2, 0, gpsimd_move, "shared0")
+                    interleave_recon(1, 1, gpsimd_move, "shared0")
                     stage1_passes(0, 0, (0,), "acc0")
-                    stage1_passes(0, 2, (0,), "acc1")
                     turn_slopes(2, 0)
                     turn_slopes(2, 1)
                 elif step == 1:
                     interleave_recon(3, 1, gpsimd_move, "shared1")
-                    stage1_passes(0, 0, (1, 2), None)
+                    stage1_passes(0, 2, (0,), "acc1")
+                    stage1_passes(0, 0, (1,), None)
                     stage1_passes(0, 2, (1,), None)
                     gain_bank = psum.tile([P, P], F32, name="h0")
                     nc.tensor.transpose(gain_bank[:], gain_rows32[:], ident[:])
@@ -576,9 +587,10 @@ def tile_modal_response_estimate_s7_kernel(
                     first_actuator += WINDOWS[step]
             if step == 2:
                 stage1_passes(1, 0, (0,), "h0")
+                stage1_passes(0, 0, (2,), None)
                 stage1_passes(0, 2, (2,), None)
-                stage1_passes(0, 0, (3,), None)
                 stage1_passes(0, 2, (3,), None)
+                stage1_passes(0, 0, (3,), None)
                 stage1_passes(1, 0, (1,), None)
                 turn_slopes(4, 0)
                 turn_slopes(4, 1)
@@ -606,57 +618,62 @@ def tile_modal_response_estimate_s7_kernel(
 
         for plane in plane_steps.get(STEPS - 1, ()):
             weigh_h_plane(*plane[:2])
-        for mb in (0, 2):
-            stage1_passes(LAST, mb, (2, 3), None)
+        for g in (2, 3):
+            for mb in (0, 2):
+                stage1_passes(LAST, mb, (g,), None)
+        for mb in range(MODE_BLOCKS):
             limit(LAST, mb)
-            limit(LAST, mb + 1)
         for part in LATE_H:
             interleave_h(2, part)
         interleave_commands(first_actuator, PASSES * A - first_actuator, scalar_move, "shared15")
         quantize_commands(0, 0)
-        quantize_h_group(0)
+        quantize_h_group(0, 0, 1)
+        quantize_h_group(0, 1, 1)
+        quantize_h_group(0, 2, 2)
         quantize_commands(0, 1)
-        for half in range(2):
-            for mb in range(3):
-                one_pass(0, mb, half)
-        turn_h(3, 0, "acc0")
-        turn_h(3, 1, "acc1")
-        interleave_h(1, 1, vector_move)
         quantize_commands(1, 0)
         quantize_h_group(1)
         quantize_commands(1, 1)
+        for half, mb in ((0, 0), (0, 1), (0, 2), (1, 0), (1, 1)):
+            one_pass(0, mb, half)
+        turn_h(3, 0, "acc0")
+        turn_h(3, 1, "acc1")
+        for mb in range(3):
+            one_pass(1, mb, 0)
+        one_pass(0, 2, 1)
+        for mb in range(3):
+            one_pass(1, mb, 1)
         weigh_h(3, 0)
-        for half in range(2):
-            for mb in range(3):
-                one_pass(1, mb, half)
+        weigh_h(3, 1)
         turn_h(3, 2, "acc0")
+        turn_h(3, 3, "acc1")
         quantize_commands(2, 0)
-        quantize_h_group(2)
         quantize_h(3, 0)
         quantize_commands(3, 0)
-        weigh_h(3, 1)
-        quantize_commands(2, 1)
         quantize_h(3, 1)
+        quantize_h_group(2)
+        quantize_commands(2, 1)
         weigh_h(3, 2)
         quantize_commands(3, 1)
         quantize_h(3, 2)
-        for mb in range(3):
-            one_pass(2, mb, 0)
-        one_pass(3, 0, 0)
-        store(0, 0, scalar_move)
-        turn_h(3, 3, "acc1")
         weigh_h(3, 3)
         quantize_h(3, 3)
-        one_pass(3, 1, 0)
-        store(1, 0, scalar_move)
+        for mb in range(2):
+            stage2(mb, 0, (3,), last=2)
+        for mb in range(2):
+            stage2(mb, 0, (2,), last=2)
+            store(mb, 0, scalar_move)
+        one_pass(2, 2, 0)
         for mb in range(3):
             one_pass(2, mb, 1)
-        one_pass(3, 2, 0)
+        one_pass(3, 0, 1)
+        store(0, 1, scalar_move)
+        one_pass(3, 1, 1)
+        store(1, 1, vector_move)
+        passes(3, 2)
         store(2, 0, scalar_move)
-        for mb in range(3):
-            one_pass(3, mb, 1)
-            store(mb, 1, vector_move if mb == 1 else scalar_move)
+        store(2, 1, vector_move)
         stage2(3, 0, (0, 1, 2, 3), "turn2")
-        store(3, 0, vector_move)
-        last_tile(0, "h0", scalar_move)
-        last_tile(1, "acc0", vector_move)
+        store(3, 0, scalar_move)
+        last_tile(0, "h0", vector_move)
+        last_tile(1, "acc0", scalar_move)

@@ -34,9 +34,9 @@ WIDE_BUFS = 8
 FIRST_PLANE = 4
 HPB = 3
 CUT_A = 6
-TWO_RUNS_FROM = 6
+TWO_RUNS_FROM = 10
 CUT_B = 3
-SORTED = range(6, 16)
+SORTED = (6, 7, 9, 11, 12, 13, 14, 15)
 H_PIECES = {12: (0, 0), 13: (0, 1), 14: (1, 0), 15: (1, 1)}
 ROWS = (0, 0, 3, 3, 2, 2, 2, 2, 2, 2, 2, 2, 0, 0, 0, 0)
 WINDOWS = {0: 0, 1: 0, 2: 256, 3: 640, 5: 512, 7: 640, 9: 640, 11: 512, 13: 256, 14: 256, 15: 0}

@@ -415,7 +415,7 @@ def tile_modal_response_estimate_s7_kernel(
 
         make_identity(nc, ident[:])
         scale_view = slopes_scale.rearrange("o (g p j) -> p (o g) j", p=P, j=J)
-        nc.scalar.dma_start(out=scale[0][:], in_=scale_view[:, 0:2, :])
+        nc.sync.dma_start(out=scale[0][:], in_=scale_view[:, 0:2, :])
         nc.scalar.activation(out=gain_rows[:], in_=ident[:], func=COPY, scale=0.0)
         load_first_bytes(0, 0)
         load_first_bytes(0, 1)

@@ -23,26 +23,22 @@ PASSES = 4
 HALF = S // 2
 UNIT = 2 * P
 UNITS = T // UNIT
-STEPS = 2 * UNITS
 LAST = UNITS - 1
 MODE_BLOCKS = Z // P
 COLS = 512
 PIECE = 256
-
-TURN_BANKS = 4
-WIDE_BUFS = 8
-FIRST_PLANE = 4
-HPB = 3
+WIDE_BUFS = 14
+SORTS = (6, 7, 8, 9, 10, 11, 12, 13, 14, 15)
+FOUR_FROM = 3
 CUT_A = 6
-TWO_RUNS_FROM = 10
 CUT_B = 3
-SORTED = (6, 7, 9, 11, 12, 13, 14, 15)
-H_PIECES = {12: (0, 0), 13: (0, 1), 14: (1, 0), 15: (1, 1)}
-ROWS = (0, 0, 3, 3, 2, 2, 2, 2, 2, 2, 2, 2, 0, 0, 0, 0)
-WINDOWS = {0: 0, 1: 0, 2: 256, 3: 640, 5: 512, 7: 640, 9: 640, 11: 512, 13: 256, 14: 256, 15: 0}
-LAST_PLANES = {14: [(2, 2, "h0"), (2, 3, "h1")]}
-LATE_H = (0, 1)
-RECON_STEPS = {0: ((0, 0),), 1: ((0, 1), (1, 0), (1, 1)), 2: ((2, 0), (2, 1), (3, 1), (3, 0))}
+F0 = 7
+F1 = 3
+F1B = 1
+F2 = 4
+FA = 2
+FB = 4
+RESP_BANKS = (("acc0", "acc1", "turn2", "turn3"), ("turn0", "turn1", "h0", "h1"))
 
 
 def tile_modal_response_estimate_s7_kernel(
@@ -76,13 +72,10 @@ def tile_modal_response_estimate_s7_kernel(
         h_sbytes = once.tile([P, PASSES * Z], U8, name="h_sbytes", align_bytes=64)
 
         byte_rows = {}
-        first_bytes = {}
         recon_raw = {}
         recon_grouped = {}
-        recon_banks = {}
-        acc_bank = {}
         com_raw = {}
-        com_grouped = []
+        com_grouped = {}
         widened = {}
         sorted_words = {}
         turned = {}
@@ -91,9 +84,8 @@ def tile_modal_response_estimate_s7_kernel(
         acc = {}
         h_raw = {}
         h_turned = {}
-        h_grouped = {}
         h_planes = {}
-        h_group = {}
+        h_grouped = {}
         resp = {}
 
         def scalar_move(out, in_):
@@ -104,6 +96,12 @@ def tile_modal_response_estimate_s7_kernel(
 
         def vector_move(out, in_):
             nc.vector.tensor_copy(out=out, in_=in_)
+
+        def interleave(move, grouped, raw):
+            move(
+                grouped.rearrange("p (c i j) -> p c j i", i=4, j=J),
+                raw.rearrange("p j (c i) -> p c j i", i=4),
+            )
 
         def load_bytes(unit, halves):
             g, pair = divmod(unit, 2)
@@ -118,283 +116,214 @@ def tile_modal_response_estimate_s7_kernel(
         def load_first_bytes(b, row):
             row_bytes = once.tile([P, 512], U8, name="first_bytes%d_%d" % (b, row))
             nc.sync.dma_start(out=row_bytes[:], in_=bytes_view[0][:, row, 512 * b : 512 * (b + 1)])
-            first_bytes[b, row] = row_bytes
+            byte_rows["first", b, row] = row_bytes[:]
 
         def load_recon(g, parts):
             z0 = parts[0] * PIECE
             raw = once.tile([P, J, len(parts) * PIECE], BF16, name="recon_raw%d_%d" % (g, parts[0]))
             nc.sync.dma_start(out=raw[:], in_=recon_view[g][:, :, z0 : z0 + len(parts) * PIECE])
+            recon_raw[g, parts] = raw[:]
             for i, part in enumerate(parts):
-                recon_raw[g, part] = raw[:, :, i * PIECE : (i + 1) * PIECE]
+                recon_raw[g, (part,)] = raw[:, :, i * PIECE : (i + 1) * PIECE]
 
-        def load_commands(g):
-            raw = work.tile([P, J, A], BF16, name="com_raw", bufs=3)
-            nc.sync.dma_start(out=raw[:], in_=commands_view[g])
-            com_raw[g] = raw
+        def load_commands(g, half):
+            raw = work.tile([P, J, COLS], BF16, name="com_raw", bufs=4)
+            nc.sync.dma_start(out=raw[:], in_=commands_view[g][:, :, half * COLS : (half + 1) * COLS])
+            com_raw[g, half] = raw
 
-        def interleave(move, grouped, raw):
-            move(
-                grouped.rearrange("p (c i j) -> p c j i", i=4, j=J),
-                raw.rearrange("p j (c i) -> p c j i", i=4),
-            )
+        def interleave_recon(g, parts, move, name):
+            grouped = once.tile([P, J * len(parts) * PIECE], BF16, name=name, align_bytes=64)
+            interleave(move, grouped[:], recon_raw[g, parts])
+            recon_grouped[g, parts] = grouped
 
-        def interleave_recon(g, part, move, name):
-            grouped = once.tile([P, J * PIECE], BF16, name=name, align_bytes=64)
-            interleave(move, grouped[:], recon_raw[g, part])
-            recon_grouped[g, part] = grouped
-
-        def quantize_recon(g, part):
-            cols = slice(g * Z + part * PIECE, g * Z + (part + 1) * PIECE)
+        def quantize_recon(g, parts):
+            cols = slice(g * Z + parts[0] * PIECE, g * Z + (parts[-1] + 1) * PIECE)
             nc.vector.quantize_mx(
-                out=recon_codes[:, cols].bitcast(E4M3X4), scales=recon_sbytes[:, cols], in_=recon_grouped[g, part][:]
+                out=recon_codes[:, cols].bitcast(E4M3X4), scales=recon_sbytes[:, cols], in_=recon_grouped[g, parts][:]
             )
 
-        def interleave_commands(first, count, move, name):
-            grouped = once.tile([P, J * count], BF16, name=name, align_bytes=64)
-            done = 0
-            while done < count:
-                g, a0 = divmod(first + done, A)
-                width = min(count - done, A - a0)
-                interleave(move, grouped[:, J * done : J * (done + width)], com_raw[g][:, :, a0 : a0 + width])
-                done += width
-            com_grouped.append((first, count, grouped))
+        def interleave_commands(g, half, move, name=None, first=0, count=COLS):
+            if name:
+                com_grouped[g, half] = once.tile([P, J * COLS], BF16, name=name, align_bytes=64)
+            interleave(
+                move,
+                com_grouped[g, half][:, J * first : J * (first + count)],
+                com_raw[g, half][:, :, first : first + count],
+            )
 
-        def quantize_commands(g, half):
-            lo = g * A + half * COLS
-            hi = lo + COLS
-            for first, count, grouped in com_grouped:
-                c0 = max(lo, first)
-                c1 = min(hi, first + count)
-                if c0 < c1:
-                    nc.vector.quantize_mx(
-                        out=com_codes[:, c0:c1].bitcast(E4M3X4),
-                        scales=com_sbytes[:, c0:c1],
-                        in_=grouped[:, J * (c0 - first) : J * (c1 - first)],
-                    )
+        def quantize_commands(g, half, first=0, count=COLS):
+            c0 = g * A + half * COLS + first
+            nc.vector.quantize_mx(
+                out=com_codes[:, c0 : c0 + count].bitcast(E4M3X4),
+                scales=com_sbytes[:, c0 : c0 + count],
+                in_=com_grouped[g, half][:, J * first : J * (first + count)],
+            )
 
-        def widen(step, row):
-            unit, half = divmod(step, 2)
+        def widen(unit, half, row):
             wide = work.tile([P, HALF], BF16, name="wide", bufs=WIDE_BUFS)
-            widened[step, row] = wide
+            widened[unit, half, row] = wide
             nc.scalar.copy(out=wide[:], in_=byte_rows[unit, half, row].bitcast(E4M3))
 
-        def first_step(b, row):
+        def first_turn(b, row):
             wide = work.tile([P, 512], BF16, name="wide", bufs=WIDE_BUFS)
-            nc.scalar.copy(out=wide[:], in_=first_bytes[b, row][:].bitcast(E4M3))
+            nc.scalar.copy(out=wide[:], in_=byte_rows["first", b, row].bitcast(E4M3))
             bank = psum.tile([P, 2, P], F32, name=("turn%d", "h%d")[row] % b)
-            turned[0, b, row] = bank
+            turned["first", b, row] = bank
             words = wide[:].bitcast(F32)
             for w in range(2):
                 nc.tensor.transpose(bank[:, w, :], words[:, w:256:2], ident[:])
 
-        def sort_words(step, row):
-            ordered = work.tile([P, 2, 2, P], F32, name="ordered", bufs=3)
+        def sort_words(unit, half):
+            ordered = work.tile([P, 2, 2, P], F32, name="ordered", bufs=6)
             nc.scalar.copy(
-                out=ordered[:], in_=widened[step, row][:].bitcast(F32).rearrange("p (b m w) -> p b w m", b=2, w=2)
+                out=ordered[:], in_=widened[unit, half, 1][:].bitcast(F32).rearrange("p (b m w) -> p b w m", b=2, w=2)
             )
-            sorted_words[step, row] = ordered
+            sorted_words[unit, half] = ordered
 
-        def turn_slopes(step, b):
-            bank = psum.tile([P, 2, UNIT], F32, name="turn%d" % ((2 * step + b) % TURN_BANKS))
-            turned[step, b] = bank
+        def turn_slopes(unit, g):
+            half, b = divmod(g, 2)
+            bank = psum.tile([P, 2, UNIT], F32, name="turn%d" % g)
+            turned[unit, g] = bank
             for row in range(2):
-                words = widened[step, row][:].bitcast(F32)
+                words = widened[unit, half, row][:].bitcast(F32)
                 for w in range(2):
-                    if (step, row) in sorted_words:
-                        source = sorted_words[step, row][:, b, w, :]
+                    if row == 1 and (unit, half) in sorted_words:
+                        source = sorted_words[unit, half][:, b, w, :]
                     else:
                         source = words[:, 256 * b + w : 256 * (b + 1) : 2]
                     nc.tensor.transpose(bank[:, w, row * P : (row + 1) * P], source, ident[:])
 
-        def scale_slopes(step, b):
-            if step not in WINDOWS:
-                if b == 0:
-                    slopes_grouped[step] = work.tile([P, 2 * UNIT * J], BF16, name="step_grouped", bufs=2, align_bytes=64)
-                grouped = slopes_grouped[step][:, b * UNIT * J : (b + 1) * UNIT * J]
+        def scale_slopes(unit, g):
+            half, b = divmod(g, 2)
+            if b == 0 and half == 0:
+                slopes_grouped[unit, half] = once.tile([P, 2 * UNIT * J], BF16, name="held%d" % (unit % LAST), align_bytes=64)
+            if b == 0 and half == 1:
+                slopes_grouped[unit, half] = work.tile([P, 2 * UNIT * J], BF16, name="second_half", bufs=1, align_bytes=64)
+            grouped = slopes_grouped[unit, half][:, b * UNIT * J : (b + 1) * UNIT * J]
+            if unit == 0 and half == 0:
+                parts = [(turned["first", b, row], grouped[:, row * P * J : (row + 1) * P * J], P) for row in range(2)]
             else:
-                if b == 0:
-                    tile = work.tile([P, UNIT * J], BF16, name="bank_grouped", bufs=2, align_bytes=64)
-                else:
-                    tile = once.tile([P, UNIT * J], BF16, name="shared%d" % step, align_bytes=64)
-                slopes_grouped[step, b] = tile
-                grouped = tile[:]
-            g = 2 * (step % 2) + b
-            if step == 0:
-                parts = [(turned[0, b, row], grouped[:, row * P * J : (row + 1) * P * J], P) for row in range(2)]
-            else:
-                parts = [(turned[step, b], grouped, UNIT)]
+                parts = [(turned[unit, g], grouped, UNIT)]
             for bank, target, frames in parts:
                 values = bank[:].rearrange("p w r -> p (w r)").bitcast(BF16)
                 nc.vector.tensor_tensor(
                     out=target.rearrange("p (r w e) -> p r w e", w=2, e=2),
                     in0=values.rearrange("p (w r e) -> p r w e", w=2, e=2),
-                    in1=scale[g // 2][:, g % 2, :].rearrange("p (w e) -> p w e", e=2).unsqueeze(1).to_broadcast([P, frames, 2, 2]),
+                    in1=scale[half][:, b, :].rearrange("p (w e) -> p w e", e=2).unsqueeze(1).to_broadcast([P, frames, 2, 2]),
                     op=MULT,
                 )
 
-        def quantize_slopes(step, b=None):
-            unit, half = divmod(step, 2)
-            if half == 0 and not b:
+        def quantize_slopes(unit, first, count):
+            if first == 0:
                 slope_codes[unit] = (
                     work.tile([P, PASSES * UNIT], U32, name="slope_codes", bufs=3, align_bytes=64),
                     work.tile([P, PASSES * UNIT], U8, name="slope_sbytes", bufs=3, align_bytes=64),
                 )
             codes, sbytes = slope_codes[unit]
-            if b is None:
-                cols = slice(2 * half * UNIT, (2 * half + 2) * UNIT)
-                grouped = slopes_grouped[step]
-            else:
-                cols = slice((2 * half + b) * UNIT, (2 * half + b + 1) * UNIT)
-                grouped = slopes_grouped[step, b]
-            nc.vector.quantize_mx(out=codes[:, cols].bitcast(E4M3X4), scales=sbytes[:, cols], in_=grouped[:])
+            half, b = divmod(first, 2)
+            cols = slice(first * UNIT, (first + count) * UNIT)
+            nc.vector.quantize_mx(
+                out=codes[:, cols].bitcast(E4M3X4),
+                scales=sbytes[:, cols],
+                in_=slopes_grouped[unit, half][:, b * UNIT * J : (b + count) * UNIT * J],
+            )
 
-        def stage1(unit, blocks, bank_name):
-            bank = psum.tile([P, 2, UNIT], F32, name=bank_name)
-            codes, sbytes = slope_codes[unit]
-            for i, mb in enumerate(blocks):
-                for g in range(PASSES):
-                    z0 = g * Z + mb * P
-                    r0 = g * UNIT
-                    nc.tensor.matmul_mx(
-                        out=bank[:, i, :],
-                        lhsT=recon_codes[:, z0 : z0 + P].bitcast(E4M3X4),
-                        lhsT_scale=recon_sbytes[:, z0 : z0 + P],
-                        rhs=codes[:, r0 : r0 + UNIT].bitcast(E4M3X4),
-                        rhs_scale=sbytes[:, r0 : r0 + UNIT],
-                        start=(g == 0),
-                        stop=(g == PASSES - 1),
-                    )
-                acc[unit, mb] = bank[:, i, :]
-
-        def stage1_run(step, first, last):
-            unit, mb0 = stage1_steps[step]
+        def stage1(unit, pair, first, last, bank_name=None):
             if first == 0:
-                acc_bank[unit, mb0] = psum.tile([P, 2, UNIT], F32, name="acc%d" % (step % 2))
-            bank = acc_bank[unit, mb0]
+                acc[unit, pair] = psum.tile([P, 2, UNIT], F32, name=bank_name or "acc%d" % pair)
             codes, sbytes = slope_codes[unit]
             for n in range(first, last):
-                i, g = divmod(n, PASSES)
-                z0 = g * Z + (mb0 + i) * P
+                g, i = divmod(n, 2)
+                z0 = g * Z + (2 * pair + i) * P
                 r0 = g * UNIT
                 nc.tensor.matmul_mx(
-                    out=bank[:, i, :],
+                    out=acc[unit, pair][:, i, :],
                     lhsT=recon_codes[:, z0 : z0 + P].bitcast(E4M3X4),
                     lhsT_scale=recon_sbytes[:, z0 : z0 + P],
                     rhs=codes[:, r0 : r0 + UNIT].bitcast(E4M3X4),
                     rhs_scale=sbytes[:, r0 : r0 + UNIT],
-                    start=(g == 0),
-                    stop=(g == PASSES - 1),
+                    start=(n == 0),
+                    stop=(n == 2 * PASSES - 1),
                 )
-                acc[unit, mb0 + i] = bank[:, i, :]
 
-        def limit_pair(step):
-            unit, mb0 = stage1_steps[step]
-            limit(unit, mb0)
-            limit(unit, mb0 + 1)
+        def limit(unit, pair):
+            for i in range(2):
+                mb = 2 * pair + i
+                h_raw[unit, mb] = work.tile([P, UNIT], F32, name="h_raw", bufs=12)
+                nc.scalar.activation(
+                    out=h_raw[unit, mb][:], in_=acc[unit, pair][:, i, :], func=TANH, scale=gain_cols[:, mb : mb + 1]
+                )
 
-        def stage1_passes(unit, mb0, groups, bank_name):
-            if groups[0] == 0:
-                acc_bank[unit, mb0] = psum.tile([P, 2, UNIT], F32, name=bank_name)
-            bank = acc_bank[unit, mb0]
-            codes, sbytes = slope_codes[unit]
-            for g in groups:
-                for i in range(2):
-                    z0 = g * Z + (mb0 + i) * P
-                    r0 = g * UNIT
-                    nc.tensor.matmul_mx(
-                        out=bank[:, i, :],
-                        lhsT=recon_codes[:, z0 : z0 + P].bitcast(E4M3X4),
-                        lhsT_scale=recon_sbytes[:, z0 : z0 + P],
-                        rhs=codes[:, r0 : r0 + UNIT].bitcast(E4M3X4),
-                        rhs_scale=sbytes[:, r0 : r0 + UNIT],
-                        start=(g == 0 and i == 0),
-                        stop=(g == PASSES - 1 and i == 1),
-                    )
-                    acc[unit, mb0 + i] = bank[:, i, :]
-
-        def limit(unit, mb):
-            g, pair = divmod(unit, 2)
-            if pair == 0:
-                h_raw[g, mb] = work.tile([P, J * P], F32, name="h_raw", bufs=8)
-            nc.scalar.activation(
-                out=h_raw[g, mb][:, pair * UNIT : (pair + 1) * UNIT],
-                in_=acc[unit, mb],
-                func=TANH,
-                scale=gain_cols[:, mb : mb + 1],
-            )
-
-        def turn_h(g, mb, bank_name):
-            bank = psum.tile([P, J * P], F32, name=bank_name)
-            for t in range(J):
-                nc.tensor.transpose(bank[:, t * P : (t + 1) * P], h_raw[g, mb][:, t * P : (t + 1) * P], ident[:])
-            h_turned[g, mb] = bank
-
-        def turn_h_plane(g, t, bank_name):
-            bank = psum.tile([P, Z], F32, name=bank_name)
+        def turn_plane(unit, row, bank_name=None):
+            bank = psum.tile([P, Z], F32, name=bank_name or "h%d" % row)
             for mb in range(MODE_BLOCKS):
-                nc.tensor.transpose(bank[:, mb * P : (mb + 1) * P], h_raw[g, mb][:, t * P : (t + 1) * P], ident[:])
-            h_turned[g, t] = bank
+                nc.tensor.transpose(bank[:, mb * P : (mb + 1) * P], h_raw[unit, mb][:, row * P : (row + 1) * P], ident[:])
+            h_turned[unit, row] = bank
 
-        def weigh_h_plane(g, t):
+        def weigh_plane(unit, row):
+            g, t = divmod(2 * unit + row, J)
             if t == 0:
-                h_planes[g] = work.tile([P, J, Z], BF16, name="h_planes", bufs=HPB)
+                h_planes[g] = work.tile([P, J, Z], BF16, name="h_planes", bufs=3)
             nc.scalar.activation(
-                out=h_planes[g][:, t, :], in_=h_turned[g, t][:], func=COPY, scale=weight32[:, g, t : t + 1]
+                out=h_planes[g][:, t, :], in_=h_turned[unit, row][:], func=COPY, scale=weight32[:, g, t : t + 1]
             )
 
-        def interleave_h(g, part, move=scalar_move):
-            if part == 0:
-                h_group[g] = once.tile([P, J * Z], BF16, name="h_group%d" % g, align_bytes=64)
+        def turn_last(pair):
+            bank = psum.tile([P, 2, PIECE], F32, name="h%d" % pair)
+            for row in range(2):
+                for i in range(2):
+                    nc.tensor.transpose(
+                        bank[:, row, i * P : (i + 1) * P], h_raw[LAST, 2 * pair + i][:, row * P : (row + 1) * P], ident[:]
+                    )
+            h_turned["last", pair] = bank
+
+        def weigh_last(pair):
+            for row in range(2):
+                g, t = divmod(2 * LAST + row, J)
+                nc.scalar.activation(
+                    out=h_planes[g][:, t, pair * PIECE : (pair + 1) * PIECE],
+                    in_=h_turned["last", pair][:, row, :],
+                    func=COPY,
+                    scale=weight32[:, g, t : t + 1],
+                )
+
+        def interleave_h(g, pair, move):
+            if pair == 0:
+                h_grouped[g] = once.tile([P, J * Z], BF16, name="h_grouped%d" % g, align_bytes=64)
             interleave(
                 move,
-                h_group[g][:, part * J * PIECE : (part + 1) * J * PIECE],
-                h_planes[g][:, :, part * PIECE : (part + 1) * PIECE],
+                h_grouped[g][:, pair * J * PIECE : (pair + 1) * J * PIECE],
+                h_planes[g][:, :, pair * PIECE : (pair + 1) * PIECE],
             )
 
-        def quantize_h_group(g, first=0, count=MODE_BLOCKS):
+        def quantize_h(g, first=0, count=MODE_BLOCKS):
             cols = slice(g * Z + first * P, g * Z + (first + count) * P)
             nc.vector.quantize_mx(
                 out=h_codes[:, cols].bitcast(E4M3X4),
                 scales=h_sbytes[:, cols],
-                in_=h_group[g][:, first * J * P : (first + count) * J * P],
+                in_=h_grouped[g][:, first * J * P : (first + count) * J * P],
             )
 
-        def weigh_h(g, mb):
-            h_grouped[g, mb] = work.tile([P, J * P], BF16, name="h_grouped", bufs=4, align_bytes=64)
-            nc.vector.tensor_tensor(
-                out=h_grouped[g, mb][:].rearrange("p (z t) -> p z t", t=J),
-                in0=h_turned[g, mb][:].rearrange("p (t z) -> p z t", t=J),
-                in1=weight[:, g, :].unsqueeze(1).to_broadcast([P, P, J]),
-                op=MULT,
+        def stage2(mb, half, g, first=0, count=COLS):
+            if g == 0 and first == 0:
+                resp[mb, half] = psum.tile([P, COLS], F32, name=RESP_BANKS[half][mb])
+            z0 = g * Z + mb * P
+            a0 = g * A + half * COLS + first
+            nc.tensor.matmul_mx(
+                out=resp[mb, half][:, first : first + count],
+                lhsT=h_codes[:, z0 : z0 + P].bitcast(E4M3X4),
+                lhsT_scale=h_sbytes[:, z0 : z0 + P],
+                rhs=com_codes[:, a0 : a0 + count].bitcast(E4M3X4),
+                rhs_scale=com_sbytes[:, a0 : a0 + count],
+                start=(g == 0 and first == 0),
+                stop=(g == PASSES - 1 and first + count == COLS),
             )
-
-        def quantize_h(g, mb):
-            cols = slice(g * Z + mb * P, g * Z + (mb + 1) * P)
-            nc.vector.quantize_mx(
-                out=h_codes[:, cols].bitcast(E4M3X4), scales=h_sbytes[:, cols], in_=h_grouped[g, mb][:]
-            )
-
-        def stage2(mb, half, groups, bank_name=None, last=PASSES - 1):
-            if bank_name:
-                resp[mb, half] = psum.tile([P, COLS], F32, name=bank_name)
-            for g in groups:
-                z0 = g * Z + mb * P
-                a0 = g * A + half * COLS
-                nc.tensor.matmul_mx(
-                    out=resp[mb, half][:],
-                    lhsT=h_codes[:, z0 : z0 + P].bitcast(E4M3X4),
-                    lhsT_scale=h_sbytes[:, z0 : z0 + P],
-                    rhs=com_codes[:, a0 : a0 + COLS].bitcast(E4M3X4),
-                    rhs_scale=com_sbytes[:, a0 : a0 + COLS],
-                    start=(g == 0),
-                    stop=(g == last),
-                )
 
         def last_tile(part, bank_name, move):
             bank = psum.tile([P, PIECE], F32, name=bank_name)
             a0 = COLS + part * PIECE
             for g in range(PASSES):
-                z0 = g * Z + 3 * P
+                z0 = g * Z + (MODE_BLOCKS - 1) * P
                 nc.tensor.matmul_mx(
                     out=bank[:],
                     lhsT=h_codes[:, z0 : z0 + P].bitcast(E4M3X4),
@@ -406,12 +335,13 @@ def tile_modal_response_estimate_s7_kernel(
                 )
             result = work.tile([P, PIECE], F32, name="wide", bufs=WIDE_BUFS)
             move(result[:], bank[:])
-            nc.sync.dma_start(out=out[3 * P : 4 * P, a0 : a0 + PIECE], in_=result[:])
+            nc.sync.dma_start(out=out[(MODE_BLOCKS - 1) * P :, a0 : a0 + PIECE], in_=result[:])
 
-        def store(mb, half, move):
-            result = work.tile([P, COLS], F32, name="wide", bufs=WIDE_BUFS)
-            move(result[:], resp[mb, half][:])
-            nc.sync.dma_start(out=out[mb * P : (mb + 1) * P, half * COLS : (half + 1) * COLS], in_=result[:])
+        def store(mb, half, move, first=0, count=COLS):
+            result = work.tile([P, count], F32, name="wide", bufs=WIDE_BUFS)
+            move(result[:], resp[mb, half][:, first : first + count])
+            a0 = half * COLS + first
+            nc.sync.dma_start(out=out[mb * P : (mb + 1) * P, a0 : a0 + count], in_=result[:])
 
         make_identity(nc, ident[:])
         scale_view = slopes_scale.rearrange("o (g p j) -> p (o g) j", p=P, j=J)
@@ -419,261 +349,256 @@ def tile_modal_response_estimate_s7_kernel(
         nc.scalar.activation(out=gain_rows[:], in_=ident[:], func=COPY, scale=0.0)
         load_first_bytes(0, 0)
         load_first_bytes(0, 1)
+        load_recon(0, (0,))
         load_first_bytes(1, 0)
         load_first_bytes(1, 1)
-        load_recon(0, (0, 1))
+        load_recon(0, (1,))
         load_bytes(0, (1,))
         nc.sync.dma_start(out=scale[1][:], in_=scale_view[:, 2:4, :])
         load_recon(1, (0, 1))
         load_bytes(1, (0,))
+        load_bytes(1, (1,))
+        nc.sync.dma_start(out=gain_rows[0:MODE_BLOCKS, :], in_=gain.rearrange("(c p) -> c p", p=P))
         load_recon(2, (0, 1))
         load_recon(3, (0, 1))
-        load_bytes(1, (1,))
         load_bytes(2, (0, 1))
-        nc.sync.dma_start(out=gain_rows[0:MODE_BLOCKS, :], in_=gain.rearrange("(c p) -> c p", p=P))
-        load_commands(0)
         load_bytes(3, (0, 1))
+        load_commands(0, 0)
+        load_commands(2, 1)
         nc.sync.dma_start(out=weight[:], in_=frame_weight.rearrange("(g p t) -> p g t", p=P, t=J))
         load_bytes(4, (0, 1))
-        load_commands(1)
+        load_commands(1, 0)
+        load_bytes(5, (0, 1))
+        load_commands(2, 0)
 
         for b in range(2):
             for row in range(2):
-                first_step(b, row)
-        interleave_recon(0, 0, gpsimd_move, "shared2")
-        widen(1, 0)
-        widen(1, 1)
+                first_turn(b, row)
+        interleave_recon(0, (0,), vector_move, "early0")
+        interleave_recon(0, (1,), gpsimd_move, "early1")
+        scale_slopes(0, 0)
+        scale_slopes(0, 1)
+        widen(0, 1, 0)
+        widen(0, 1, 1)
+        turn_slopes(0, 2)
+        turn_slopes(0, 3)
+        interleave_recon(1, (1,), scalar_move, "early2")
+        widen(1, 0, 0)
+        widen(1, 0, 1)
+        quantize_recon(0, (0,))
+        quantize_slopes(0, 0, 1)
+        quantize_recon(0, (1,))
+        quantize_slopes(0, 1, 1)
+        interleave_recon(1, (0,), gpsimd_move, "early1")
         turn_slopes(1, 0)
         turn_slopes(1, 1)
-        interleave_recon(0, 1, scalar_move, "shared3")
-        interleave_recon(1, 0, scalar_move, "shared5")
-        widen(2, 0)
-        widen(2, 1)
-        interleave_recon(2, 0, scalar_move, "shared7")
-        widen(3, 0)
-        widen(3, 1)
+        scale_slopes(0, 2)
+        scale_slopes(0, 3)
+        widen(1, 1, 0)
+        widen(1, 1, 1)
         nc.scalar.copy(out=gain_rows32[:], in_=gain_rows[:])
-        interleave_recon(2, 1, scalar_move, "shared9")
+        interleave_recon(2, (0,), scalar_move, "early0")
+        quantize_recon(1, (0,))
+        quantize_recon(1, (1,))
+        quantize_slopes(0, 2, 2)
 
-        pairs = [(u, mb) for u in range(LAST) for mb in (0, 2)]
-        stage1_steps = {i + 2: pair for i, pair in enumerate(pairs)}
+        fillers = []
+        for unit in range(2, UNITS):
+            for half in range(2):
+                fillers.append((widen, (unit, half, 1)))
+                fillers.append((widen, (unit, half, 0)))
+                if 2 * unit + half in SORTS:
+                    fillers.append((sort_words, (unit, half)))
 
-        def stage1_step(step):
-            unit, mb = stage1_steps[step]
-            stage1(unit, (mb, mb + 1), "acc%d" % (step % 2))
-            limit(unit, mb)
-            limit(unit, mb + 1)
+        def fill(count):
+            for job, args in fillers[:count]:
+                job(*args)
+            fillers[:count] = []
 
-        rows = [divmod(i, 2) for i in range(10, 2 * STEPS)]
-        rows_in_step = {}
-        for step in range(STEPS):
-            count = ROWS[step]
-            rows_in_step[step] = rows[:count]
-            rows = rows[count:]
-        plane_steps = {FIRST_PLANE + i: [(i // J, i % J, "h%d" % (i % 2))] for i in range(10)}
-        h_piece_steps = dict(H_PIECES)
-        plane_steps.update(LAST_PLANES)
+        def planes(unit):
+            turn_plane(unit, 0)
+            turn_plane(unit, 1)
 
-        first_actuator = 0
+        def weigh(unit):
+            weigh_plane(unit, 0)
+            weigh_plane(unit, 1)
 
-        def side_work(step):
-            for row in rows_in_step.pop(step):
-                widen(*row)
-            if step + 3 in SORTED:
-                sort_words(step + 3, 1)
+        window_pieces = {2: (0, 0), 3: (1, 0), 4: (2, 0), 5: (0, 1), 6: (3, 0), 7: (1, 1)}
 
-        def middle_step(step):
-            if step >= TWO_RUNS_FROM:
-                side_work(step)
-                stage1_run(step, 0, 8)
-                if step > TWO_RUNS_FROM:
-                    weigh_h_plane(*plane_steps[step - 1][0][:2])
-                limit_pair(step)
-                turn_slopes(step + 2, 0)
-                turn_slopes(step + 2, 1)
-                turn_h_plane(*plane_steps[step][0])
-                if step == 13:
-                    weigh_h_plane(*plane_steps[step][0][:2])
-            elif step % 2 == 0:
-                side_work(step)
-                stage1_run(step, 0, CUT_A)
-                turn_slopes(step + 2, 0)
-                turn_h_plane(*plane_steps[step][0])
-                stage1_run(step, CUT_A, 8)
-                stage1_run(step + 1, 0, CUT_B)
-                weigh_h_plane(*plane_steps[step][0][:2])
-                limit_pair(step)
-                turn_slopes(step + 2, 1)
-                turn_h_plane(*plane_steps[step + 1][0])
-            else:
-                side_work(step)
-                stage1_run(step, CUT_B, 8)
-                weigh_h_plane(*plane_steps[step][0][:2])
-                limit_pair(step)
-                turn_slopes(step + 2, 0)
-                turn_slopes(step + 2, 1)
-            if step in h_piece_steps:
-                interleave_h(*h_piece_steps[step])
+        def window(unit):
+            interleave_commands(*window_pieces[unit], gpsimd_move, "early2" if unit == 2 else "held%d" % (unit - 1))
+            if unit in (2, 3):
+                interleave_commands(2, 1, gpsimd_move, "held1" if unit == 2 else None, (unit - 2) * PIECE, PIECE)
+            if unit in (4, 5):
+                interleave_h(0, unit - 4, gpsimd_move)
+            if unit == 6:
+                interleave_h(1, 0, gpsimd_move)
 
-        for step in range(STEPS):
-            middle = 4 <= step < 14
-            if step in (1, 2, 3):
-                load_bytes(step + 4, (0, 1))
-            scale_slopes(step, 0)
-            scale_slopes(step, 1)
-            if step == 4:
-                side_work(step)
-                limit_pair(4)
-                turn_slopes(6, 0)
-                turn_h_plane(0, 0, "acc0")
-                turn_slopes(6, 1)
-                stage1_passes(1, 2, (2, 3), None)
-                weigh_h_plane(0, 0)
-                limit_pair(5)
-            if step == 5:
-                side_work(step)
-                turn_h_plane(0, 1, "acc1")
-                turn_slopes(7, 0)
-                turn_slopes(7, 1)
-                weigh_h_plane(0, 1)
-            if 6 <= step < 14:
-                middle_step(step)
-            if step == STEPS - 1:
-                stage1_step(step)
-            if step == STEPS - 1:
-                for plane in plane_steps[step - 1]:
-                    weigh_h_plane(*plane[:2])
-            if step == 14:
-                stage1_step(step)
-            if not middle:
-                side_work(step)
-                if step in h_piece_steps:
-                    interleave_h(*h_piece_steps[step])
+        interleave_recon(2, (1,), gpsimd_move, "early2")
+        turn_slopes(1, 2)
+        turn_slopes(1, 3)
+        gain_bank = psum.tile([P, P], F32, name="h1")
+        nc.tensor.transpose(gain_bank[:], gain_rows32[:], ident[:])
+        stage1(0, 0, 0, 2)
+        stage1(0, 1, 0, 2)
+        stage1(0, 0, 2, 4)
+        stage1(0, 1, 2, 4)
+        fill(2)
+        interleave_recon(3, (0,), scalar_move, "early1")
+        nc.scalar.copy(out=gain_cols[:], in_=gain_bank[:, 0:MODE_BLOCKS])
+        fill(F0)
+        scale_slopes(1, 0)
+        scale_slopes(1, 1)
+        quantize_recon(2, (0,))
+        quantize_recon(2, (1,))
+        quantize_slopes(1, 0, 2)
+        interleave_recon(3, (1,), gpsimd_move, "early2")
+        scale_slopes(1, 2)
+        scale_slopes(1, 3)
+        stage1(0, 0, 4, 6)
+        stage1(0, 1, 4, 6)
+        stage1(1, 0, 0, 4, "h0")
+        turn_slopes(2, 0)
+        turn_slopes(2, 1)
+        stage1(1, 1, 0, 4, "h1")
+        quantize_recon(3, (0,))
+        quantize_recon(3, (1,))
+        quantize_slopes(1, 2, 2)
+        load_bytes(6, (0, 1))
+        load_commands(0, 1)
 
-            if step == 14:
-                for plane in plane_steps[step]:
-                    turn_h_plane(*plane)
-            if step == STEPS - 1:
-                stage1_passes(LAST, 0, (0, 1), "acc0")
-                stage1_passes(LAST, 2, (0, 1), "turn1")
-            if step in WINDOWS:
-                if step > 0 and step - 1 not in WINDOWS:
-                    quantize_slopes(step - 1)
-                quantize_slopes(step, 0)
-                if step == 2:
-                    interleave_recon(3, 0, vector_move, "shared11")
-                for g, part in RECON_STEPS.get(step, ()):
-                    quantize_recon(g, part)
-                quantize_slopes(step, 1)
-                if step == 0:
-                    interleave_recon(1, 1, gpsimd_move, "shared0")
-                    stage1_passes(0, 0, (0,), "acc0")
-                    turn_slopes(2, 0)
-                    turn_slopes(2, 1)
-                elif step == 1:
-                    interleave_recon(3, 1, gpsimd_move, "shared1")
-                    stage1_passes(0, 2, (0,), "acc1")
-                    stage1_passes(0, 0, (1,), None)
-                    stage1_passes(0, 2, (1,), None)
-                    gain_bank = psum.tile([P, P], F32, name="h0")
-                    nc.tensor.transpose(gain_bank[:], gain_rows32[:], ident[:])
-                    nc.scalar.copy(out=gain_cols[:], in_=gain_bank[:, 0:MODE_BLOCKS])
-                    widen(4, 0)
-                    widen(4, 1)
-                    turn_slopes(3, 0)
-                    turn_slopes(3, 1)
-                elif WINDOWS[step]:
-                    interleave_commands(first_actuator, WINDOWS[step], gpsimd_move, "shared%d" % step)
-                    first_actuator += WINDOWS[step]
-            if step == 2:
-                stage1_passes(1, 0, (0,), "h0")
-                stage1_passes(0, 0, (2,), None)
-                stage1_passes(0, 2, (2,), None)
-                stage1_passes(0, 2, (3,), None)
-                stage1_passes(0, 0, (3,), None)
-                stage1_passes(1, 0, (1,), None)
-                turn_slopes(4, 0)
-                turn_slopes(4, 1)
-                stage1_passes(1, 2, (0, 1), "h1")
-                limit_pair(2)
-                limit_pair(3)
-                nc.scalar.copy(out=weight32[:], in_=weight[:])
-            if step == 3:
-                turn_slopes(5, 0)
-                turn_slopes(5, 1)
-                stage1_passes(1, 0, (2, 3), None)
-            if step == 3:
-                load_commands(2)
-            if step == 6:
-                load_commands(3)
+        window(2)
+        stage1(0, 0, 6, 8)
+        stage1(0, 1, 6, 8)
+        fill(F1)
+        limit(0, 0)
+        limit(0, 1)
+        nc.scalar.copy(out=weight32[:], in_=weight[:])
+        turn_slopes(2, 2)
+        turn_slopes(2, 3)
+        for g in range(PASSES):
+            scale_slopes(2, g)
+        stage1(1, 0, 4, 8)
+        fill(F1B)
+        limit(1, 0)
+        turn_slopes(3, 0)
+        turn_plane(0, 0, "acc0")
+        turn_plane(0, 1, "acc1")
+        weigh(0)
+        stage1(1, 1, 4, 8)
+        limit(1, 1)
+        turn_slopes(3, 1)
+        turn_slopes(3, 2)
+        turn_slopes(3, 3)
+        fill(F2)
+        quantize_slopes(2, 0, 2)
+        quantize_slopes(2, 2, 2)
+        load_bytes(7, (0, 1))
+        load_commands(3, 0)
 
-        banks = {0: ("turn2", "turn3"), 1: ("h0", "h1"), 2: ("turn0", "turn1"), 3: ("turn2", "turn3")}
+        for unit in range(3, LAST):
+            window(unit)
+            stage1(unit - 1, 0, 0, CUT_A)
+            for g in range(PASSES):
+                scale_slopes(unit, g)
+            planes(unit - 2)
+            turn_slopes(unit + 1, 0)
+            weigh(unit - 2)
+            stage1(unit - 1, 0, CUT_A, 8)
+            stage1(unit - 1, 1, 0, CUT_B)
+            limit(unit - 1, 0)
+            fill(FA)
+            turn_slopes(unit + 1, 1)
+            stage1(unit - 1, 1, CUT_B, 8)
+            if unit == LAST - 1:
+                interleave_h(1, 1, scalar_move)
+            limit(unit - 1, 1)
+            fill(FB)
+            turn_slopes(unit + 1, 2)
+            turn_slopes(unit + 1, 3)
+            quantize_slopes(unit, 0, 2)
+            quantize_slopes(unit, 2, 2)
+            if unit == 3:
+                load_commands(3, 1)
+            if unit == 4:
+                load_commands(1, 1)
 
-        def one_pass(g, mb, half):
-            stage2(mb, half, (g,), banks[mb][half] if g == 0 else None)
+        interleave_commands(1, 1, gpsimd_move, "held6", 0, PIECE)
+        scale_slopes(LAST, 0)
+        scale_slopes(LAST, 1)
+        quantize_h(0, 0, 2)
+        quantize_slopes(LAST, 0, 2)
+        interleave_commands(3, 1, gpsimd_move, "held0", 0, PIECE)
+        scale_slopes(LAST, 2)
+        scale_slopes(LAST, 3)
+        quantize_slopes(LAST, 2, 1)
+        quantize_slopes(LAST, 3, 1)
+        interleave_commands(1, 1, scalar_move, None, PIECE, PIECE)
+        stage1(LAST - 1, 0, 0, 8)
+        limit(LAST - 1, 0)
+        stage1(LAST - 1, 1, 0, 8)
+        limit(LAST - 1, 1)
+        planes(LAST - 2)
+        weigh(LAST - 2)
+        stage1(LAST, 0, 0, 4, "turn0")
+        stage1(LAST, 1, 0, 4, "turn1")
+        planes(LAST - 1)
+        interleave_h(2, 0, scalar_move)
+        weigh(LAST - 1)
+        stage1(LAST, 0, 4, 6)
+        stage1(LAST, 1, 4, 6)
+        stage1(LAST, 0, 6, 8)
+        stage1(LAST, 1, 6, 8)
+        limit(LAST, 0)
+        limit(LAST, 1)
 
-        def passes(g, mb):
-            one_pass(g, mb, 0)
-            one_pass(g, mb, 1)
-
-        for plane in plane_steps.get(STEPS - 1, ()):
-            weigh_h_plane(*plane[:2])
-        for g in (2, 3):
-            for mb in (0, 2):
-                stage1_passes(LAST, mb, (g,), None)
-        for mb in range(MODE_BLOCKS):
-            limit(LAST, mb)
-        for part in LATE_H:
-            interleave_h(2, part)
-        interleave_commands(first_actuator, PASSES * A - first_actuator, scalar_move, "shared15")
-        quantize_commands(0, 0)
-        quantize_h_group(0, 0, 1)
-        quantize_h_group(0, 1, 1)
-        quantize_h_group(0, 2, 2)
-        quantize_commands(0, 1)
+        quantize_commands(0, 0, 0, PIECE)
+        quantize_commands(0, 0, PIECE, PIECE)
+        quantize_h(0, 2, 2)
+        quantize_h(1)
         quantize_commands(1, 0)
-        quantize_h_group(1)
-        quantize_commands(1, 1)
-        for half, mb in ((0, 0), (0, 1), (0, 2), (1, 0), (1, 1)):
-            one_pass(0, mb, half)
-        turn_h(3, 0, "acc0")
-        turn_h(3, 1, "acc1")
-        for mb in range(3):
-            one_pass(1, mb, 0)
-        one_pass(0, 2, 1)
-        for mb in range(3):
-            one_pass(1, mb, 1)
-        weigh_h(3, 0)
-        weigh_h(3, 1)
-        turn_h(3, 2, "acc0")
-        turn_h(3, 3, "acc1")
         quantize_commands(2, 0)
-        quantize_h(3, 0)
+        quantize_h(2, 0, 2)
+        quantize_commands(0, 1)
         quantize_commands(3, 0)
-        quantize_h(3, 1)
-        quantize_h_group(2)
+        for first in (0, PIECE):
+            for mb in range(2):
+                stage2(mb, 0, 0, first, PIECE)
+        for mb in (2, 3):
+            stage2(mb, 0, 0)
+        turn_last(0)
+        turn_last(1)
+        weigh_last(0)
+        weigh_last(1)
+        interleave_h(2, 1, scalar_move)
+        interleave_commands(3, 1, scalar_move, None, PIECE, PIECE)
+        interleave_h(3, 0, vector_move)
+        quantize_commands(1, 1)
+        quantize_h(3, 0, 2)
+        interleave_h(3, 1, vector_move)
+        quantize_h(2, 2, 2)
+        quantize_h(3, 2, 2)
         quantize_commands(2, 1)
-        weigh_h(3, 2)
         quantize_commands(3, 1)
-        quantize_h(3, 2)
-        weigh_h(3, 3)
-        quantize_h(3, 3)
+        for mb in range(MODE_BLOCKS):
+            stage2(mb, 0, 1)
         for mb in range(2):
-            stage2(mb, 0, (3,), last=2)
-        for mb in range(2):
-            stage2(mb, 0, (2,), last=2)
-            store(mb, 0, scalar_move)
-        one_pass(2, 2, 0)
+            stage2(mb, 0, 2)
         for mb in range(3):
-            one_pass(2, mb, 1)
-        one_pass(3, 0, 1)
-        store(0, 1, scalar_move)
-        one_pass(3, 1, 1)
-        store(1, 1, vector_move)
-        passes(3, 2)
-        store(2, 0, scalar_move)
-        store(2, 1, vector_move)
-        stage2(3, 0, (0, 1, 2, 3), "turn2")
-        store(3, 0, scalar_move)
-        last_tile(0, "h0", vector_move)
-        last_tile(1, "acc0", scalar_move)
+            stage2(mb, 1, 0)
+        for mb in range(2):
+            stage2(mb, 0, 3)
+            store(mb, 0, scalar_move)
+        for mb in range(2):
+            stage2(mb, 1, 1)
+        for mb in (2, 3):
+            stage2(mb, 0, 2)
+            stage2(mb, 0, 3)
+            store(mb, 0, (vector_move, scalar_move)[mb % 2])
+        stage2(2, 1, 1)
+        for mb in range(3):
+            stage2(mb, 1, 2)
+            stage2(mb, 1, 3)
+            store(mb, 1, (vector_move, scalar_move)[mb % 2])
+        last_tile(0, "h1", scalar_move)
+        last_tile(1, "acc0", vector_move)

@@ -343,10 +343,12 @@ def tile_modal_response_estimate_s7_kernel(
             a0 = half * COLS + first
             nc.sync.dma_start(out=out[mb * P : (mb + 1) * P, a0 : a0 + count], in_=result[:])
 
-        make_identity(nc, ident[:])
+        nc.vector.memset(ident[:], 0.0)
+        nc.vector.memset(gain_rows32[:], 0.0)
+        make_identity(nc, ident[:], nomemset=True)
         scale_view = slopes_scale.rearrange("o (g p j) -> p (o g) j", p=P, j=J)
         nc.sync.dma_start(out=scale[0][:], in_=scale_view[:, 0:2, :])
-        nc.scalar.activation(out=gain_rows[:], in_=ident[:], func=COPY, scale=0.0)
+        nc.scalar.activation(out=gain_rows[:], in_=gain_rows32[:], func=COPY)
         load_first_bytes(0, 0)
         load_first_bytes(0, 1)
         load_recon(0, (0,))

@@ -30,15 +30,30 @@ PIECE = 256
 WIDE_BUFS = 14
 SORTS = (6, 7, 8, 9, 10, 11, 12, 13, 14, 15)
 FOUR_FROM = 3
+SHORT = 384
+SHORT_C = 320
+REST = 64
+OFF = 5
+F3 = 1
+F4 = 1
+SA = 0
+PLANE_LAST = 5
+VO = 0
+SB = 1
+BEFORE = 0
+GA = 3
+GB = 3
+ON_SCALAR = ()
+FOUR = (3, 4, 5, 6)
 CUT_A = 6
 CUT_B = 3
-F0 = 7
+F0 = 8
 F1 = 3
 F1B = 1
 F2 = 4
 FA = 2
 FB = 4
-RESP_BANKS = (("acc0", "acc1", "turn2", "turn3"), ("turn0", "turn1", "h0", "h1"))
+RESP_BANKS = (("acc1", "acc0", "turn2", "turn3"), ("turn1", "h0", "h1"))
 
 
 def tile_modal_response_estimate_s7_kernel(
@@ -81,12 +96,14 @@ def tile_modal_response_estimate_s7_kernel(
         turned = {}
         slopes_grouped = {}
         slope_codes = {}
+        slope_planes = {}
         acc = {}
         h_raw = {}
         h_turned = {}
         h_planes = {}
         h_grouped = {}
         resp = {}
+        H_TAG = {}
 
         def scalar_move(out, in_):
             nc.scalar.copy(out=out, in_=in_)
@@ -118,29 +135,27 @@ def tile_modal_response_estimate_s7_kernel(
             nc.sync.dma_start(out=row_bytes[:], in_=bytes_view[0][:, row, 512 * b : 512 * (b + 1)])
             byte_rows["first", b, row] = row_bytes[:]
 
-        def load_recon(g, parts):
-            z0 = parts[0] * PIECE
-            raw = once.tile([P, J, len(parts) * PIECE], BF16, name="recon_raw%d_%d" % (g, parts[0]))
-            nc.sync.dma_start(out=raw[:], in_=recon_view[g][:, :, z0 : z0 + len(parts) * PIECE])
-            recon_raw[g, parts] = raw[:]
-            for i, part in enumerate(parts):
-                recon_raw[g, (part,)] = raw[:, :, i * PIECE : (i + 1) * PIECE]
+        def load_recon(g, first, last):
+            raw = once.tile([P, J, last - first], BF16, name="recon_raw%d_%d" % (g, first))
+            nc.sync.dma_start(out=raw[:], in_=recon_view[g][:, :, first:last])
+            recon_raw[g, first // PIECE] = (raw, first)
+            recon_raw[g, (last - 1) // PIECE] = (raw, first)
 
         def load_commands(g, half):
             raw = work.tile([P, J, COLS], BF16, name="com_raw", bufs=4)
             nc.sync.dma_start(out=raw[:], in_=commands_view[g][:, :, half * COLS : (half + 1) * COLS])
             com_raw[g, half] = raw
 
-        def interleave_recon(g, parts, move, name):
-            grouped = once.tile([P, J * len(parts) * PIECE], BF16, name=name, align_bytes=64)
-            interleave(move, grouped[:], recon_raw[g, parts])
-            recon_grouped[g, parts] = grouped
+        def interleave_recon(g, first, last, move, name):
+            raw, z0 = recon_raw[g, first // PIECE]
+            grouped = once.tile([P, J * (last - first)], BF16, name=name, align_bytes=64)
+            interleave(move, grouped[:], raw[:, :, first - z0 : last - z0])
+            recon_grouped[g, first] = (grouped, last)
 
-        def quantize_recon(g, parts):
-            cols = slice(g * Z + parts[0] * PIECE, g * Z + (parts[-1] + 1) * PIECE)
-            nc.vector.quantize_mx(
-                out=recon_codes[:, cols].bitcast(E4M3X4), scales=recon_sbytes[:, cols], in_=recon_grouped[g, parts][:]
-            )
+        def quantize_recon(g, first):
+            grouped, last = recon_grouped[g, first]
+            cols = slice(g * Z + first, g * Z + last)
+            nc.vector.quantize_mx(out=recon_codes[:, cols].bitcast(E4M3X4), scales=recon_sbytes[:, cols], in_=grouped[:])
 
         def interleave_commands(g, half, move, name=None, first=0, count=COLS):
             if name:
@@ -195,7 +210,7 @@ def tile_modal_response_estimate_s7_kernel(
 
         def scale_slopes(unit, g):
             half, b = divmod(g, 2)
-            if b == 0 and half == 0:
+            if half == 0 and (unit, half) not in slopes_grouped:
                 slopes_grouped[unit, half] = once.tile([P, 2 * UNIT * J], BF16, name="held%d" % (unit % LAST), align_bytes=64)
             if b == 0 and half == 1:
                 slopes_grouped[unit, half] = work.tile([P, 2 * UNIT * J], BF16, name="second_half", bufs=1, align_bytes=64)
@@ -212,6 +227,23 @@ def tile_modal_response_estimate_s7_kernel(
                     in1=scale[half][:, b, :].rearrange("p (w e) -> p w e", e=2).unsqueeze(1).to_broadcast([P, frames, 2, 2]),
                     op=MULT,
                 )
+
+        def scale_on_scalar(unit, g):
+            half, b = divmod(g, 2)
+            slope_planes[unit] = work.tile([P, J, UNIT], BF16, name="slope_planes", bufs=1)
+            for t in range(J):
+                w, e = divmod(t, 2)
+                nc.scalar.activation(
+                    out=slope_planes[unit][:, t, :],
+                    in_=turned[unit, g][:, w, :].bitcast(BF16)[:, e : 2 * UNIT : 2],
+                    func=COPY,
+                    scale=scale[half][:, b, t : t + 1],
+                )
+
+        def group_on_scalar(unit, g):
+            half, b = divmod(g, 2)
+            slopes_grouped[unit, half] = once.tile([P, 2 * UNIT * J], BF16, name="held%d" % (unit % LAST), align_bytes=64)
+            interleave(scalar_move, slopes_grouped[unit, half][:, b * UNIT * J : (b + 1) * UNIT * J], slope_planes[unit][:])
 
         def quantize_slopes(unit, first, count):
             if first == 0:
@@ -268,24 +300,50 @@ def tile_modal_response_estimate_s7_kernel(
                 out=h_planes[g][:, t, :], in_=h_turned[unit, row][:], func=COPY, scale=weight32[:, g, t : t + 1]
             )
 
-        def turn_last(pair):
-            bank = psum.tile([P, 2, PIECE], F32, name="h%d" % pair)
+        def turn_half_planes(unit, bank_name):
+            bank = psum.tile([P, 2, PIECE], F32, name=bank_name)
             for row in range(2):
                 for i in range(2):
                     nc.tensor.transpose(
-                        bank[:, row, i * P : (i + 1) * P], h_raw[LAST, 2 * pair + i][:, row * P : (row + 1) * P], ident[:]
+                        bank[:, row, i * P : (i + 1) * P], h_raw[unit, 2 + i][:, row * P : (row + 1) * P], ident[:]
                     )
-            h_turned["last", pair] = bank
+            h_turned["half", unit] = bank
 
-        def weigh_last(pair):
+        def weigh_half_planes(unit):
+            g = unit // 2
+            if unit % 2 == 0:
+                h_planes[g] = work.tile([P, J, PIECE], BF16, name="h_planes", bufs=3)
             for row in range(2):
-                g, t = divmod(2 * LAST + row, J)
+                t = 2 * (unit % 2) + row
                 nc.scalar.activation(
-                    out=h_planes[g][:, t, pair * PIECE : (pair + 1) * PIECE],
-                    in_=h_turned["last", pair][:, row, :],
-                    func=COPY,
-                    scale=weight32[:, g, t : t + 1],
+                    out=h_planes[g][:, t, :], in_=h_turned["half", unit][:, row, :], func=COPY, scale=weight32[:, g, t : t + 1]
                 )
+
+        def turn_block(unit, mb):
+            if unit % 2 == 0:
+                h_turned["block", mb] = psum.tile([P, J, P], F32, name="h%d" % mb)
+            for row in range(2):
+                nc.tensor.transpose(
+                    h_turned["block", mb][:, 2 * (unit % 2) + row, :], h_raw[unit, mb][:, row * P : (row + 1) * P], ident[:]
+                )
+
+        def weigh_block(g, mb):
+            if mb == 0:
+                h_grouped[g] = once.tile([P, J * Z], BF16, name="h_grouped%d" % g, align_bytes=64)
+            nc.vector.tensor_tensor(
+                out=h_grouped[g][:, mb * J * P : (mb + 1) * J * P].rearrange("p (z t) -> p z t", t=J),
+                in0=h_turned["block", mb][:].rearrange("p t z -> p z t"),
+                in1=weight[:, g, :].unsqueeze(1).to_broadcast([P, P, J]),
+                op=MULT,
+            )
+
+        def interleave_last_half(g, move):
+            interleave(move, h_grouped[g][:, J * PIECE :], h_planes[g][:])
+
+        def interleave_h_columns(g, first, last, move):
+            if first == 0:
+                h_grouped[g] = once.tile([P, J * Z], BF16, name=H_TAG.get(g, "h_grouped%d" % g), align_bytes=64)
+            interleave(move, h_grouped[g][:, J * first : J * last], h_planes[g][:, :, first:last])
 
         def interleave_h(g, pair, move):
             if pair == 0:
@@ -304,7 +362,7 @@ def tile_modal_response_estimate_s7_kernel(
                 in_=h_grouped[g][:, first * J * P : (first + count) * J * P],
             )
 
-        def stage2(mb, half, g, first=0, count=COLS):
+        def stage2(mb, half, g, first=0, count=COLS, last=PASSES - 1):
             if g == 0 and first == 0:
                 resp[mb, half] = psum.tile([P, COLS], F32, name=RESP_BANKS[half][mb])
             z0 = g * Z + mb * P
@@ -316,26 +374,32 @@ def tile_modal_response_estimate_s7_kernel(
                 rhs=com_codes[:, a0 : a0 + count].bitcast(E4M3X4),
                 rhs_scale=com_sbytes[:, a0 : a0 + count],
                 start=(g == 0 and first == 0),
-                stop=(g == PASSES - 1 and first + count == COLS),
+                stop=(g == last and first + count == COLS),
             )
 
-        def last_tile(part, bank_name, move):
-            bank = psum.tile([P, PIECE], F32, name=bank_name)
+        def quarter(blocks, part, groups, bank_name=None):
+            if bank_name:
+                resp[blocks, part] = psum.tile([P, len(blocks), PIECE], F32, name=bank_name)
+            for g in groups:
+                a0 = g * A + COLS + part * PIECE
+                for i, mb in enumerate(blocks):
+                    z0 = g * Z + mb * P
+                    nc.tensor.matmul_mx(
+                        out=resp[blocks, part][:, i, :],
+                        lhsT=h_codes[:, z0 : z0 + P].bitcast(E4M3X4),
+                        lhsT_scale=h_sbytes[:, z0 : z0 + P],
+                        rhs=com_codes[:, a0 : a0 + PIECE].bitcast(E4M3X4),
+                        rhs_scale=com_sbytes[:, a0 : a0 + PIECE],
+                        start=(g == 0 and i == 0),
+                        stop=(g == PASSES - 1 and i == len(blocks) - 1),
+                    )
+
+        def store_quarter(blocks, part, move):
+            result = work.tile([P, len(blocks), PIECE], F32, name="wide", bufs=WIDE_BUFS)
+            move(result[:], resp[blocks, part][:])
             a0 = COLS + part * PIECE
-            for g in range(PASSES):
-                z0 = g * Z + (MODE_BLOCKS - 1) * P
-                nc.tensor.matmul_mx(
-                    out=bank[:],
-                    lhsT=h_codes[:, z0 : z0 + P].bitcast(E4M3X4),
-                    lhsT_scale=h_sbytes[:, z0 : z0 + P],
-                    rhs=com_codes[:, g * A + a0 : g * A + a0 + PIECE].bitcast(E4M3X4),
-                    rhs_scale=com_sbytes[:, g * A + a0 : g * A + a0 + PIECE],
-                    start=(g == 0),
-                    stop=(g == PASSES - 1),
-                )
-            result = work.tile([P, PIECE], F32, name="wide", bufs=WIDE_BUFS)
-            move(result[:], bank[:])
-            nc.sync.dma_start(out=out[(MODE_BLOCKS - 1) * P :, a0 : a0 + PIECE], in_=result[:])
+            rows = out.rearrange("(m p) a -> p m a", p=P)
+            nc.sync.dma_start(out=rows[:, blocks[0] : blocks[-1] + 1, a0 : a0 + PIECE], in_=result[:])
 
         def store(mb, half, move, first=0, count=COLS):
             result = work.tile([P, count], F32, name="wide", bufs=WIDE_BUFS)
@@ -351,19 +415,19 @@ def tile_modal_response_estimate_s7_kernel(
         nc.scalar.activation(out=gain_rows[:], in_=gain_rows32[:], func=COPY)
         load_first_bytes(0, 0)
         load_first_bytes(0, 1)
-        load_recon(0, (0,))
+        load_recon(0, 0, PIECE)
         load_first_bytes(1, 0)
         load_first_bytes(1, 1)
-        load_recon(0, (1,))
+        load_recon(0, PIECE, Z)
         load_bytes(0, (1,))
         nc.sync.dma_start(out=scale[1][:], in_=scale_view[:, 2:4, :])
-        load_recon(1, (0, 1))
+        load_recon(1, 0, Z)
         load_bytes(1, (0,))
         load_bytes(1, (1,))
         nc.sync.dma_start(out=gain_rows[0:MODE_BLOCKS, :], in_=gain.rearrange("(c p) -> c p", p=P))
-        load_recon(2, (0, 1))
-        load_recon(3, (0, 1))
+        load_recon(2, 0, Z)
         load_bytes(2, (0, 1))
+        load_recon(3, 0, Z)
         load_bytes(3, (0, 1))
         load_commands(0, 0)
         load_commands(2, 1)
@@ -376,22 +440,22 @@ def tile_modal_response_estimate_s7_kernel(
         for b in range(2):
             for row in range(2):
                 first_turn(b, row)
-        interleave_recon(0, (0,), vector_move, "early0")
-        interleave_recon(0, (1,), gpsimd_move, "early1")
+        interleave_recon(0, 0, PIECE, vector_move, "early0")
+        interleave_recon(0, PIECE, Z, gpsimd_move, "early1")
         scale_slopes(0, 0)
         scale_slopes(0, 1)
         widen(0, 1, 0)
         widen(0, 1, 1)
         turn_slopes(0, 2)
         turn_slopes(0, 3)
-        interleave_recon(1, (1,), scalar_move, "early2")
+        interleave_recon(1, SHORT, Z, scalar_move, "early2")
         widen(1, 0, 0)
         widen(1, 0, 1)
-        quantize_recon(0, (0,))
+        quantize_recon(0, 0)
         quantize_slopes(0, 0, 1)
-        quantize_recon(0, (1,))
+        quantize_recon(0, PIECE)
         quantize_slopes(0, 1, 1)
-        interleave_recon(1, (0,), gpsimd_move, "early1")
+        interleave_recon(1, 0, SHORT, gpsimd_move, "early1")
         turn_slopes(1, 0)
         turn_slopes(1, 1)
         scale_slopes(0, 2)
@@ -399,9 +463,9 @@ def tile_modal_response_estimate_s7_kernel(
         widen(1, 1, 0)
         widen(1, 1, 1)
         nc.scalar.copy(out=gain_rows32[:], in_=gain_rows[:])
-        interleave_recon(2, (0,), scalar_move, "early0")
-        quantize_recon(1, (0,))
-        quantize_recon(1, (1,))
+        interleave_recon(2, SHORT, Z, scalar_move, "early0")
+        quantize_recon(1, 0)
+        quantize_recon(1, SHORT)
         quantize_slopes(0, 2, 2)
 
         fillers = []
@@ -427,16 +491,24 @@ def tile_modal_response_estimate_s7_kernel(
 
         window_pieces = {2: (0, 0), 3: (1, 0), 4: (2, 0), 5: (0, 1), 6: (3, 0), 7: (1, 1)}
 
+        def extra_piece(unit, move):
+            if unit in (2, 3):
+                interleave_commands(2, 1, move, "held1" if unit == 2 else None, (unit - 2) * PIECE, PIECE)
+            if unit in (4, 5):
+                interleave_h(0, unit - 4, move)
+            if unit == 6:
+                interleave_commands(3, 1, move, "early3", 0, PIECE)
+
         def window(unit):
             interleave_commands(*window_pieces[unit], gpsimd_move, "early2" if unit == 2 else "held%d" % (unit - 1))
-            if unit in (2, 3):
-                interleave_commands(2, 1, gpsimd_move, "held1" if unit == 2 else None, (unit - 2) * PIECE, PIECE)
-            if unit in (4, 5):
-                interleave_h(0, unit - 4, gpsimd_move)
-            if unit == 6:
-                interleave_h(1, 0, gpsimd_move)
+            if unit != OFF:
+                extra_piece(unit, gpsimd_move)
+            elif unit == 3:
+                interleave_commands(2, 1, gpsimd_move, None, PIECE, REST)
+            else:
+                interleave_h_columns(0, (unit - 4) * PIECE, (unit - 4) * PIECE + REST, gpsimd_move)
 
-        interleave_recon(2, (1,), gpsimd_move, "early2")
+        interleave_recon(2, 0, SHORT, gpsimd_move, "early2")
         turn_slopes(1, 2)
         turn_slopes(1, 3)
         gain_bank = psum.tile([P, P], F32, name="h1")
@@ -446,15 +518,16 @@ def tile_modal_response_estimate_s7_kernel(
         stage1(0, 0, 2, 4)
         stage1(0, 1, 2, 4)
         fill(2)
-        interleave_recon(3, (0,), scalar_move, "early1")
+        interleave_recon(3, SHORT, Z, scalar_move, "early1")
+        fill(2)
         nc.scalar.copy(out=gain_cols[:], in_=gain_bank[:, 0:MODE_BLOCKS])
         fill(F0)
         scale_slopes(1, 0)
         scale_slopes(1, 1)
-        quantize_recon(2, (0,))
-        quantize_recon(2, (1,))
+        quantize_recon(2, SHORT)
+        quantize_recon(2, 0)
         quantize_slopes(1, 0, 2)
-        interleave_recon(3, (1,), gpsimd_move, "early2")
+        interleave_recon(3, 0, SHORT, gpsimd_move, "early2")
         scale_slopes(1, 2)
         scale_slopes(1, 3)
         stage1(0, 0, 4, 6)
@@ -463,8 +536,8 @@ def tile_modal_response_estimate_s7_kernel(
         turn_slopes(2, 0)
         turn_slopes(2, 1)
         stage1(1, 1, 0, 4, "h1")
-        quantize_recon(3, (0,))
-        quantize_recon(3, (1,))
+        quantize_recon(3, SHORT)
+        quantize_recon(3, 0)
         quantize_slopes(1, 2, 2)
         load_bytes(6, (0, 1))
         load_commands(0, 1)
@@ -492,6 +565,10 @@ def tile_modal_response_estimate_s7_kernel(
         turn_slopes(3, 1)
         turn_slopes(3, 2)
         turn_slopes(3, 3)
+        if OFF == 3:
+            scale_on_scalar(3, 0)
+            fill(F3)
+            group_on_scalar(3, 0)
         fill(F2)
         quantize_slopes(2, 0, 2)
         quantize_slopes(2, 2, 2)
@@ -500,24 +577,58 @@ def tile_modal_response_estimate_s7_kernel(
 
         for unit in range(3, LAST):
             window(unit)
-            stage1(unit - 1, 0, 0, CUT_A)
-            for g in range(PASSES):
+            for g in range(unit == OFF, PASSES):
                 scale_slopes(unit, g)
-            planes(unit - 2)
-            turn_slopes(unit + 1, 0)
-            weigh(unit - 2)
-            stage1(unit - 1, 0, CUT_A, 8)
-            stage1(unit - 1, 1, 0, CUT_B)
-            limit(unit - 1, 0)
-            fill(FA)
-            turn_slopes(unit + 1, 1)
-            stage1(unit - 1, 1, CUT_B, 8)
-            if unit == LAST - 1:
-                interleave_h(1, 1, scalar_move)
-            limit(unit - 1, 1)
-            fill(FB)
-            turn_slopes(unit + 1, 2)
-            turn_slopes(unit + 1, 3)
+            if unit in FOUR:
+                stage1(unit - 1, 0, 0, 8)
+                if unit < PLANE_LAST:
+                    turn_plane(unit - 2, 0)
+                turn_slopes(unit + 1, 0)
+                turn_slopes(unit + 1, 1)
+                if unit >= PLANE_LAST:
+                    turn_plane(unit - 2, 0)
+                limit(unit - 1, 0)
+                weigh_plane(unit - 2, 0)
+                if unit + 1 == OFF:
+                    scale_on_scalar(OFF, 0)
+                    fill(F4)
+                else:
+                    fill(GA)
+                stage1(unit - 1, 1, 0, 8)
+                turn_plane(unit - 2, 1)
+                turn_slopes(unit + 1, 2)
+                turn_slopes(unit + 1, 3)
+                limit(unit - 1, 1)
+                weigh_plane(unit - 2, 1)
+                if unit + 1 == OFF:
+                    group_on_scalar(OFF, 0)
+                    fill(F3)
+                else:
+                    fill(GB)
+            else:
+                stage1(unit - 1, 0, 0, CUT_A)
+                planes(unit - 2)
+                turn_slopes(unit + 1, 0)
+                weigh(unit - 2)
+                stage1(unit - 1, 0, CUT_A, 8)
+                stage1(unit - 1, 1, 0, CUT_B)
+                limit(unit - 1, 0)
+                if unit + 1 == OFF:
+                    scale_on_scalar(OFF, 0)
+                else:
+                    fill(FA)
+                turn_slopes(unit + 1, 1)
+                stage1(unit - 1, 1, CUT_B, 8)
+                if unit == LAST - 1:
+                    interleave_h(1, 1, scalar_move)
+                limit(unit - 1, 1)
+                if unit + 1 == OFF:
+                    group_on_scalar(OFF, 0)
+                    fill(F3)
+                else:
+                    fill(FB)
+                turn_slopes(unit + 1, 2)
+                turn_slopes(unit + 1, 3)
             quantize_slopes(unit, 0, 2)
             quantize_slopes(unit, 2, 2)
             if unit == 3:
@@ -525,17 +636,18 @@ def tile_modal_response_estimate_s7_kernel(
             if unit == 4:
                 load_commands(1, 1)
 
-        interleave_commands(1, 1, gpsimd_move, "held6", 0, PIECE)
+        interleave_h_columns(0, PIECE + REST, Z, scalar_move)
+        H_TAG[1] = "held6"
+        interleave_h_columns(1, 0, SHORT_C, gpsimd_move)
         scale_slopes(LAST, 0)
         scale_slopes(LAST, 1)
         quantize_h(0, 0, 2)
         quantize_slopes(LAST, 0, 2)
-        interleave_commands(3, 1, gpsimd_move, "held0", 0, PIECE)
+        interleave_commands(1, 1, gpsimd_move, "held0", 0, SHORT_C)
         scale_slopes(LAST, 2)
         scale_slopes(LAST, 3)
         quantize_slopes(LAST, 2, 1)
         quantize_slopes(LAST, 3, 1)
-        interleave_commands(1, 1, scalar_move, None, PIECE, PIECE)
         stage1(LAST - 1, 0, 0, 8)
         limit(LAST - 1, 0)
         stage1(LAST - 1, 1, 0, 8)
@@ -544,63 +656,79 @@ def tile_modal_response_estimate_s7_kernel(
         weigh(LAST - 2)
         stage1(LAST, 0, 0, 4, "turn0")
         stage1(LAST, 1, 0, 4, "turn1")
-        planes(LAST - 1)
-        interleave_h(2, 0, scalar_move)
-        weigh(LAST - 1)
-        stage1(LAST, 0, 4, 6)
-        stage1(LAST, 1, 4, 6)
-        stage1(LAST, 0, 6, 8)
-        stage1(LAST, 1, 6, 8)
+        turn_half_planes(LAST - 1, "acc0")
+        turn_block(LAST - 1, 0)
+        turn_block(LAST - 1, 1)
+        interleave_h_columns(1, SHORT_C, Z, scalar_move)
+        weigh_half_planes(LAST - 1)
+        if SB == 0:
+            interleave_h(2, 0, scalar_move)
+        stage1(LAST, 0, 4, 8)
+        stage1(LAST, 1, 4, 8)
         limit(LAST, 0)
         limit(LAST, 1)
+        if SB == 1:
+            interleave_h(2, 0, scalar_move)
 
         quantize_commands(0, 0, 0, PIECE)
         quantize_commands(0, 0, PIECE, PIECE)
         quantize_h(0, 2, 2)
         quantize_h(1)
         quantize_commands(1, 0)
-        quantize_commands(2, 0)
-        quantize_h(2, 0, 2)
+        stage2(0, 0, 0, 0, PIECE)
+        stage2(0, 0, 0, PIECE, PIECE)
+        stage2(2, 0, 0)
+        stage2(3, 0, 0)
+        stage2(1, 0, 0)
+        for mb in range(BEFORE):
+            stage2(mb, 0, 1)
+        turn_block(LAST, 0)
+        turn_block(LAST, 1)
+        turn_half_planes(LAST, "turn0")
+        weigh_half_planes(LAST)
+        interleave_h(2, 1, scalar_move)
+        interleave_commands(1, 1, scalar_move, None, SHORT_C, COLS - SHORT_C)
+        for mb in range(BEFORE, MODE_BLOCKS):
+            stage2(mb, 0, 1)
         quantize_commands(0, 1)
         quantize_commands(3, 0)
-        for first in (0, PIECE):
-            for mb in range(2):
-                stage2(mb, 0, 0, first, PIECE)
-        for mb in (2, 3):
-            stage2(mb, 0, 0)
-        turn_last(0)
-        turn_last(1)
-        weigh_last(0)
-        weigh_last(1)
-        interleave_h(2, 1, scalar_move)
-        interleave_commands(3, 1, scalar_move, None, PIECE, PIECE)
-        interleave_h(3, 0, vector_move)
-        quantize_commands(1, 1)
-        quantize_h(3, 0, 2)
-        interleave_h(3, 1, vector_move)
+        weigh_block(3, 0)
+        weigh_block(3, 1)
+        if VO == 0:
+            quantize_commands(2, 0)
+            quantize_h(3, 0, 2)
+            quantize_h(2, 0, 2)
+        else:
+            quantize_h(2, 0, 2)
+            quantize_h(3, 0, 2)
+            quantize_commands(2, 0)
+        interleave_last_half(3, vector_move)
         quantize_h(2, 2, 2)
         quantize_h(3, 2, 2)
-        quantize_commands(2, 1)
-        quantize_commands(3, 1)
-        for mb in range(MODE_BLOCKS):
-            stage2(mb, 0, 1)
+        for g in (1, 2, 3):
+            quantize_commands(g, 1, 0, PIECE)
+        interleave_commands(3, 1, vector_move, None, PIECE, PIECE)
+        for g in (1, 2, 3):
+            quantize_commands(g, 1, PIECE, PIECE)
+        quarter((0, 1), 0, (0,), "turn1")
+        quarter((2, 3), 0, (0,), "h0")
+        quarter((0, 1), 1, (0,), "h1")
         for mb in range(2):
-            stage2(mb, 0, 2)
-        for mb in range(3):
-            stage2(mb, 1, 0)
+            stage2(mb, 0, 3, last=2)
         for mb in range(2):
-            stage2(mb, 0, 3)
+            stage2(mb, 0, 2, last=2)
             store(mb, 0, scalar_move)
-        for mb in range(2):
-            stage2(mb, 1, 1)
         for mb in (2, 3):
             stage2(mb, 0, 2)
             stage2(mb, 0, 3)
-            store(mb, 0, (vector_move, scalar_move)[mb % 2])
-        stage2(2, 1, 1)
-        for mb in range(3):
-            stage2(mb, 1, 2)
-            stage2(mb, 1, 3)
-            store(mb, 1, (vector_move, scalar_move)[mb % 2])
-        last_tile(0, "h1", scalar_move)
-        last_tile(1, "acc0", vector_move)
+            store(mb, 0, scalar_move)
+        quarter((0, 1), 0, (1, 2, 3))
+        store_quarter((0, 1), 0, scalar_move)
+        quarter((2, 3), 0, (1, 2, 3))
+        store_quarter((2, 3), 0, vector_move)
+        quarter((0, 1), 1, (1, 2, 3))
+        store_quarter((0, 1), 1, scalar_move)
+        quarter((2,), 1, (0, 1, 2, 3), "turn0")
+        store_quarter((2,), 1, vector_move)
+        quarter((3,), 1, (0, 1, 2, 3), "acc1")
+        store_quarter((3,), 1, scalar_move)

@@ -28,31 +28,37 @@ MODE_BLOCKS = Z // P
 COLS = 512
 PIECE = 256
 WIDE_BUFS = 14
-SORTS = (6, 7, 8, 9, 10, 11, 12, 13, 14, 15)
+SORTS = (7, 9, 11, 12, 13, 14, 15)
 FOUR_FROM = 3
 SHORT = 384
 SHORT_C = 320
 REST = 64
+HV = 128
+HG = 96
+TAIL = 0
+LO = 0
+EXI = (0, 0, 0, 1)
 OFF = 5
-F3 = 1
+F3 = 2
 F4 = 1
 SA = 0
 PLANE_LAST = 5
-VO = 0
+PLANE_MID = 3
+VO = 1
 SB = 1
 BEFORE = 0
 GA = 3
 GB = 3
 ON_SCALAR = ()
-FOUR = (3, 4, 5, 6)
+FOUR = (5, 6)
 CUT_A = 6
 CUT_B = 3
-F0 = 8
-F1 = 3
+F0 = 11
+F1 = 1
 F1B = 1
-F2 = 4
+F2 = 5
 FA = 2
-FB = 4
+FB = 3
 RESP_BANKS = (("acc1", "acc0", "turn2", "turn3"), ("turn1", "h0", "h1"))
 
 
@@ -152,6 +158,12 @@ def tile_modal_response_estimate_s7_kernel(
             interleave(move, grouped[:], raw[:, :, first - z0 : last - z0])
             recon_grouped[g, first] = (grouped, last)
 
+        def share_recon(g, part, first, last, move, name=None):
+            raw, z0 = recon_raw[g, part]
+            if name:
+                recon_grouped[g, z0] = (once.tile([P, J * PIECE], BF16, name=name, align_bytes=64), z0 + PIECE)
+            interleave(move, recon_grouped[g, z0][0][:, J * first : J * last], raw[:, :, first:last])
+
         def quantize_recon(g, first):
             grouped, last = recon_grouped[g, first]
             cols = slice(g * Z + first, g * Z + last)
@@ -195,9 +207,9 @@ def tile_modal_response_estimate_s7_kernel(
             )
             sorted_words[unit, half] = ordered
 
-        def turn_slopes(unit, g):
+        def turn_slopes(unit, g, slot=None):
             half, b = divmod(g, 2)
-            bank = psum.tile([P, 2, UNIT], F32, name="turn%d" % g)
+            bank = psum.tile([P, 2, UNIT], F32, name="turn%d" % (g if slot is None else slot))
             turned[unit, g] = bank
             for row in range(2):
                 words = widened[unit, half, row][:].bitcast(F32)
@@ -211,9 +223,9 @@ def tile_modal_response_estimate_s7_kernel(
         def scale_slopes(unit, g):
             half, b = divmod(g, 2)
             if half == 0 and (unit, half) not in slopes_grouped:
-                slopes_grouped[unit, half] = once.tile([P, 2 * UNIT * J], BF16, name="held%d" % (unit % LAST), align_bytes=64)
+                slopes_grouped[unit, half] = once.tile([P, 2 * UNIT * J], BF16, name="held%d" % unit, align_bytes=64)
             if b == 0 and half == 1:
-                slopes_grouped[unit, half] = work.tile([P, 2 * UNIT * J], BF16, name="second_half", bufs=1, align_bytes=64)
+                slopes_grouped[unit, half] = work.tile([P, 2 * UNIT * J], BF16, name="second_half", bufs=2, align_bytes=64)
             grouped = slopes_grouped[unit, half][:, b * UNIT * J : (b + 1) * UNIT * J]
             if unit == 0 and half == 0:
                 parts = [(turned["first", b, row], grouped[:, row * P * J : (row + 1) * P * J], P) for row in range(2)]
@@ -242,7 +254,7 @@ def tile_modal_response_estimate_s7_kernel(
 
         def group_on_scalar(unit, g):
             half, b = divmod(g, 2)
-            slopes_grouped[unit, half] = once.tile([P, 2 * UNIT * J], BF16, name="held%d" % (unit % LAST), align_bytes=64)
+            slopes_grouped[unit, half] = once.tile([P, 2 * UNIT * J], BF16, name="held%d" % unit, align_bytes=64)
             interleave(scalar_move, slopes_grouped[unit, half][:, b * UNIT * J : (b + 1) * UNIT * J], slope_planes[unit][:])
 
         def quantize_slopes(unit, first, count):
@@ -415,24 +427,29 @@ def tile_modal_response_estimate_s7_kernel(
         nc.scalar.activation(out=gain_rows[:], in_=gain_rows32[:], func=COPY)
         load_first_bytes(0, 0)
         load_first_bytes(0, 1)
-        load_recon(0, 0, PIECE)
+        if LO == 0:
+            load_recon(0, 0, PIECE)
         load_first_bytes(1, 0)
+        if LO == 1:
+            load_recon(0, 0, PIECE)
         load_first_bytes(1, 1)
-        load_recon(0, PIECE, Z)
-        load_bytes(0, (1,))
-        nc.sync.dma_start(out=scale[1][:], in_=scale_view[:, 2:4, :])
-        load_recon(1, 0, Z)
+        if LO == 2:
+            load_recon(0, 0, PIECE)
         load_bytes(1, (0,))
-        load_bytes(1, (1,))
+        load_recon(0, PIECE, Z)
+        load_recon(1, 0, Z)
+        nc.sync.dma_start(out=scale[1][:], in_=scale_view[:, 2:4, :])
+        load_bytes(0, (1,))
         nc.sync.dma_start(out=gain_rows[0:MODE_BLOCKS, :], in_=gain.rearrange("(c p) -> c p", p=P))
+        load_bytes(1, (1,))
         load_recon(2, 0, Z)
         load_bytes(2, (0, 1))
         load_recon(3, 0, Z)
         load_bytes(3, (0, 1))
         load_commands(0, 0)
+        load_bytes(4, (0, 1))
         load_commands(2, 1)
         nc.sync.dma_start(out=weight[:], in_=frame_weight.rearrange("(g p t) -> p g t", p=P, t=J))
-        load_bytes(4, (0, 1))
         load_commands(1, 0)
         load_bytes(5, (0, 1))
         load_commands(2, 0)
@@ -440,33 +457,37 @@ def tile_modal_response_estimate_s7_kernel(
         for b in range(2):
             for row in range(2):
                 first_turn(b, row)
-        interleave_recon(0, 0, PIECE, vector_move, "early0")
-        interleave_recon(0, PIECE, Z, gpsimd_move, "early1")
+        share_recon(0, 0, 0, HV, vector_move, "early0")
+        share_recon(0, 0, HV, PIECE, scalar_move)
+        share_recon(0, 1, 0, HG, gpsimd_move, "early1")
         scale_slopes(0, 0)
         scale_slopes(0, 1)
-        widen(0, 1, 0)
-        widen(0, 1, 1)
-        turn_slopes(0, 2)
-        turn_slopes(0, 3)
-        interleave_recon(1, SHORT, Z, scalar_move, "early2")
         widen(1, 0, 0)
         widen(1, 0, 1)
-        quantize_recon(0, 0)
+        turn_slopes(1, 0, 2)
+        turn_slopes(1, 1, 3)
+        share_recon(0, 1, HG, PIECE, scalar_move)
+        interleave_recon(1, SHORT, Z, scalar_move, "early2")
+        widen(0, 1, 0)
+        widen(0, 1, 1)
+        nc.scalar.copy(out=gain_rows32[:], in_=gain_rows[:])
         quantize_slopes(0, 0, 1)
-        quantize_recon(0, PIECE)
+        quantize_recon(0, 0)
         quantize_slopes(0, 1, 1)
-        interleave_recon(1, 0, SHORT, gpsimd_move, "early1")
-        turn_slopes(1, 0)
-        turn_slopes(1, 1)
-        scale_slopes(0, 2)
-        scale_slopes(0, 3)
+        quantize_recon(0, PIECE)
+        interleave_recon(1, 0, SHORT, gpsimd_move, "held0")
+        turn_slopes(0, 2, 0)
+        turn_slopes(0, 3, 1)
+        gain_bank = psum.tile([P, P], F32, name="h1")
+        nc.tensor.transpose(gain_bank[:], gain_rows32[:], ident[:])
+        scale_slopes(1, 0)
+        scale_slopes(1, 1)
         widen(1, 1, 0)
         widen(1, 1, 1)
-        nc.scalar.copy(out=gain_rows32[:], in_=gain_rows[:])
         interleave_recon(2, SHORT, Z, scalar_move, "early0")
-        quantize_recon(1, 0)
         quantize_recon(1, SHORT)
-        quantize_slopes(0, 2, 2)
+        quantize_recon(1, 0)
+        quantize_slopes(1, 0, 2)
 
         fillers = []
         for unit in range(2, UNITS):
@@ -500,7 +521,7 @@ def tile_modal_response_estimate_s7_kernel(
                 interleave_commands(3, 1, move, "early3", 0, PIECE)
 
         def window(unit):
-            interleave_commands(*window_pieces[unit], gpsimd_move, "early2" if unit == 2 else "held%d" % (unit - 1))
+            interleave_commands(*window_pieces[unit], gpsimd_move, "held0" if unit == 2 else "held%d" % (unit - 1))
             if unit != OFF:
                 extra_piece(unit, gpsimd_move)
             elif unit == 3:
@@ -508,34 +529,32 @@ def tile_modal_response_estimate_s7_kernel(
             else:
                 interleave_h_columns(0, (unit - 4) * PIECE, (unit - 4) * PIECE + REST, gpsimd_move)
 
-        interleave_recon(2, 0, SHORT, gpsimd_move, "early2")
-        turn_slopes(1, 2)
-        turn_slopes(1, 3)
-        gain_bank = psum.tile([P, P], F32, name="h1")
-        nc.tensor.transpose(gain_bank[:], gain_rows32[:], ident[:])
+        interleave_recon(2, 0, SHORT, gpsimd_move, "held0")
         stage1(0, 0, 0, 2)
         stage1(0, 1, 0, 2)
         stage1(0, 0, 2, 4)
         stage1(0, 1, 2, 4)
         fill(2)
-        interleave_recon(3, SHORT, Z, scalar_move, "early1")
-        fill(2)
         nc.scalar.copy(out=gain_cols[:], in_=gain_bank[:, 0:MODE_BLOCKS])
+        interleave_recon(3, SHORT, Z, scalar_move, "early1")
         fill(F0)
-        scale_slopes(1, 0)
-        scale_slopes(1, 1)
+        turn_slopes(1, 2)
+        stage1(1, 0, 0, 4, "h0")
+        turn_slopes(1, 3)
+        scale_slopes(0, 2)
+        scale_slopes(0, 3)
         quantize_recon(2, SHORT)
         quantize_recon(2, 0)
-        quantize_slopes(1, 0, 2)
-        interleave_recon(3, 0, SHORT, gpsimd_move, "early2")
+        quantize_slopes(0, 2, 2)
+        interleave_recon(3, 0, SHORT, gpsimd_move, "held0")
         scale_slopes(1, 2)
         scale_slopes(1, 3)
+        turn_slopes(2, 0)
+        stage1(1, 1, 0, 4, "h1")
+        turn_slopes(2, 1)
+        turn_slopes(2, 2)
         stage1(0, 0, 4, 6)
         stage1(0, 1, 4, 6)
-        stage1(1, 0, 0, 4, "h0")
-        turn_slopes(2, 0)
-        turn_slopes(2, 1)
-        stage1(1, 1, 0, 4, "h1")
         quantize_recon(3, SHORT)
         quantize_recon(3, 0)
         quantize_slopes(1, 2, 2)
@@ -545,30 +564,24 @@ def tile_modal_response_estimate_s7_kernel(
         window(2)
         stage1(0, 0, 6, 8)
         stage1(0, 1, 6, 8)
-        fill(F1)
         limit(0, 0)
         limit(0, 1)
         nc.scalar.copy(out=weight32[:], in_=weight[:])
-        turn_slopes(2, 2)
         turn_slopes(2, 3)
         for g in range(PASSES):
             scale_slopes(2, g)
-        stage1(1, 0, 4, 8)
-        fill(F1B)
-        limit(1, 0)
         turn_slopes(3, 0)
+        stage1(1, 0, 4, 8)
+        fill(F1)
+        limit(1, 0)
         turn_plane(0, 0, "acc0")
         turn_plane(0, 1, "acc1")
+        turn_slopes(3, 1)
         weigh(0)
         stage1(1, 1, 4, 8)
         limit(1, 1)
-        turn_slopes(3, 1)
         turn_slopes(3, 2)
         turn_slopes(3, 3)
-        if OFF == 3:
-            scale_on_scalar(3, 0)
-            fill(F3)
-            group_on_scalar(3, 0)
         fill(F2)
         quantize_slopes(2, 0, 2)
         quantize_slopes(2, 2, 2)
@@ -581,9 +594,11 @@ def tile_modal_response_estimate_s7_kernel(
                 scale_slopes(unit, g)
             if unit in FOUR:
                 stage1(unit - 1, 0, 0, 8)
-                if unit < PLANE_LAST:
+                if unit < PLANE_MID:
                     turn_plane(unit - 2, 0)
                 turn_slopes(unit + 1, 0)
+                if PLANE_MID <= unit < PLANE_LAST:
+                    turn_plane(unit - 2, 0)
                 turn_slopes(unit + 1, 1)
                 if unit >= PLANE_LAST:
                     turn_plane(unit - 2, 0)
@@ -643,7 +658,7 @@ def tile_modal_response_estimate_s7_kernel(
         scale_slopes(LAST, 1)
         quantize_h(0, 0, 2)
         quantize_slopes(LAST, 0, 2)
-        interleave_commands(1, 1, gpsimd_move, "held0", 0, SHORT_C)
+        interleave_commands(1, 1, gpsimd_move, "held7", 0, SHORT_C)
         scale_slopes(LAST, 2)
         scale_slopes(LAST, 3)
         quantize_slopes(LAST, 2, 1)
@@ -670,6 +685,7 @@ def tile_modal_response_estimate_s7_kernel(
         if SB == 1:
             interleave_h(2, 0, scalar_move)
 
+        EX = [(scalar_move, vector_move)[i] for i in EXI]
         quantize_commands(0, 0, 0, PIECE)
         quantize_commands(0, 0, PIECE, PIECE)
         quantize_h(0, 2, 2)
@@ -687,26 +703,28 @@ def tile_modal_response_estimate_s7_kernel(
         turn_half_planes(LAST, "turn0")
         weigh_half_planes(LAST)
         interleave_h(2, 1, scalar_move)
-        interleave_commands(1, 1, scalar_move, None, SHORT_C, COLS - SHORT_C)
         for mb in range(BEFORE, MODE_BLOCKS):
             stage2(mb, 0, 1)
         quantize_commands(0, 1)
-        quantize_commands(3, 0)
+        quantize_commands(3, 0, 0, PIECE)
         weigh_block(3, 0)
+        interleave_last_half(3, scalar_move)
         weigh_block(3, 1)
-        if VO == 0:
-            quantize_commands(2, 0)
-            quantize_h(3, 0, 2)
-            quantize_h(2, 0, 2)
-        else:
-            quantize_h(2, 0, 2)
-            quantize_h(3, 0, 2)
-            quantize_commands(2, 0)
-        interleave_last_half(3, vector_move)
+        quantize_commands(3, 0, PIECE, PIECE)
+        quantize_h(3, 0, 2)
+        quantize_h(2, 0, 2)
+        quantize_commands(2, 0)
         quantize_h(2, 2, 2)
-        quantize_h(3, 2, 2)
-        for g in (1, 2, 3):
-            quantize_commands(g, 1, 0, PIECE)
+        if VO == 0:
+            for g in (1, 2, 3):
+                quantize_commands(g, 1, 0, PIECE)
+            quantize_h(3, 2, 2)
+        else:
+            quantize_commands(1, 1, 0, PIECE)
+            quantize_commands(2, 1, 0, PIECE)
+            quantize_h(3, 2, 2)
+            quantize_commands(3, 1, 0, PIECE)
+        interleave_commands(1, 1, vector_move, None, SHORT_C, COLS - SHORT_C)
         interleave_commands(3, 1, vector_move, None, PIECE, PIECE)
         for g in (1, 2, 3):
             quantize_commands(g, 1, PIECE, PIECE)
@@ -720,15 +738,40 @@ def tile_modal_response_estimate_s7_kernel(
             store(mb, 0, scalar_move)
         for mb in (2, 3):
             stage2(mb, 0, 2)
+        if VO == 0:
+            quarter((0, 1), 0, (1, 2, 3))
+            store_quarter((0, 1), 0, EX[0])
+        for mb in (2, 3):
             stage2(mb, 0, 3)
-            store(mb, 0, scalar_move)
-        quarter((0, 1), 0, (1, 2, 3))
-        store_quarter((0, 1), 0, scalar_move)
+            store(mb, 0, EX[mb - 1])
+        if VO == 1:
+            quarter((0, 1), 0, (1, 2, 3))
+            store_quarter((0, 1), 0, EX[0])
         quarter((2, 3), 0, (1, 2, 3))
-        store_quarter((2, 3), 0, vector_move)
+        store_quarter((2, 3), 0, EX[3])
         quarter((0, 1), 1, (1, 2, 3))
         store_quarter((0, 1), 1, scalar_move)
         quarter((2,), 1, (0, 1, 2, 3), "turn0")
         store_quarter((2,), 1, vector_move)
-        quarter((3,), 1, (0, 1, 2, 3), "acc1")
-        store_quarter((3,), 1, scalar_move)
+        if TAIL == 0:
+            quarter((3,), 1, (0, 1, 2, 3), "acc1")
+            store_quarter((3,), 1, scalar_move)
+        else:
+            for i, (bank_name, move) in enumerate((("acc1", scalar_move), ("acc0", vector_move))):
+                bank = psum.tile([P, P], F32, name=bank_name)
+                for g in range(PASSES):
+                    z0 = g * Z + 3 * P
+                    a0 = g * A + COLS + PIECE + i * P
+                    nc.tensor.matmul_mx(
+                        out=bank[:],
+                        lhsT=h_codes[:, z0 : z0 + P].bitcast(E4M3X4),
+                        lhsT_scale=h_sbytes[:, z0 : z0 + P],
+                        rhs=com_codes[:, a0 : a0 + P].bitcast(E4M3X4),
+                        rhs_scale=com_sbytes[:, a0 : a0 + P],
+                        start=(g == 0),
+                        stop=(g == PASSES - 1),
+                    )
+                result = work.tile([P, P], F32, name="wide", bufs=WIDE_BUFS)
+                move(result[:], bank[:])
+                a0 = COLS + PIECE + i * P
+                nc.sync.dma_start(out=out[3 * P :, a0 : a0 + P], in_=result[:])

@@ -28,38 +28,13 @@ MODE_BLOCKS = Z // P
 COLS = 512
 PIECE = 256
 WIDE_BUFS = 14
-SORTS = (7, 9, 11, 12, 13, 14, 15)
-FOUR_FROM = 3
 SHORT = 384
-SHORT_C = 320
+SHORT_LATE = 320
+FIRST_GPSIMD = 96
 REST = 64
-HV = 128
-HG = 96
-TAIL = 0
-LO = 0
-EXI = (0, 0, 0, 1)
-OFF = 5
-F3 = 2
-F4 = 1
-SA = 0
-PLANE_LAST = 5
-PLANE_MID = 3
-VO = 1
-SB = 1
-BEFORE = 0
-GA = 3
-GB = 3
-ON_SCALAR = ()
-FOUR = (5, 6)
-CUT_A = 6
-CUT_B = 3
-F0 = 11
-F1 = 1
-F1B = 1
-F2 = 5
-FA = 2
-FB = 3
-RESP_BANKS = (("acc1", "acc0", "turn2", "turn3"), ("turn1", "h0", "h1"))
+ON_SCALAR = 5
+TWO_RUNS = 5
+RESP_BANKS = ("acc1", "acc0", "turn2", "turn3")
 
 
 def tile_modal_response_estimate_s7_kernel(
@@ -109,7 +84,6 @@ def tile_modal_response_estimate_s7_kernel(
         h_planes = {}
         h_grouped = {}
         resp = {}
-        H_TAG = {}
 
         def scalar_move(out, in_):
             nc.scalar.copy(out=out, in_=in_)
@@ -352,19 +326,10 @@ def tile_modal_response_estimate_s7_kernel(
         def interleave_last_half(g, move):
             interleave(move, h_grouped[g][:, J * PIECE :], h_planes[g][:])
 
-        def interleave_h_columns(g, first, last, move):
+        def interleave_h(g, first, last, move, name=None):
             if first == 0:
-                h_grouped[g] = once.tile([P, J * Z], BF16, name=H_TAG.get(g, "h_grouped%d" % g), align_bytes=64)
+                h_grouped[g] = once.tile([P, J * Z], BF16, name=name or "h_grouped%d" % g, align_bytes=64)
             interleave(move, h_grouped[g][:, J * first : J * last], h_planes[g][:, :, first:last])
-
-        def interleave_h(g, pair, move):
-            if pair == 0:
-                h_grouped[g] = once.tile([P, J * Z], BF16, name="h_grouped%d" % g, align_bytes=64)
-            interleave(
-                move,
-                h_grouped[g][:, pair * J * PIECE : (pair + 1) * J * PIECE],
-                h_planes[g][:, :, pair * PIECE : (pair + 1) * PIECE],
-            )
 
         def quantize_h(g, first=0, count=MODE_BLOCKS):
             cols = slice(g * Z + first * P, g * Z + (first + count) * P)
@@ -374,13 +339,13 @@ def tile_modal_response_estimate_s7_kernel(
                 in_=h_grouped[g][:, first * J * P : (first + count) * J * P],
             )
 
-        def stage2(mb, half, g, first=0, count=COLS, last=PASSES - 1):
+        def stage2(mb, g, first=0, count=COLS, last=PASSES - 1):
             if g == 0 and first == 0:
-                resp[mb, half] = psum.tile([P, COLS], F32, name=RESP_BANKS[half][mb])
+                resp[mb] = psum.tile([P, COLS], F32, name=RESP_BANKS[mb])
             z0 = g * Z + mb * P
-            a0 = g * A + half * COLS + first
+            a0 = g * A + first
             nc.tensor.matmul_mx(
-                out=resp[mb, half][:, first : first + count],
+                out=resp[mb][:, first : first + count],
                 lhsT=h_codes[:, z0 : z0 + P].bitcast(E4M3X4),
                 lhsT_scale=h_sbytes[:, z0 : z0 + P],
                 rhs=com_codes[:, a0 : a0 + count].bitcast(E4M3X4),
@@ -413,11 +378,22 @@ def tile_modal_response_estimate_s7_kernel(
             rows = out.rearrange("(m p) a -> p m a", p=P)
             nc.sync.dma_start(out=rows[:, blocks[0] : blocks[-1] + 1, a0 : a0 + PIECE], in_=result[:])
 
-        def store(mb, half, move, first=0, count=COLS):
-            result = work.tile([P, count], F32, name="wide", bufs=WIDE_BUFS)
-            move(result[:], resp[mb, half][:, first : first + count])
-            a0 = half * COLS + first
-            nc.sync.dma_start(out=out[mb * P : (mb + 1) * P, a0 : a0 + count], in_=result[:])
+        def store(mb):
+            result = work.tile([P, COLS], F32, name="wide", bufs=WIDE_BUFS)
+            nc.scalar.copy(out=result[:], in_=resp[mb][:])
+            nc.sync.dma_start(out=out[mb * P : (mb + 1) * P, 0:COLS], in_=result[:])
+
+        def casts(unit, half):
+            widen(unit, half, 1)
+            widen(unit, half, 0)
+
+        def planes(unit):
+            turn_plane(unit, 0)
+            turn_plane(unit, 1)
+
+        def weigh(unit):
+            weigh_plane(unit, 0)
+            weigh_plane(unit, 1)
 
         nc.vector.memset(ident[:], 0.0)
         nc.vector.memset(gain_rows32[:], 0.0)
@@ -427,14 +403,9 @@ def tile_modal_response_estimate_s7_kernel(
         nc.scalar.activation(out=gain_rows[:], in_=gain_rows32[:], func=COPY)
         load_first_bytes(0, 0)
         load_first_bytes(0, 1)
-        if LO == 0:
-            load_recon(0, 0, PIECE)
+        load_recon(0, 0, PIECE)
         load_first_bytes(1, 0)
-        if LO == 1:
-            load_recon(0, 0, PIECE)
         load_first_bytes(1, 1)
-        if LO == 2:
-            load_recon(0, 0, PIECE)
         load_bytes(1, (0,))
         load_recon(0, PIECE, Z)
         load_recon(1, 0, Z)
@@ -457,16 +428,16 @@ def tile_modal_response_estimate_s7_kernel(
         for b in range(2):
             for row in range(2):
                 first_turn(b, row)
-        share_recon(0, 0, 0, HV, vector_move, "early0")
-        share_recon(0, 0, HV, PIECE, scalar_move)
-        share_recon(0, 1, 0, HG, gpsimd_move, "early1")
+        share_recon(0, 0, 0, P, vector_move, "early0")
+        share_recon(0, 0, P, PIECE, scalar_move)
+        share_recon(0, 1, 0, FIRST_GPSIMD, gpsimd_move, "early1")
         scale_slopes(0, 0)
         scale_slopes(0, 1)
         widen(1, 0, 0)
         widen(1, 0, 1)
         turn_slopes(1, 0, 2)
         turn_slopes(1, 1, 3)
-        share_recon(0, 1, HG, PIECE, scalar_move)
+        share_recon(0, 1, FIRST_GPSIMD, PIECE, scalar_move)
         interleave_recon(1, SHORT, Z, scalar_move, "early2")
         widen(0, 1, 0)
         widen(0, 1, 1)
@@ -489,55 +460,19 @@ def tile_modal_response_estimate_s7_kernel(
         quantize_recon(1, 0)
         quantize_slopes(1, 0, 2)
 
-        fillers = []
-        for unit in range(2, UNITS):
-            for half in range(2):
-                fillers.append((widen, (unit, half, 1)))
-                fillers.append((widen, (unit, half, 0)))
-                if 2 * unit + half in SORTS:
-                    fillers.append((sort_words, (unit, half)))
-
-        def fill(count):
-            for job, args in fillers[:count]:
-                job(*args)
-            fillers[:count] = []
-
-        def planes(unit):
-            turn_plane(unit, 0)
-            turn_plane(unit, 1)
-
-        def weigh(unit):
-            weigh_plane(unit, 0)
-            weigh_plane(unit, 1)
-
-        window_pieces = {2: (0, 0), 3: (1, 0), 4: (2, 0), 5: (0, 1), 6: (3, 0), 7: (1, 1)}
-
-        def extra_piece(unit, move):
-            if unit in (2, 3):
-                interleave_commands(2, 1, move, "held1" if unit == 2 else None, (unit - 2) * PIECE, PIECE)
-            if unit in (4, 5):
-                interleave_h(0, unit - 4, move)
-            if unit == 6:
-                interleave_commands(3, 1, move, "early3", 0, PIECE)
-
-        def window(unit):
-            interleave_commands(*window_pieces[unit], gpsimd_move, "held0" if unit == 2 else "held%d" % (unit - 1))
-            if unit != OFF:
-                extra_piece(unit, gpsimd_move)
-            elif unit == 3:
-                interleave_commands(2, 1, gpsimd_move, None, PIECE, REST)
-            else:
-                interleave_h_columns(0, (unit - 4) * PIECE, (unit - 4) * PIECE + REST, gpsimd_move)
-
         interleave_recon(2, 0, SHORT, gpsimd_move, "held0")
-        stage1(0, 0, 0, 2)
-        stage1(0, 1, 0, 2)
-        stage1(0, 0, 2, 4)
-        stage1(0, 1, 2, 4)
-        fill(2)
+        for first in (0, 2):
+            stage1(0, 0, first, first + 2)
+            stage1(0, 1, first, first + 2)
+        casts(2, 0)
         nc.scalar.copy(out=gain_cols[:], in_=gain_bank[:, 0:MODE_BLOCKS])
         interleave_recon(3, SHORT, Z, scalar_move, "early1")
-        fill(F0)
+        casts(2, 1)
+        casts(3, 0)
+        casts(3, 1)
+        sort_words(3, 1)
+        casts(4, 0)
+        casts(4, 1)
         turn_slopes(1, 2)
         stage1(1, 0, 0, 4, "h0")
         turn_slopes(1, 3)
@@ -561,18 +496,29 @@ def tile_modal_response_estimate_s7_kernel(
         load_bytes(6, (0, 1))
         load_commands(0, 1)
 
-        window(2)
+        def window(unit):
+            g, half = ((0, 0), (1, 0), (2, 0), (0, 1), (3, 0))[unit - 2]
+            interleave_commands(g, half, gpsimd_move, "held0" if unit == 2 else "held%d" % (unit - 1))
+            if unit < 4:
+                interleave_commands(2, 1, gpsimd_move, "held1" if unit == 2 else None, (unit - 2) * PIECE, PIECE)
+            elif unit < 6:
+                first = (unit - 4) * PIECE
+                interleave_h(0, first, first + (REST if unit == ON_SCALAR else PIECE), gpsimd_move)
+            else:
+                interleave_commands(3, 1, gpsimd_move, "early3", 0, PIECE)
+            for g in range(unit == ON_SCALAR, PASSES):
+                scale_slopes(unit, g)
+
         stage1(0, 0, 6, 8)
         stage1(0, 1, 6, 8)
         limit(0, 0)
         limit(0, 1)
         nc.scalar.copy(out=weight32[:], in_=weight[:])
         turn_slopes(2, 3)
-        for g in range(PASSES):
-            scale_slopes(2, g)
+        window(2)
         turn_slopes(3, 0)
         stage1(1, 0, 4, 8)
-        fill(F1)
+        sort_words(4, 1)
         limit(1, 0)
         turn_plane(0, 0, "acc0")
         turn_plane(0, 1, "acc1")
@@ -582,83 +528,74 @@ def tile_modal_response_estimate_s7_kernel(
         limit(1, 1)
         turn_slopes(3, 2)
         turn_slopes(3, 3)
-        fill(F2)
+        casts(5, 0)
+        casts(5, 1)
+        sort_words(5, 1)
         quantize_slopes(2, 0, 2)
         quantize_slopes(2, 2, 2)
         load_bytes(7, (0, 1))
         load_commands(3, 0)
 
-        for unit in range(3, LAST):
+        for unit in range(3, TWO_RUNS):
             window(unit)
-            for g in range(unit == OFF, PASSES):
-                scale_slopes(unit, g)
-            if unit in FOUR:
-                stage1(unit - 1, 0, 0, 8)
-                if unit < PLANE_MID:
-                    turn_plane(unit - 2, 0)
-                turn_slopes(unit + 1, 0)
-                if PLANE_MID <= unit < PLANE_LAST:
-                    turn_plane(unit - 2, 0)
-                turn_slopes(unit + 1, 1)
-                if unit >= PLANE_LAST:
-                    turn_plane(unit - 2, 0)
-                limit(unit - 1, 0)
-                weigh_plane(unit - 2, 0)
-                if unit + 1 == OFF:
-                    scale_on_scalar(OFF, 0)
-                    fill(F4)
-                else:
-                    fill(GA)
-                stage1(unit - 1, 1, 0, 8)
-                turn_plane(unit - 2, 1)
-                turn_slopes(unit + 1, 2)
-                turn_slopes(unit + 1, 3)
-                limit(unit - 1, 1)
-                weigh_plane(unit - 2, 1)
-                if unit + 1 == OFF:
-                    group_on_scalar(OFF, 0)
-                    fill(F3)
-                else:
-                    fill(GB)
+            stage1(unit - 1, 0, 0, 6)
+            planes(unit - 2)
+            turn_slopes(unit + 1, 0)
+            weigh(unit - 2)
+            stage1(unit - 1, 0, 6, 8)
+            stage1(unit - 1, 1, 0, 3)
+            limit(unit - 1, 0)
+            if unit + 1 == ON_SCALAR:
+                scale_on_scalar(ON_SCALAR, 0)
             else:
-                stage1(unit - 1, 0, 0, CUT_A)
-                planes(unit - 2)
-                turn_slopes(unit + 1, 0)
-                weigh(unit - 2)
-                stage1(unit - 1, 0, CUT_A, 8)
-                stage1(unit - 1, 1, 0, CUT_B)
-                limit(unit - 1, 0)
-                if unit + 1 == OFF:
-                    scale_on_scalar(OFF, 0)
-                else:
-                    fill(FA)
-                turn_slopes(unit + 1, 1)
-                stage1(unit - 1, 1, CUT_B, 8)
-                if unit == LAST - 1:
-                    interleave_h(1, 1, scalar_move)
-                limit(unit - 1, 1)
-                if unit + 1 == OFF:
-                    group_on_scalar(OFF, 0)
-                    fill(F3)
-                else:
-                    fill(FB)
-                turn_slopes(unit + 1, 2)
-                turn_slopes(unit + 1, 3)
+                casts(6, 0)
+            turn_slopes(unit + 1, 1)
+            stage1(unit - 1, 1, 3, 8)
+            limit(unit - 1, 1)
+            if unit + 1 == ON_SCALAR:
+                group_on_scalar(ON_SCALAR, 0)
+                sort_words(6, 1)
+                widen(LAST, 0, 1)
+            else:
+                sort_words(6, 0)
+                casts(6, 1)
+            turn_slopes(unit + 1, 2)
+            turn_slopes(unit + 1, 3)
             quantize_slopes(unit, 0, 2)
             quantize_slopes(unit, 2, 2)
-            if unit == 3:
-                load_commands(3, 1)
-            if unit == 4:
-                load_commands(1, 1)
+            load_commands((3, 1)[unit - 3], 1)
 
-        interleave_h_columns(0, PIECE + REST, Z, scalar_move)
-        H_TAG[1] = "held6"
-        interleave_h_columns(1, 0, SHORT_C, gpsimd_move)
+        for unit in range(TWO_RUNS, LAST):
+            window(unit)
+            stage1(unit - 1, 0, 0, 8)
+            turn_slopes(unit + 1, 0)
+            turn_slopes(unit + 1, 1)
+            turn_plane(unit - 2, 0)
+            limit(unit - 1, 0)
+            weigh_plane(unit - 2, 0)
+            if unit + 2 == LAST:
+                widen(LAST, 0, 0)
+                sort_words(LAST, 0)
+                widen(LAST, 1, 1)
+            stage1(unit - 1, 1, 0, 8)
+            turn_plane(unit - 2, 1)
+            turn_slopes(unit + 1, 2)
+            turn_slopes(unit + 1, 3)
+            limit(unit - 1, 1)
+            weigh_plane(unit - 2, 1)
+            if unit + 2 == LAST:
+                widen(LAST, 1, 0)
+                sort_words(LAST, 1)
+            quantize_slopes(unit, 0, 2)
+            quantize_slopes(unit, 2, 2)
+
+        interleave_h(0, PIECE + REST, Z, scalar_move)
+        interleave_h(1, 0, SHORT_LATE, gpsimd_move, "held6")
         scale_slopes(LAST, 0)
         scale_slopes(LAST, 1)
         quantize_h(0, 0, 2)
         quantize_slopes(LAST, 0, 2)
-        interleave_commands(1, 1, gpsimd_move, "held7", 0, SHORT_C)
+        interleave_commands(1, 1, gpsimd_move, "held7", 0, SHORT_LATE)
         scale_slopes(LAST, 2)
         scale_slopes(LAST, 3)
         quantize_slopes(LAST, 2, 1)
@@ -674,37 +611,30 @@ def tile_modal_response_estimate_s7_kernel(
         turn_half_planes(LAST - 1, "acc0")
         turn_block(LAST - 1, 0)
         turn_block(LAST - 1, 1)
-        interleave_h_columns(1, SHORT_C, Z, scalar_move)
+        interleave_h(1, SHORT_LATE, Z, scalar_move)
         weigh_half_planes(LAST - 1)
-        if SB == 0:
-            interleave_h(2, 0, scalar_move)
         stage1(LAST, 0, 4, 8)
         stage1(LAST, 1, 4, 8)
         limit(LAST, 0)
         limit(LAST, 1)
-        if SB == 1:
-            interleave_h(2, 0, scalar_move)
+        interleave_h(2, 0, PIECE, scalar_move)
 
-        EX = [(scalar_move, vector_move)[i] for i in EXI]
         quantize_commands(0, 0, 0, PIECE)
         quantize_commands(0, 0, PIECE, PIECE)
         quantize_h(0, 2, 2)
         quantize_h(1)
         quantize_commands(1, 0)
-        stage2(0, 0, 0, 0, PIECE)
-        stage2(0, 0, 0, PIECE, PIECE)
-        stage2(2, 0, 0)
-        stage2(3, 0, 0)
-        stage2(1, 0, 0)
-        for mb in range(BEFORE):
-            stage2(mb, 0, 1)
+        stage2(0, 0, 0, PIECE)
+        stage2(0, 0, PIECE, PIECE)
+        for mb in (2, 3, 1):
+            stage2(mb, 0)
         turn_block(LAST, 0)
         turn_block(LAST, 1)
         turn_half_planes(LAST, "turn0")
         weigh_half_planes(LAST)
-        interleave_h(2, 1, scalar_move)
-        for mb in range(BEFORE, MODE_BLOCKS):
-            stage2(mb, 0, 1)
+        interleave_h(2, PIECE, Z, scalar_move)
+        for mb in range(MODE_BLOCKS):
+            stage2(mb, 1)
         quantize_commands(0, 1)
         quantize_commands(3, 0, 0, PIECE)
         weigh_block(3, 0)
@@ -715,63 +645,35 @@ def tile_modal_response_estimate_s7_kernel(
         quantize_h(2, 0, 2)
         quantize_commands(2, 0)
         quantize_h(2, 2, 2)
-        if VO == 0:
-            for g in (1, 2, 3):
-                quantize_commands(g, 1, 0, PIECE)
-            quantize_h(3, 2, 2)
-        else:
-            quantize_commands(1, 1, 0, PIECE)
-            quantize_commands(2, 1, 0, PIECE)
-            quantize_h(3, 2, 2)
-            quantize_commands(3, 1, 0, PIECE)
-        interleave_commands(1, 1, vector_move, None, SHORT_C, COLS - SHORT_C)
+        quantize_commands(1, 1, 0, PIECE)
+        quantize_commands(2, 1, 0, PIECE)
+        quantize_h(3, 2, 2)
+        quantize_commands(3, 1, 0, PIECE)
+        interleave_commands(1, 1, vector_move, None, SHORT_LATE, COLS - SHORT_LATE)
         interleave_commands(3, 1, vector_move, None, PIECE, PIECE)
         for g in (1, 2, 3):
             quantize_commands(g, 1, PIECE, PIECE)
         quarter((0, 1), 0, (0,), "turn1")
         quarter((2, 3), 0, (0,), "h0")
-        quarter((0, 1), 1, (0,), "h1")
+        quarter((0,), 1, (0,), "h1")
+        quarter((1,), 1, (0,), "turn0")
         for mb in range(2):
-            stage2(mb, 0, 3, last=2)
+            stage2(mb, 3, last=2)
         for mb in range(2):
-            stage2(mb, 0, 2, last=2)
-            store(mb, 0, scalar_move)
+            stage2(mb, 2, last=2)
+            store(mb)
         for mb in (2, 3):
-            stage2(mb, 0, 2)
-        if VO == 0:
-            quarter((0, 1), 0, (1, 2, 3))
-            store_quarter((0, 1), 0, EX[0])
+            stage2(mb, 2)
         for mb in (2, 3):
-            stage2(mb, 0, 3)
-            store(mb, 0, EX[mb - 1])
-        if VO == 1:
-            quarter((0, 1), 0, (1, 2, 3))
-            store_quarter((0, 1), 0, EX[0])
+            stage2(mb, 3)
+            store(mb)
+        quarter((0, 1), 0, (1, 2, 3))
+        store_quarter((0, 1), 0, scalar_move)
         quarter((2, 3), 0, (1, 2, 3))
-        store_quarter((2, 3), 0, EX[3])
-        quarter((0, 1), 1, (1, 2, 3))
-        store_quarter((0, 1), 1, scalar_move)
-        quarter((2,), 1, (0, 1, 2, 3), "turn0")
-        store_quarter((2,), 1, vector_move)
-        if TAIL == 0:
-            quarter((3,), 1, (0, 1, 2, 3), "acc1")
-            store_quarter((3,), 1, scalar_move)
-        else:
-            for i, (bank_name, move) in enumerate((("acc1", scalar_move), ("acc0", vector_move))):
-                bank = psum.tile([P, P], F32, name=bank_name)
-                for g in range(PASSES):
-                    z0 = g * Z + 3 * P
-                    a0 = g * A + COLS + PIECE + i * P
-                    nc.tensor.matmul_mx(
-                        out=bank[:],
-                        lhsT=h_codes[:, z0 : z0 + P].bitcast(E4M3X4),
-                        lhsT_scale=h_sbytes[:, z0 : z0 + P],
-                        rhs=com_codes[:, a0 : a0 + P].bitcast(E4M3X4),
-                        rhs_scale=com_sbytes[:, a0 : a0 + P],
-                        start=(g == 0),
-                        stop=(g == PASSES - 1),
-                    )
-                result = work.tile([P, P], F32, name="wide", bufs=WIDE_BUFS)
-                move(result[:], bank[:])
-                a0 = COLS + PIECE + i * P
-                nc.sync.dma_start(out=out[3 * P :, a0 : a0 + P], in_=result[:])
+        store_quarter((2, 3), 0, vector_move)
+        for mb in range(2):
+            quarter((mb,), 1, (1, 2, 3))
+            store_quarter((mb,), 1, (scalar_move, vector_move)[mb])
+        for mb in (2, 3):
+            quarter((mb,), 1, (0, 1, 2, 3), ("turn2", "acc1")[mb - 2])
+            store_quarter((mb,), 1, (scalar_move, vector_move)[mb - 2])

@@ -34,6 +34,12 @@ FIRST_GPSIMD = 96
 REST = 64
 ON_SCALAR = 5
 TWO_RUNS = 5
+HW_BUFS = 3
+SCALAR_UNITS = (4, 6)
+BROAD = 320
+NARROW = 128
+LATE = 192
+AHEAD = 3
 RESP_BANKS = ("acc1", "acc0", "turn2", "turn3")
 
 
@@ -57,8 +63,10 @@ def tile_modal_response_estimate_s7_kernel(
         gain_rows = once.tile([P, P], BF16, name="gain_rows")
         gain_rows32 = once.tile([P, P], F32, name="gain_rows32")
         gain_cols = once.tile([P, MODE_BLOCKS], F32, name="gain_cols")
-        weight = once.tile([P, PASSES, J], BF16, name="weight")
-        weight32 = once.tile([P, PASSES, J], F32, name="weight32")
+        weight = [once.tile([P, P * J], BF16, name="weight%d" % g) for g in range(PASSES - 1)]
+        last_weight = once.tile([P, J], BF16, name="last_weight")
+        last_weight32 = once.tile([P, J], F32, name="last_weight32")
+        last_planes = once.tile([P, J, PIECE], BF16, name="last_planes")
 
         recon_codes = once.tile([P, PASSES * Z], U32, name="recon_codes", align_bytes=64)
         recon_sbytes = once.tile([P, PASSES * Z], U8, name="recon_sbytes", align_bytes=64)
@@ -81,7 +89,7 @@ def tile_modal_response_estimate_s7_kernel(
         acc = {}
         h_raw = {}
         h_turned = {}
-        h_planes = {}
+        h_words = {}
         h_grouped = {}
         resp = {}
 
@@ -122,9 +130,12 @@ def tile_modal_response_estimate_s7_kernel(
             recon_raw[g, (last - 1) // PIECE] = (raw, first)
 
         def load_commands(g, half):
-            raw = work.tile([P, J, COLS], BF16, name="com_raw", bufs=4)
+            raw = work.tile([P, J, COLS], BF16, name="com_raw", bufs=5)
             nc.sync.dma_start(out=raw[:], in_=commands_view[g][:, :, half * COLS : (half + 1) * COLS])
             com_raw[g, half] = raw
+
+        def load_weight(g):
+            nc.sync.dma_start(out=weight[g][:], in_=frame_weight[g * P * J : (g + 1) * P * J].partition_broadcast(P))
 
         def interleave_recon(g, first, last, move, name):
             raw, z0 = recon_raw[g, first // PIECE]
@@ -175,7 +186,7 @@ def tile_modal_response_estimate_s7_kernel(
                 nc.tensor.transpose(bank[:, w, :], words[:, w:256:2], ident[:])
 
         def sort_words(unit, half):
-            ordered = work.tile([P, 2, 2, P], F32, name="ordered", bufs=6)
+            ordered = work.tile([P, 2, 2, P], F32, name="ordered", bufs=2)
             nc.scalar.copy(
                 out=ordered[:], in_=widened[unit, half, 1][:].bitcast(F32).rearrange("p (b m w) -> p b w m", b=2, w=2)
             )
@@ -247,7 +258,7 @@ def tile_modal_response_estimate_s7_kernel(
             )
 
         def stage1(unit, pair, first, last, bank_name=None):
-            if first == 0:
+            if first == 0 and last > 0 and (unit, pair) not in acc:
                 acc[unit, pair] = psum.tile([P, 2, UNIT], F32, name=bank_name or "acc%d" % pair)
             codes, sbytes = slope_codes[unit]
             for n in range(first, last):
@@ -265,53 +276,71 @@ def tile_modal_response_estimate_s7_kernel(
                 )
 
         def limit(unit, pair):
+            if pair == 0:
+                h_raw[unit] = work.tile([P, MODE_BLOCKS * UNIT], F32, name="h_raw", bufs=3)
             for i in range(2):
                 mb = 2 * pair + i
-                h_raw[unit, mb] = work.tile([P, UNIT], F32, name="h_raw", bufs=12)
+                order = "p (e r) -> p r e" if unit < LAST - 1 else "p (r e) -> p r e"
                 nc.scalar.activation(
-                    out=h_raw[unit, mb][:], in_=acc[unit, pair][:, i, :], func=TANH, scale=gain_cols[:, mb : mb + 1]
+                    out=h_raw[unit][:, mb * UNIT : (mb + 1) * UNIT].rearrange("p (r e) -> p r e", e=2),
+                    in_=acc[unit, pair][:, i, :].rearrange(order, e=2),
+                    func=TANH,
+                    scale=gain_cols[:, mb : mb + 1],
                 )
 
-        def turn_plane(unit, row, bank_name=None):
-            bank = psum.tile([P, Z], F32, name=bank_name or "h%d" % row)
-            for mb in range(MODE_BLOCKS):
-                nc.tensor.transpose(bank[:, mb * P : (mb + 1) * P], h_raw[unit, mb][:, row * P : (row + 1) * P], ident[:])
-            h_turned[unit, row] = bank
-
-        def weigh_plane(unit, row):
-            g, t = divmod(2 * unit + row, J)
-            if t == 0:
-                h_planes[g] = work.tile([P, J, Z], BF16, name="h_planes", bufs=3)
-            nc.scalar.activation(
-                out=h_planes[g][:, t, :], in_=h_turned[unit, row][:], func=COPY, scale=weight32[:, g, t : t + 1]
+        def weigh(unit, engine, first=0, count=MODE_BLOCKS, name=None):
+            g, pair = divmod(unit, 2)
+            if name:
+                words = once.tile([P, count * UNIT], BF16, name=name, align_bytes=64)
+            else:
+                words = work.tile([P, count * UNIT], BF16, name="h_words", bufs=HW_BUFS)
+            for i in range(count):
+                h_words[unit, first + i] = words[:].bitcast(F32)[:, i * P : (i + 1) * P]
+            factors = weight[g][:].rearrange("p (r t) -> p r t", t=J)[:, :, 2 * pair : 2 * pair + 2]
+            engine.tensor_tensor(
+                out=words[:].rearrange("p (m r e) -> p m r e", m=count, e=2),
+                in0=h_raw[unit][:, first * UNIT : (first + count) * UNIT].rearrange("p (m r e) -> p m r e", m=count, e=2),
+                in1=factors.unsqueeze(1).to_broadcast([P, count, P, 2]),
+                op=MULT,
             )
+
+        def turn_h(unit, half, bank_name=None):
+            g, pair = divmod(unit, 2)
+            if pair == 0:
+                h_turned[g, half] = psum.tile([P, 2, PIECE], F32, name=bank_name or "h%d" % half)
+            for i in range(2):
+                nc.tensor.transpose(h_turned[g, half][:, pair, i * P : (i + 1) * P], h_words[unit, 2 * half + i], ident[:])
+
+        def take_h(g, half, move=scalar_move):
+            if half == 0:
+                h_grouped[g] = once.tile([P, J * Z], BF16, name="h_grouped%d" % g, align_bytes=64)
+            move(
+                h_grouped[g][:, half * J * PIECE : (half + 1) * J * PIECE].bitcast(F32).rearrange("p (z w) -> p z w", w=2),
+                h_turned[g, half][:].rearrange("p w z -> p z w"),
+            )
+
+        def raw_rows(unit, mb, row):
+            return h_raw[unit][:, mb * UNIT + row * P : mb * UNIT + (row + 1) * P]
 
         def turn_half_planes(unit, bank_name):
             bank = psum.tile([P, 2, PIECE], F32, name=bank_name)
             for row in range(2):
                 for i in range(2):
-                    nc.tensor.transpose(
-                        bank[:, row, i * P : (i + 1) * P], h_raw[unit, 2 + i][:, row * P : (row + 1) * P], ident[:]
-                    )
+                    nc.tensor.transpose(bank[:, row, i * P : (i + 1) * P], raw_rows(unit, 2 + i, row), ident[:])
             h_turned["half", unit] = bank
 
         def weigh_half_planes(unit):
-            g = unit // 2
-            if unit % 2 == 0:
-                h_planes[g] = work.tile([P, J, PIECE], BF16, name="h_planes", bufs=3)
             for row in range(2):
                 t = 2 * (unit % 2) + row
                 nc.scalar.activation(
-                    out=h_planes[g][:, t, :], in_=h_turned["half", unit][:, row, :], func=COPY, scale=weight32[:, g, t : t + 1]
+                    out=last_planes[:, t, :], in_=h_turned["half", unit][:, row, :], func=COPY, scale=last_weight32[:, t : t + 1]
                 )
 
         def turn_block(unit, mb):
             if unit % 2 == 0:
                 h_turned["block", mb] = psum.tile([P, J, P], F32, name="h%d" % mb)
             for row in range(2):
-                nc.tensor.transpose(
-                    h_turned["block", mb][:, 2 * (unit % 2) + row, :], h_raw[unit, mb][:, row * P : (row + 1) * P], ident[:]
-                )
+                nc.tensor.transpose(h_turned["block", mb][:, 2 * (unit % 2) + row, :], raw_rows(unit, mb, row), ident[:])
 
         def weigh_block(g, mb):
             if mb == 0:
@@ -319,17 +348,12 @@ def tile_modal_response_estimate_s7_kernel(
             nc.vector.tensor_tensor(
                 out=h_grouped[g][:, mb * J * P : (mb + 1) * J * P].rearrange("p (z t) -> p z t", t=J),
                 in0=h_turned["block", mb][:].rearrange("p t z -> p z t"),
-                in1=weight[:, g, :].unsqueeze(1).to_broadcast([P, P, J]),
+                in1=last_weight[:].unsqueeze(1).to_broadcast([P, P, J]),
                 op=MULT,
             )
 
         def interleave_last_half(g, move):
-            interleave(move, h_grouped[g][:, J * PIECE :], h_planes[g][:])
-
-        def interleave_h(g, first, last, move, name=None):
-            if first == 0:
-                h_grouped[g] = once.tile([P, J * Z], BF16, name=name or "h_grouped%d" % g, align_bytes=64)
-            interleave(move, h_grouped[g][:, J * first : J * last], h_planes[g][:, :, first:last])
+            interleave(move, h_grouped[g][:, J * PIECE :], last_planes[:])
 
         def quantize_h(g, first=0, count=MODE_BLOCKS):
             cols = slice(g * Z + first * P, g * Z + (first + count) * P)
@@ -387,14 +411,6 @@ def tile_modal_response_estimate_s7_kernel(
             widen(unit, half, 1)
             widen(unit, half, 0)
 
-        def planes(unit):
-            turn_plane(unit, 0)
-            turn_plane(unit, 1)
-
-        def weigh(unit):
-            weigh_plane(unit, 0)
-            weigh_plane(unit, 1)
-
         nc.vector.memset(ident[:], 0.0)
         nc.vector.memset(gain_rows32[:], 0.0)
         make_identity(nc, ident[:], nomemset=True)
@@ -419,10 +435,9 @@ def tile_modal_response_estimate_s7_kernel(
         load_bytes(3, (0, 1))
         load_commands(0, 0)
         load_bytes(4, (0, 1))
-        load_commands(2, 1)
-        nc.sync.dma_start(out=weight[:], in_=frame_weight.rearrange("(g p t) -> p g t", p=P, t=J))
         load_commands(1, 0)
         load_bytes(5, (0, 1))
+        load_weight(0)
         load_commands(2, 0)
 
         for b in range(2):
@@ -470,7 +485,6 @@ def tile_modal_response_estimate_s7_kernel(
         casts(2, 1)
         casts(3, 0)
         casts(3, 1)
-        sort_words(3, 1)
         casts(4, 0)
         casts(4, 1)
         turn_slopes(1, 2)
@@ -495,129 +509,120 @@ def tile_modal_response_estimate_s7_kernel(
         quantize_slopes(1, 2, 2)
         load_bytes(6, (0, 1))
         load_commands(0, 1)
+        load_weight(1)
 
-        def window(unit):
-            g, half = ((0, 0), (1, 0), (2, 0), (0, 1), (3, 0))[unit - 2]
-            interleave_commands(g, half, gpsimd_move, "held0" if unit == 2 else "held%d" % (unit - 1))
-            if unit < 4:
-                interleave_commands(2, 1, gpsimd_move, "held1" if unit == 2 else None, (unit - 2) * PIECE, PIECE)
-            elif unit < 6:
-                first = (unit - 4) * PIECE
-                interleave_h(0, first, first + (REST if unit == ON_SCALAR else PIECE), gpsimd_move)
+
+        def window(unit, share):
+            g, half = ((0, 0), (2, 0), (0, 1), (3, 0), (2, 1), (1, 1))[unit - 2]
+            interleave_commands(g, half, gpsimd_move, "held0" if unit == 2 else "held%d" % (unit - 1), 0, share)
+            if unit == 2:
+                weigh(0, nc.gpsimd, 0, 2)
             else:
-                interleave_commands(3, 1, gpsimd_move, "early3", 0, PIECE)
-            for g in range(unit == ON_SCALAR, PASSES):
+                if unit == 3:
+                    weigh(0, nc.gpsimd, 2, 2)
+                weigh(unit - 2, nc.gpsimd)
+            for g in range(unit in SCALAR_UNITS, PASSES):
                 scale_slopes(unit, g)
 
+        def two_runs(unit, a, b, c, ahead=0):
+            stage1(unit - 1, 0, 0, 8)
+            stage1(unit - 1, 1, 0, ahead)
+            turn_h(unit - 3, 0)
+            turn_slopes(unit + 1, 0)
+            turn_slopes(unit + 1, 1)
+            a()
+            limit(unit - 1, 0)
+            stage1(unit - 1, 1, ahead, 8)
+            turn_h(unit - 3, 1)
+            turn_slopes(unit + 1, 2)
+            turn_slopes(unit + 1, 3)
+            b()
+            limit(unit - 1, 1)
+            c()
+            quantize_slopes(unit, 0, 2)
+            quantize_slopes(unit, 2, 2)
+
+        def il(g, half, first, last, name=None):
+            interleave_commands(g, half, scalar_move, name, first, last - first)
+
+        def nothing():
+            return None
+
+        il(1, 0, 0, 192, "held1")
         stage1(0, 0, 6, 8)
         stage1(0, 1, 6, 8)
         limit(0, 0)
         limit(0, 1)
-        nc.scalar.copy(out=weight32[:], in_=weight[:])
         turn_slopes(2, 3)
-        window(2)
+        window(2, COLS)
         turn_slopes(3, 0)
         stage1(1, 0, 4, 8)
-        sort_words(4, 1)
-        limit(1, 0)
-        turn_plane(0, 0, "acc0")
-        turn_plane(0, 1, "acc1")
-        turn_slopes(3, 1)
-        weigh(0)
-        stage1(1, 1, 4, 8)
-        limit(1, 1)
-        turn_slopes(3, 2)
-        turn_slopes(3, 3)
         casts(5, 0)
+        limit(1, 0)
+        turn_slopes(3, 1)
+        turn_slopes(3, 2)
+        stage1(1, 1, 4, 8)
         casts(5, 1)
-        sort_words(5, 1)
+        limit(1, 1)
+        turn_slopes(3, 3)
         quantize_slopes(2, 0, 2)
         quantize_slopes(2, 2, 2)
         load_bytes(7, (0, 1))
         load_commands(3, 0)
+        load_weight(2)
+        nc.sync.dma_start(out=last_weight[:], in_=frame_weight.rearrange("(g p t) -> g p t", p=P, t=J)[PASSES - 1])
+        load_commands(2, 1)
 
-        for unit in range(3, TWO_RUNS):
-            window(unit)
-            stage1(unit - 1, 0, 0, 6)
-            planes(unit - 2)
-            turn_slopes(unit + 1, 0)
-            weigh(unit - 2)
-            stage1(unit - 1, 0, 6, 8)
-            stage1(unit - 1, 1, 0, 3)
-            limit(unit - 1, 0)
-            if unit + 1 == ON_SCALAR:
-                scale_on_scalar(ON_SCALAR, 0)
-            else:
-                casts(6, 0)
-            turn_slopes(unit + 1, 1)
-            stage1(unit - 1, 1, 3, 8)
-            limit(unit - 1, 1)
-            if unit + 1 == ON_SCALAR:
-                group_on_scalar(ON_SCALAR, 0)
-                sort_words(6, 1)
-                widen(LAST, 0, 1)
-            else:
-                sort_words(6, 0)
-                casts(6, 1)
-            turn_slopes(unit + 1, 2)
-            turn_slopes(unit + 1, 3)
-            quantize_slopes(unit, 0, 2)
-            quantize_slopes(unit, 2, 2)
-            load_commands((3, 1)[unit - 3], 1)
+        window(3, REST)
+        two_runs(3, lambda: (il(1, 0, 192, COLS), load_commands(1, 1)), lambda: (scale_on_scalar(4, 0), casts(6, 0)), lambda: (il(2, 0, REST, 192), group_on_scalar(4, 0)), AHEAD)
+        window(4, NARROW)
+        two_runs(4, lambda: casts(6, 1), lambda: (casts(7, 0), take_h(0, 0)), lambda: take_h(0, 1))
+        window(5, BROAD)
+        two_runs(5, lambda: casts(7, 1), lambda: scale_on_scalar(6, 0), lambda: group_on_scalar(6, 0))
+        window(6, NARROW)
+        two_runs(
+            6,
+            lambda: (il(2, 0, 192, COLS), load_commands(3, 1)),
+            lambda: (take_h(1, 0), il(0, 1, NARROW, PIECE)),
+            lambda: (take_h(1, 1), nc.scalar.copy(out=last_weight32[:], in_=last_weight[:])),
+        )
 
-        for unit in range(TWO_RUNS, LAST):
-            window(unit)
-            stage1(unit - 1, 0, 0, 8)
-            turn_slopes(unit + 1, 0)
-            turn_slopes(unit + 1, 1)
-            turn_plane(unit - 2, 0)
-            limit(unit - 1, 0)
-            weigh_plane(unit - 2, 0)
-            if unit + 2 == LAST:
-                widen(LAST, 0, 0)
-                sort_words(LAST, 0)
-                widen(LAST, 1, 1)
-            stage1(unit - 1, 1, 0, 8)
-            turn_plane(unit - 2, 1)
-            turn_slopes(unit + 1, 2)
-            turn_slopes(unit + 1, 3)
-            limit(unit - 1, 1)
-            weigh_plane(unit - 2, 1)
-            if unit + 2 == LAST:
-                widen(LAST, 1, 0)
-                sort_words(LAST, 1)
-            quantize_slopes(unit, 0, 2)
-            quantize_slopes(unit, 2, 2)
-
-        interleave_h(0, PIECE + REST, Z, scalar_move)
-        interleave_h(1, 0, SHORT_LATE, gpsimd_move, "held6")
+        weigh(LAST - 2, nc.gpsimd, 0, 2, "held6")
+        weigh(LAST - 2, nc.gpsimd, 2, 1)
         scale_slopes(LAST, 0)
         scale_slopes(LAST, 1)
         quantize_h(0, 0, 2)
         quantize_slopes(LAST, 0, 2)
-        interleave_commands(1, 1, gpsimd_move, "held7", 0, SHORT_LATE)
+        weigh(LAST - 2, nc.gpsimd, 3, 1, "held7")
+        interleave_commands(1, 1, gpsimd_move, "early4", 0, LATE)
         scale_slopes(LAST, 2)
         scale_slopes(LAST, 3)
         quantize_slopes(LAST, 2, 1)
         quantize_slopes(LAST, 3, 1)
         stage1(LAST - 1, 0, 0, 8)
+        il(3, 0, BROAD, COLS)
+        il(2, 1, NARROW, PIECE)
         limit(LAST - 1, 0)
         stage1(LAST - 1, 1, 0, 8)
         limit(LAST - 1, 1)
-        planes(LAST - 2)
-        weigh(LAST - 2)
+        turn_h(LAST - 3, 0)
+        turn_h(LAST - 2, 0)
+        turn_block(LAST - 1, 1)
+        take_h(2, 0)
         stage1(LAST, 0, 0, 4, "turn0")
         stage1(LAST, 1, 0, 4, "turn1")
+        turn_h(LAST - 3, 1, "acc1")
+        turn_h(LAST - 2, 1)
         turn_half_planes(LAST - 1, "acc0")
         turn_block(LAST - 1, 0)
-        turn_block(LAST - 1, 1)
-        interleave_h(1, SHORT_LATE, Z, scalar_move)
+        il(0, 1, PIECE, COLS)
+        take_h(2, 1)
         weigh_half_planes(LAST - 1)
         stage1(LAST, 0, 4, 8)
         stage1(LAST, 1, 4, 8)
         limit(LAST, 0)
         limit(LAST, 1)
-        interleave_h(2, 0, PIECE, scalar_move)
+        il(3, 1, 0, PIECE, "early3")
 
         quantize_commands(0, 0, 0, PIECE)
         quantize_commands(0, 0, PIECE, PIECE)
@@ -632,44 +637,41 @@ def tile_modal_response_estimate_s7_kernel(
         turn_block(LAST, 1)
         turn_half_planes(LAST, "turn0")
         weigh_half_planes(LAST)
-        interleave_h(2, PIECE, Z, scalar_move)
-        for mb in range(MODE_BLOCKS):
-            stage2(mb, 1)
-        quantize_commands(0, 1)
-        quantize_commands(3, 0, 0, PIECE)
+        il(2, 1, PIECE, PIECE + 64)
+        quantize_h(2)
+        quantize_commands(2, 0)
         weigh_block(3, 0)
         interleave_last_half(3, scalar_move)
+        il(2, 1, PIECE + 64, COLS)
         weigh_block(3, 1)
-        quantize_commands(3, 0, PIECE, PIECE)
+        quantize_commands(3, 0)
         quantize_h(3, 0, 2)
-        quantize_h(2, 0, 2)
-        quantize_commands(2, 0)
-        quantize_h(2, 2, 2)
-        quantize_commands(1, 1, 0, PIECE)
-        quantize_commands(2, 1, 0, PIECE)
+        quantize_commands(0, 1)
         quantize_h(3, 2, 2)
+        interleave_commands(1, 1, vector_move, None, LATE, COLS - LATE)
+        quantize_commands(2, 1, 0, PIECE)
+        quantize_commands(1, 1, 0, PIECE)
         quantize_commands(3, 1, 0, PIECE)
-        interleave_commands(1, 1, vector_move, None, SHORT_LATE, COLS - SHORT_LATE)
+        for g in (1, 2):
+            for mb in range(MODE_BLOCKS):
+                stage2(mb, g)
+        for mb in range(2):
+            stage2(mb, 3)
+            store(mb)
+        quarter((0, 1), 0, (0,), "turn1")
+        quarter((2, 3), 0, (0,), "h0")
+        for mb in (2, 3):
+            stage2(mb, 3)
+        for mb in (2, 3):
+            store(mb)
         interleave_commands(3, 1, vector_move, None, PIECE, PIECE)
         for g in (1, 2, 3):
             quantize_commands(g, 1, PIECE, PIECE)
-        quarter((0, 1), 0, (0,), "turn1")
-        quarter((2, 3), 0, (0,), "h0")
         quarter((0,), 1, (0,), "h1")
         quarter((1,), 1, (0,), "turn0")
-        for mb in range(2):
-            stage2(mb, 3, last=2)
-        for mb in range(2):
-            stage2(mb, 2, last=2)
-            store(mb)
-        for mb in (2, 3):
-            stage2(mb, 2)
-        for mb in (2, 3):
-            stage2(mb, 3)
-            store(mb)
-        quarter((0, 1), 0, (1, 2, 3))
+        quarter((0, 1), 0, (2, 1, 3))
         store_quarter((0, 1), 0, scalar_move)
-        quarter((2, 3), 0, (1, 2, 3))
+        quarter((2, 3), 0, (2, 1, 3))
         store_quarter((2, 3), 0, vector_move)
         for mb in range(2):
             quarter((mb,), 1, (1, 2, 3))

@@ -22,25 +22,23 @@ J = 4
 PASSES = 4
 HALF = S // 2
 UNIT = 2 * P
-UNITS = T // UNIT
-LAST = UNITS - 1
+LAST = T // UNIT - 1
 MODE_BLOCKS = Z // P
 COLS = 512
-PIECE = 256
+PIECE = COLS // 2
 WIDE_BUFS = 14
+
 SHORT = 384
-SHORT_LATE = 320
-FIRST_GPSIMD = 96
-REST = 64
-ON_SCALAR = 5
-TWO_RUNS = 5
-HW_BUFS = 3
-SCALAR_UNITS = (4, 6)
 BROAD = 320
-NARROW = 128
-LATE = 192
-AHEAD = 3
-RESP_BANKS = ("acc1", "acc0", "turn2", "turn3")
+NARROW = 96
+REST = 64
+LATE = 2 * NARROW
+SCALAR_UNITS = (2, 4)
+AHEAD = 4
+
+WINDOW_HALVES = ((0, 0), (2, 0), (0, 1), (3, 0), (2, 1), (1, 1))
+BLOCK_BANKS = ("acc0", "turn2")
+RESP_BANKS = ("h0", "acc1", "h1", "turn3")
 
 
 def tile_modal_response_estimate_s7_kernel(
@@ -81,7 +79,6 @@ def tile_modal_response_estimate_s7_kernel(
         com_raw = {}
         com_grouped = {}
         widened = {}
-        sorted_words = {}
         turned = {}
         slopes_grouped = {}
         slope_codes = {}
@@ -130,7 +127,7 @@ def tile_modal_response_estimate_s7_kernel(
             recon_raw[g, (last - 1) // PIECE] = (raw, first)
 
         def load_commands(g, half):
-            raw = work.tile([P, J, COLS], BF16, name="com_raw", bufs=5)
+            raw = work.tile([P, J, COLS], BF16, name="com_raw", bufs=6)
             nc.sync.dma_start(out=raw[:], in_=commands_view[g][:, :, half * COLS : (half + 1) * COLS])
             com_raw[g, half] = raw
 
@@ -154,14 +151,10 @@ def tile_modal_response_estimate_s7_kernel(
             cols = slice(g * Z + first, g * Z + last)
             nc.vector.quantize_mx(out=recon_codes[:, cols].bitcast(E4M3X4), scales=recon_sbytes[:, cols], in_=grouped[:])
 
-        def interleave_commands(g, half, move, name=None, first=0, count=COLS):
+        def interleave_commands(g, half, first, last, move=scalar_move, name=None):
             if name:
                 com_grouped[g, half] = once.tile([P, J * COLS], BF16, name=name, align_bytes=64)
-            interleave(
-                move,
-                com_grouped[g, half][:, J * first : J * (first + count)],
-                com_raw[g, half][:, :, first : first + count],
-            )
+            interleave(move, com_grouped[g, half][:, J * first : J * last], com_raw[g, half][:, :, first:last])
 
         def quantize_commands(g, half, first=0, count=COLS):
             c0 = g * A + half * COLS + first
@@ -176,6 +169,10 @@ def tile_modal_response_estimate_s7_kernel(
             widened[unit, half, row] = wide
             nc.scalar.copy(out=wide[:], in_=byte_rows[unit, half, row].bitcast(E4M3))
 
+        def casts(unit, half):
+            widen(unit, half, 1)
+            widen(unit, half, 0)
+
         def first_turn(b, row):
             wide = work.tile([P, 512], BF16, name="wide", bufs=WIDE_BUFS)
             nc.scalar.copy(out=wide[:], in_=byte_rows["first", b, row].bitcast(E4M3))
@@ -185,13 +182,6 @@ def tile_modal_response_estimate_s7_kernel(
             for w in range(2):
                 nc.tensor.transpose(bank[:, w, :], words[:, w:256:2], ident[:])
 
-        def sort_words(unit, half):
-            ordered = work.tile([P, 2, 2, P], F32, name="ordered", bufs=2)
-            nc.scalar.copy(
-                out=ordered[:], in_=widened[unit, half, 1][:].bitcast(F32).rearrange("p (b m w) -> p b w m", b=2, w=2)
-            )
-            sorted_words[unit, half] = ordered
-
         def turn_slopes(unit, g, slot=None):
             half, b = divmod(g, 2)
             bank = psum.tile([P, 2, UNIT], F32, name="turn%d" % (g if slot is None else slot))
@@ -199,11 +189,7 @@ def tile_modal_response_estimate_s7_kernel(
             for row in range(2):
                 words = widened[unit, half, row][:].bitcast(F32)
                 for w in range(2):
-                    if row == 1 and (unit, half) in sorted_words:
-                        source = sorted_words[unit, half][:, b, w, :]
-                    else:
-                        source = words[:, 256 * b + w : 256 * (b + 1) : 2]
-                    nc.tensor.transpose(bank[:, w, row * P : (row + 1) * P], source, ident[:])
+                    nc.tensor.transpose(bank[:, w, row * P : (row + 1) * P], words[:, 256 * b + w : 256 * (b + 1) : 2], ident[:])
 
         def scale_slopes(unit, g):
             half, b = divmod(g, 2)
@@ -225,22 +211,20 @@ def tile_modal_response_estimate_s7_kernel(
                     op=MULT,
                 )
 
-        def scale_on_scalar(unit, g):
-            half, b = divmod(g, 2)
+        def scale_on_scalar(unit):
             slope_planes[unit] = work.tile([P, J, UNIT], BF16, name="slope_planes", bufs=1)
             for t in range(J):
                 w, e = divmod(t, 2)
                 nc.scalar.activation(
                     out=slope_planes[unit][:, t, :],
-                    in_=turned[unit, g][:, w, :].bitcast(BF16)[:, e : 2 * UNIT : 2],
+                    in_=turned[unit, 0][:, w, :].bitcast(BF16)[:, e : 2 * UNIT : 2],
                     func=COPY,
-                    scale=scale[half][:, b, t : t + 1],
+                    scale=scale[0][:, 0, t : t + 1],
                 )
 
-        def group_on_scalar(unit, g):
-            half, b = divmod(g, 2)
-            slopes_grouped[unit, half] = once.tile([P, 2 * UNIT * J], BF16, name="held%d" % unit, align_bytes=64)
-            interleave(scalar_move, slopes_grouped[unit, half][:, b * UNIT * J : (b + 1) * UNIT * J], slope_planes[unit][:])
+        def group_on_scalar(unit):
+            slopes_grouped[unit, 0] = once.tile([P, 2 * UNIT * J], BF16, name="held%d" % unit, align_bytes=64)
+            interleave(scalar_move, slopes_grouped[unit, 0][:, 0 : UNIT * J], slope_planes[unit][:])
 
         def quantize_slopes(unit, first, count):
             if first == 0:
@@ -258,7 +242,7 @@ def tile_modal_response_estimate_s7_kernel(
             )
 
         def stage1(unit, pair, first, last, bank_name=None):
-            if first == 0 and last > 0 and (unit, pair) not in acc:
+            if first == 0:
                 acc[unit, pair] = psum.tile([P, 2, UNIT], F32, name=bank_name or "acc%d" % pair)
             codes, sbytes = slope_codes[unit]
             for n in range(first, last):
@@ -288,33 +272,30 @@ def tile_modal_response_estimate_s7_kernel(
                     scale=gain_cols[:, mb : mb + 1],
                 )
 
-        def weigh(unit, engine, first=0, count=MODE_BLOCKS, name=None):
+        def weigh(unit, first=0, count=MODE_BLOCKS):
             g, pair = divmod(unit, 2)
-            if name:
-                words = once.tile([P, count * UNIT], BF16, name=name, align_bytes=64)
-            else:
-                words = work.tile([P, count * UNIT], BF16, name="h_words", bufs=HW_BUFS)
+            words = work.tile([P, count * UNIT], BF16, name="h_words", bufs=3)
             for i in range(count):
                 h_words[unit, first + i] = words[:].bitcast(F32)[:, i * P : (i + 1) * P]
             factors = weight[g][:].rearrange("p (r t) -> p r t", t=J)[:, :, 2 * pair : 2 * pair + 2]
-            engine.tensor_tensor(
+            nc.gpsimd.tensor_tensor(
                 out=words[:].rearrange("p (m r e) -> p m r e", m=count, e=2),
                 in0=h_raw[unit][:, first * UNIT : (first + count) * UNIT].rearrange("p (m r e) -> p m r e", m=count, e=2),
                 in1=factors.unsqueeze(1).to_broadcast([P, count, P, 2]),
                 op=MULT,
             )
 
-        def turn_h(unit, half, bank_name=None):
+        def turn_h(unit, half):
             g, pair = divmod(unit, 2)
             if pair == 0:
-                h_turned[g, half] = psum.tile([P, 2, PIECE], F32, name=bank_name or "h%d" % half)
+                h_turned[g, half] = psum.tile([P, 2, PIECE], F32, name="h%d" % half)
             for i in range(2):
                 nc.tensor.transpose(h_turned[g, half][:, pair, i * P : (i + 1) * P], h_words[unit, 2 * half + i], ident[:])
 
-        def take_h(g, half, move=scalar_move):
+        def take_h(g, half):
             if half == 0:
                 h_grouped[g] = once.tile([P, J * Z], BF16, name="h_grouped%d" % g, align_bytes=64)
-            move(
+            scalar_move(
                 h_grouped[g][:, half * J * PIECE : (half + 1) * J * PIECE].bitcast(F32).rearrange("p (z w) -> p z w", w=2),
                 h_turned[g, half][:].rearrange("p w z -> p z w"),
             )
@@ -338,11 +319,12 @@ def tile_modal_response_estimate_s7_kernel(
 
         def turn_block(unit, mb):
             if unit % 2 == 0:
-                h_turned["block", mb] = psum.tile([P, J, P], F32, name="h%d" % mb)
+                h_turned["block", mb] = psum.tile([P, J, P], F32, name=BLOCK_BANKS[mb])
             for row in range(2):
                 nc.tensor.transpose(h_turned["block", mb][:, 2 * (unit % 2) + row, :], raw_rows(unit, mb, row), ident[:])
 
-        def weigh_block(g, mb):
+        def weigh_block(mb):
+            g = PASSES - 1
             if mb == 0:
                 h_grouped[g] = once.tile([P, J * Z], BF16, name="h_grouped%d" % g, align_bytes=64)
             nc.vector.tensor_tensor(
@@ -352,8 +334,8 @@ def tile_modal_response_estimate_s7_kernel(
                 op=MULT,
             )
 
-        def interleave_last_half(g, move):
-            interleave(move, h_grouped[g][:, J * PIECE :], last_planes[:])
+        def interleave_last_half():
+            interleave(scalar_move, h_grouped[PASSES - 1][:, J * PIECE :], last_planes[:])
 
         def quantize_h(g, first=0, count=MODE_BLOCKS):
             cols = slice(g * Z + first * P, g * Z + (first + count) * P)
@@ -363,7 +345,7 @@ def tile_modal_response_estimate_s7_kernel(
                 in_=h_grouped[g][:, first * J * P : (first + count) * J * P],
             )
 
-        def stage2(mb, g, first=0, count=COLS, last=PASSES - 1):
+        def stage2(mb, g, first=0, count=COLS):
             if g == 0 and first == 0:
                 resp[mb] = psum.tile([P, COLS], F32, name=RESP_BANKS[mb])
             z0 = g * Z + mb * P
@@ -375,7 +357,7 @@ def tile_modal_response_estimate_s7_kernel(
                 rhs=com_codes[:, a0 : a0 + count].bitcast(E4M3X4),
                 rhs_scale=com_sbytes[:, a0 : a0 + count],
                 start=(g == 0 and first == 0),
-                stop=(g == last and first + count == COLS),
+                stop=(g == PASSES - 1 and first + count == COLS),
             )
 
         def quarter(blocks, part, groups, bank_name=None):
@@ -407,10 +389,6 @@ def tile_modal_response_estimate_s7_kernel(
             nc.scalar.copy(out=result[:], in_=resp[mb][:])
             nc.sync.dma_start(out=out[mb * P : (mb + 1) * P, 0:COLS], in_=result[:])
 
-        def casts(unit, half):
-            widen(unit, half, 1)
-            widen(unit, half, 0)
-
         nc.vector.memset(ident[:], 0.0)
         nc.vector.memset(gain_rows32[:], 0.0)
         make_identity(nc, ident[:], nomemset=True)
@@ -424,9 +402,9 @@ def tile_modal_response_estimate_s7_kernel(
         load_first_bytes(1, 1)
         load_bytes(1, (0,))
         load_recon(0, PIECE, Z)
+        load_bytes(0, (1,))
         load_recon(1, 0, Z)
         nc.sync.dma_start(out=scale[1][:], in_=scale_view[:, 2:4, :])
-        load_bytes(0, (1,))
         nc.sync.dma_start(out=gain_rows[0:MODE_BLOCKS, :], in_=gain.rearrange("(c p) -> c p", p=P))
         load_bytes(1, (1,))
         load_recon(2, 0, Z)
@@ -445,17 +423,17 @@ def tile_modal_response_estimate_s7_kernel(
                 first_turn(b, row)
         share_recon(0, 0, 0, P, vector_move, "early0")
         share_recon(0, 0, P, PIECE, scalar_move)
-        share_recon(0, 1, 0, FIRST_GPSIMD, gpsimd_move, "early1")
+        share_recon(0, 1, 0, NARROW, gpsimd_move, "early1")
         scale_slopes(0, 0)
         scale_slopes(0, 1)
         widen(1, 0, 0)
         widen(1, 0, 1)
         turn_slopes(1, 0, 2)
         turn_slopes(1, 1, 3)
-        share_recon(0, 1, FIRST_GPSIMD, PIECE, scalar_move)
-        interleave_recon(1, SHORT, Z, scalar_move, "early2")
+        share_recon(0, 1, NARROW, PIECE, scalar_move)
         widen(0, 1, 0)
         widen(0, 1, 1)
+        interleave_recon(1, SHORT, Z, scalar_move, "early2")
         nc.scalar.copy(out=gain_rows32[:], in_=gain_rows[:])
         quantize_slopes(0, 0, 1)
         quantize_recon(0, 0)
@@ -485,8 +463,6 @@ def tile_modal_response_estimate_s7_kernel(
         casts(2, 1)
         casts(3, 0)
         casts(3, 1)
-        casts(4, 0)
-        casts(4, 1)
         turn_slopes(1, 2)
         stage1(1, 0, 0, 4, "h0")
         turn_slopes(1, 3)
@@ -499,6 +475,9 @@ def tile_modal_response_estimate_s7_kernel(
         scale_slopes(1, 2)
         scale_slopes(1, 3)
         turn_slopes(2, 0)
+        scale_on_scalar(2)
+        widen(4, 0, 1)
+        group_on_scalar(2)
         stage1(1, 1, 0, 4, "h1")
         turn_slopes(2, 1)
         turn_slopes(2, 2)
@@ -511,118 +490,143 @@ def tile_modal_response_estimate_s7_kernel(
         load_commands(0, 1)
         load_weight(1)
 
-
         def window(unit, share):
-            g, half = ((0, 0), (2, 0), (0, 1), (3, 0), (2, 1), (1, 1))[unit - 2]
-            interleave_commands(g, half, gpsimd_move, "held0" if unit == 2 else "held%d" % (unit - 1), 0, share)
+            g, half = WINDOW_HALVES[unit - 2]
+            interleave_commands(g, half, 0, share, gpsimd_move, "held0" if unit == 2 else "held%d" % (unit - 1))
             if unit == 2:
-                weigh(0, nc.gpsimd, 0, 2)
+                weigh(0, 0, 2)
             else:
                 if unit == 3:
-                    weigh(0, nc.gpsimd, 2, 2)
-                weigh(unit - 2, nc.gpsimd)
-            for g in range(unit in SCALAR_UNITS, PASSES):
+                    weigh(0, 2, 2)
+                weigh(unit - 2)
+            for g in range(unit in SCALAR_UNITS, PASSES if unit < LAST else PASSES - 1):
                 scale_slopes(unit, g)
 
-        def two_runs(unit, a, b, c, ahead=0):
+        def ahead(unit):
+            return 0 if unit in SCALAR_UNITS else AHEAD
+
+        def first_run(unit):
             stage1(unit - 1, 0, 0, 8)
-            stage1(unit - 1, 1, 0, ahead)
+            if ahead(unit):
+                stage1(unit - 1, 1, 0, ahead(unit))
             turn_h(unit - 3, 0)
             turn_slopes(unit + 1, 0)
             turn_slopes(unit + 1, 1)
-            a()
-            limit(unit - 1, 0)
-            stage1(unit - 1, 1, ahead, 8)
+
+        def second_run(unit):
+            stage1(unit - 1, 1, ahead(unit), 8)
             turn_h(unit - 3, 1)
             turn_slopes(unit + 1, 2)
             turn_slopes(unit + 1, 3)
-            b()
-            limit(unit - 1, 1)
-            c()
+
+        def close(unit):
             quantize_slopes(unit, 0, 2)
             quantize_slopes(unit, 2, 2)
 
-        def il(g, half, first, last, name=None):
-            interleave_commands(g, half, scalar_move, name, first, last - first)
-
-        def nothing():
-            return None
-
-        il(1, 0, 0, 192, "held1")
         stage1(0, 0, 6, 8)
         stage1(0, 1, 6, 8)
         limit(0, 0)
+        widen(4, 0, 0)
         limit(0, 1)
         turn_slopes(2, 3)
-        window(2, COLS)
+        window(2, BROAD)
         turn_slopes(3, 0)
         stage1(1, 0, 4, 8)
-        casts(5, 0)
+        casts(4, 1)
         limit(1, 0)
         turn_slopes(3, 1)
-        turn_slopes(3, 2)
         stage1(1, 1, 4, 8)
-        casts(5, 1)
         limit(1, 1)
+        interleave_commands(0, 0, BROAD, COLS)
+        turn_slopes(3, 2)
         turn_slopes(3, 3)
-        quantize_slopes(2, 0, 2)
-        quantize_slopes(2, 2, 2)
+        close(2)
         load_bytes(7, (0, 1))
         load_commands(3, 0)
         load_weight(2)
         nc.sync.dma_start(out=last_weight[:], in_=frame_weight.rearrange("(g p t) -> g p t", p=P, t=J)[PASSES - 1])
         load_commands(2, 1)
+        load_commands(1, 1)
 
         window(3, REST)
-        two_runs(3, lambda: (il(1, 0, 192, COLS), load_commands(1, 1)), lambda: (scale_on_scalar(4, 0), casts(6, 0)), lambda: (il(2, 0, REST, 192), group_on_scalar(4, 0)), AHEAD)
-        window(4, NARROW)
-        two_runs(4, lambda: casts(6, 1), lambda: (casts(7, 0), take_h(0, 0)), lambda: take_h(0, 1))
-        window(5, BROAD)
-        two_runs(5, lambda: casts(7, 1), lambda: scale_on_scalar(6, 0), lambda: group_on_scalar(6, 0))
-        window(6, NARROW)
-        two_runs(
-            6,
-            lambda: (il(2, 0, 192, COLS), load_commands(3, 1)),
-            lambda: (take_h(1, 0), il(0, 1, NARROW, PIECE)),
-            lambda: (take_h(1, 1), nc.scalar.copy(out=last_weight32[:], in_=last_weight[:])),
-        )
+        first_run(3)
+        casts(5, 0)
+        limit(2, 0)
+        second_run(3)
+        scale_on_scalar(4)
+        limit(2, 1)
+        group_on_scalar(4)
+        casts(5, 1)
+        close(3)
 
-        weigh(LAST - 2, nc.gpsimd, 0, 2, "held6")
-        weigh(LAST - 2, nc.gpsimd, 2, 1)
-        scale_slopes(LAST, 0)
-        scale_slopes(LAST, 1)
-        quantize_h(0, 0, 2)
+        window(4, NARROW)
+        first_run(4)
+        casts(6, 0)
+        limit(3, 0)
+        second_run(4)
+        casts(6, 1)
+        limit(3, 1)
+        take_h(0, 0)
+        take_h(0, 1)
+        close(4)
+
+        window(5, BROAD)
+        first_run(5)
+        interleave_commands(1, 0, 0, LATE, scalar_move, "held1")
+        casts(LAST, 0)
+        limit(4, 0)
+        second_run(5)
+        casts(LAST, 1)
+        limit(4, 1)
+        interleave_commands(1, 0, LATE, COLS)
+        load_commands(3, 1)
+        close(5)
+
+        window(6, BROAD)
+        first_run(6)
+        interleave_commands(2, 0, REST, PIECE)
+        limit(5, 0)
+        second_run(6)
+        take_h(1, 0)
+        interleave_commands(0, 1, NARROW, PIECE)
+        limit(5, 1)
+        take_h(1, 1)
+        interleave_commands(2, 0, PIECE, COLS)
+        nc.scalar.copy(out=last_weight32[:], in_=last_weight[:])
+        close(6)
+
+        window(LAST, NARROW)
         quantize_slopes(LAST, 0, 2)
-        weigh(LAST - 2, nc.gpsimd, 3, 1, "held7")
-        interleave_commands(1, 1, gpsimd_move, "early4", 0, LATE)
-        scale_slopes(LAST, 2)
-        scale_slopes(LAST, 3)
         quantize_slopes(LAST, 2, 1)
+        interleave_commands(3, 1, 0, P, gpsimd_move, "held7")
+        scale_slopes(LAST, 3)
+        quantize_h(0, 0, 2)
         quantize_slopes(LAST, 3, 1)
         stage1(LAST - 1, 0, 0, 8)
-        il(3, 0, BROAD, COLS)
-        il(2, 1, NARROW, PIECE)
         limit(LAST - 1, 0)
-        stage1(LAST - 1, 1, 0, 8)
-        limit(LAST - 1, 1)
         turn_h(LAST - 3, 0)
+        turn_h(LAST - 3, 1)
+        stage1(LAST - 1, 1, 0, 8)
+        interleave_commands(3, 0, BROAD, COLS)
+        limit(LAST - 1, 1)
+        turn_block(LAST - 1, 0)
         turn_h(LAST - 2, 0)
+        turn_h(LAST - 2, 1)
         turn_block(LAST - 1, 1)
         take_h(2, 0)
+        take_h(2, 1)
         stage1(LAST, 0, 0, 4, "turn0")
         stage1(LAST, 1, 0, 4, "turn1")
-        turn_h(LAST - 3, 1, "acc1")
-        turn_h(LAST - 2, 1)
-        turn_half_planes(LAST - 1, "acc0")
-        turn_block(LAST - 1, 0)
-        il(0, 1, PIECE, COLS)
-        take_h(2, 1)
+        turn_half_planes(LAST - 1, "acc1")
+        interleave_commands(1, 1, NARROW, LATE)
+        interleave_commands(3, 1, P, PIECE)
         weigh_half_planes(LAST - 1)
-        stage1(LAST, 0, 4, 8)
-        stage1(LAST, 1, 4, 8)
+        for first in (4, 6):
+            stage1(LAST, 0, first, first + 2)
+            stage1(LAST, 1, first, first + 2)
         limit(LAST, 0)
         limit(LAST, 1)
-        il(3, 1, 0, PIECE, "early3")
+        interleave_commands(0, 1, PIECE, COLS)
 
         quantize_commands(0, 0, 0, PIECE)
         quantize_commands(0, 0, PIECE, PIECE)
@@ -637,18 +641,18 @@ def tile_modal_response_estimate_s7_kernel(
         turn_block(LAST, 1)
         turn_half_planes(LAST, "turn0")
         weigh_half_planes(LAST)
-        il(2, 1, PIECE, PIECE + 64)
+        interleave_commands(2, 1, BROAD, BROAD + REST)
         quantize_h(2)
         quantize_commands(2, 0)
-        weigh_block(3, 0)
-        interleave_last_half(3, scalar_move)
-        il(2, 1, PIECE + 64, COLS)
-        weigh_block(3, 1)
+        weigh_block(0)
+        interleave_last_half()
+        interleave_commands(2, 1, BROAD + REST, COLS)
+        weigh_block(1)
         quantize_commands(3, 0)
         quantize_h(3, 0, 2)
         quantize_commands(0, 1)
         quantize_h(3, 2, 2)
-        interleave_commands(1, 1, vector_move, None, LATE, COLS - LATE)
+        interleave_commands(1, 1, LATE, COLS, vector_move)
         quantize_commands(2, 1, 0, PIECE)
         quantize_commands(1, 1, 0, PIECE)
         quantize_commands(3, 1, 0, PIECE)
@@ -659,15 +663,15 @@ def tile_modal_response_estimate_s7_kernel(
             stage2(mb, 3)
             store(mb)
         quarter((0, 1), 0, (0,), "turn1")
-        quarter((2, 3), 0, (0,), "h0")
+        quarter((2, 3), 0, (0,), "acc0")
         for mb in (2, 3):
             stage2(mb, 3)
         for mb in (2, 3):
             store(mb)
-        interleave_commands(3, 1, vector_move, None, PIECE, PIECE)
+        interleave_commands(3, 1, PIECE, COLS, vector_move)
         for g in (1, 2, 3):
             quantize_commands(g, 1, PIECE, PIECE)
-        quarter((0,), 1, (0,), "h1")
+        quarter((0,), 1, (0,), "turn2")
         quarter((1,), 1, (0,), "turn0")
         quarter((0, 1), 0, (2, 1, 3))
         store_quarter((0, 1), 0, scalar_move)
@@ -677,5 +681,5 @@ def tile_modal_response_estimate_s7_kernel(
             quarter((mb,), 1, (1, 2, 3))
             store_quarter((mb,), 1, (scalar_move, vector_move)[mb])
         for mb in (2, 3):
-            quarter((mb,), 1, (0, 1, 2, 3), ("turn2", "acc1")[mb - 2])
+            quarter((mb,), 1, (0, 1, 2, 3), ("h1", "h0")[mb - 2])
             store_quarter((mb,), 1, (scalar_move, vector_move)[mb - 2])

@@ -127,7 +127,7 @@ def tile_modal_response_estimate_s7_kernel(
             recon_raw[g, (last - 1) // PIECE] = (raw, first)
 
         def load_commands(g, half):
-            raw = work.tile([P, J, COLS], BF16, name="com_raw", bufs=6)
+            raw = work.tile([P, J, COLS], BF16, name="com_raw", bufs=7)
             nc.sync.dma_start(out=raw[:], in_=commands_view[g][:, :, half * COLS : (half + 1) * COLS])
             com_raw[g, half] = raw
 
@@ -413,10 +413,11 @@ def tile_modal_response_estimate_s7_kernel(
         load_bytes(3, (0, 1))
         load_commands(0, 0)
         load_bytes(4, (0, 1))
-        load_commands(1, 0)
-        load_bytes(5, (0, 1))
         load_weight(0)
         load_commands(2, 0)
+        load_bytes(5, (0, 1))
+        load_weight(1)
+        load_commands(0, 1)
 
         for b in range(2):
             for row in range(2):
@@ -487,8 +488,8 @@ def tile_modal_response_estimate_s7_kernel(
         quantize_recon(3, 0)
         quantize_slopes(1, 2, 2)
         load_bytes(6, (0, 1))
-        load_commands(0, 1)
-        load_weight(1)
+        load_commands(3, 0)
+        load_commands(1, 0)
 
         def window(unit, share):
             g, half = WINDOW_HALVES[unit - 2]
@@ -542,11 +543,11 @@ def tile_modal_response_estimate_s7_kernel(
         turn_slopes(3, 3)
         close(2)
         load_bytes(7, (0, 1))
-        load_commands(3, 0)
-        load_weight(2)
-        nc.sync.dma_start(out=last_weight[:], in_=frame_weight.rearrange("(g p t) -> g p t", p=P, t=J)[PASSES - 1])
         load_commands(2, 1)
+        load_weight(2)
         load_commands(1, 1)
+        load_commands(3, 1)
+        nc.sync.dma_start(out=last_weight[:], in_=frame_weight.rearrange("(g p t) -> g p t", p=P, t=J)[PASSES - 1])
 
         window(3, REST)
         first_run(3)
@@ -579,7 +580,6 @@ def tile_modal_response_estimate_s7_kernel(
         casts(LAST, 1)
         limit(4, 1)
         interleave_commands(1, 0, LATE, COLS)
-        load_commands(3, 1)
         close(5)
 
         window(6, BROAD)

@@ -29,10 +29,10 @@ PIECE = COLS // 2
 WIDE_BUFS = 14
 
 SHORT = 384
-BROAD = 320
-NARROW = 96
+BROAD = 304
+NARROW = 80
 REST = 64
-LATE = 2 * NARROW
+LATE = SHORT // 2
 SCALAR_UNITS = (2, 4)
 AHEAD = 4
 
@@ -156,12 +156,21 @@ def tile_modal_response_estimate_s7_kernel(
                 com_grouped[g, half] = once.tile([P, J * COLS], BF16, name=name, align_bytes=64)
             interleave(move, com_grouped[g, half][:, J * first : J * last], com_raw[g, half][:, :, first:last])
 
+        def interleave_last_quarter(first, last, move, name=None):
+            if name:
+                com_grouped["last"] = once.tile([P, J * PIECE], BF16, name=name, align_bytes=64)
+            interleave(move, com_grouped["last"][:, J * first : J * last], com_raw[3, 1][:, :, PIECE + first : PIECE + last])
+
         def quantize_commands(g, half, first=0, count=COLS):
             c0 = g * A + half * COLS + first
+            if (g, half, first) == (3, 1, PIECE):
+                grouped = com_grouped["last"][:]
+            else:
+                grouped = com_grouped[g, half][:, J * first : J * (first + count)]
             nc.vector.quantize_mx(
                 out=com_codes[:, c0 : c0 + count].bitcast(E4M3X4),
                 scales=com_sbytes[:, c0 : c0 + count],
-                in_=com_grouped[g, half][:, J * first : J * (first + count)],
+                in_=grouped,
             )
 
         def widen(unit, half, row):
@@ -644,6 +653,7 @@ def tile_modal_response_estimate_s7_kernel(
         interleave_commands(2, 1, BROAD, BROAD + REST)
         quantize_h(2)
         quantize_commands(2, 0)
+        interleave_last_quarter(0, P, gpsimd_move, "h_grouped2")
         weigh_block(0)
         interleave_last_half()
         interleave_commands(2, 1, BROAD + REST, COLS)
@@ -651,8 +661,8 @@ def tile_modal_response_estimate_s7_kernel(
         quantize_commands(3, 0)
         quantize_h(3, 0, 2)
         quantize_commands(0, 1)
+        interleave_commands(1, 1, LATE, PIECE, vector_move)
         quantize_h(3, 2, 2)
-        interleave_commands(1, 1, LATE, COLS, vector_move)
         quantize_commands(2, 1, 0, PIECE)
         quantize_commands(1, 1, 0, PIECE)
         quantize_commands(3, 1, 0, PIECE)
@@ -666,19 +676,19 @@ def tile_modal_response_estimate_s7_kernel(
         quarter((2, 3), 0, (0,), "acc0")
         for mb in (2, 3):
             stage2(mb, 3)
-        for mb in (2, 3):
             store(mb)
-        interleave_commands(3, 1, PIECE, COLS, vector_move)
-        for g in (1, 2, 3):
-            quantize_commands(g, 1, PIECE, PIECE)
         quarter((0,), 1, (0,), "turn2")
         quarter((1,), 1, (0,), "turn0")
+        interleave_commands(1, 1, PIECE, COLS, vector_move)
+        interleave_last_quarter(P, PIECE, vector_move)
+        for g in (2, 1, 3):
+            quantize_commands(g, 1, PIECE, PIECE)
         quarter((0, 1), 0, (2, 1, 3))
         store_quarter((0, 1), 0, scalar_move)
         quarter((2, 3), 0, (2, 1, 3))
         store_quarter((2, 3), 0, vector_move)
         for mb in range(2):
-            quarter((mb,), 1, (1, 2, 3))
+            quarter((mb,), 1, (2, 1, 3))
             store_quarter((mb,), 1, (scalar_move, vector_move)[mb])
         for mb in (2, 3):
             quarter((mb,), 1, (0, 1, 2, 3), ("h1", "h0")[mb - 2])

from contextlib import ExitStack

import concourse.mybir as mybir
from concourse.masks import make_identity

F32 = mybir.dt.float32
BF16 = mybir.dt.bfloat16
U32 = mybir.dt.uint32
U8 = mybir.dt.uint8
E4M3 = mybir.dt.float8_e4m3fn
E4M3X4 = mybir.dt.float8_e4m3fn_x4
ADD = mybir.AluOpType.add
MULT = mybir.AluOpType.mult
TANH = mybir.ActivationFunctionType.Tanh
COPY = mybir.ActivationFunctionType.Copy

T, S, Z, A = 2048, 2048, 512, 1024
FLOPS = 2 * T * S * Z + 2 * T * Z * A

P = 128
J = 4
PASSES = 4
HALF = S // 2
UNIT = 2 * P
LAST = T // UNIT - 1
MODE_BLOCKS = Z // P
COLS = 512
PIECE = COLS // 2
WIDE_BUFS = 14

SHORT = 384
BROAD = 304
NARROW = 80
REST = 64
LATE = SHORT // 2
SCALAR_UNITS = (2, 4)
AHEAD = 4

WINDOW_HALVES = ((0, 0), (2, 0), (0, 1), (3, 0), (2, 1), (1, 1))
BLOCK_BANKS = ("acc0", "turn2")
RESP_BANKS = ("h0", "acc1", "h1", "turn3")


def tile_modal_response_estimate_s7_kernel(
    tc, slopes_bytes, slopes_scale, recon, gain, frame_weight, commands, out
):
    nc = tc.nc

    bytes_view = slopes_bytes.rearrange("(g p t) s -> g p t s", p=P, t=J)
    recon_view = recon.rearrange("(g p j) z -> g p j z", p=P, j=J)
    commands_view = commands.rearrange("(g p j) a -> g p j a", p=P, j=J)

    with ExitStack() as ctx:
        once = ctx.enter_context(tc.tile_pool(name="once", bufs=1))
        work = ctx.enter_context(tc.tile_pool(name="work", bufs=2))
        psum = ctx.enter_context(tc.psum_pool(name="psum", bufs=1))
        ctx.enter_context(tc.manual_schedule())

        scale = [once.tile([P, 2, J], F32, name="scale%d" % half) for half in range(2)]
        ident = once.tile([P, P], F32, name="ident")
        gain_rows = once.tile([P, P], BF16, name="gain_rows")
        gain_rows32 = once.tile([P, P], F32, name="gain_rows32")
        gain_cols = once.tile([P, MODE_BLOCKS], F32, name="gain_cols")
        weight = [once.tile([P, P * J], BF16, name="weight%d" % g) for g in range(PASSES - 1)]
        last_weight = once.tile([P, J], BF16, name="last_weight")
        last_weight32 = once.tile([P, J], F32, name="last_weight32")
        last_planes = once.tile([P, J, PIECE], BF16, name="last_planes")

        recon_codes = once.tile([P, PASSES * Z], U32, name="recon_codes", align_bytes=64)
        recon_sbytes = once.tile([P, PASSES * Z], U8, name="recon_sbytes", align_bytes=64)
        com_codes = once.tile([P, PASSES * A], U32, name="com_codes", align_bytes=64)
        com_sbytes = once.tile([P, PASSES * A], U8, name="com_sbytes", align_bytes=64)
        h_codes = once.tile([P, PASSES * Z], U32, name="h_codes", align_bytes=64)
        h_sbytes = once.tile([P, PASSES * Z], U8, name="h_sbytes", align_bytes=64)

        byte_rows = {}
        recon_raw = {}
        recon_grouped = {}
        com_raw = {}
        com_grouped = {}
        widened = {}
        turned = {}
        slopes_grouped = {}
        slope_codes = {}
        slope_planes = {}
        acc = {}
        h_raw = {}
        h_turned = {}
        h_words = {}
        h_grouped = {}
        resp = {}

        def scalar_move(out, in_):
            nc.scalar.copy(out=out, in_=in_)

        def gpsimd_move(out, in_):
            nc.gpsimd.tensor_scalar(out=out, in0=in_, scalar1=1.0, scalar2=0.0, op0=MULT, op1=ADD)

        def vector_move(out, in_):
            nc.vector.tensor_copy(out=out, in_=in_)

        def interleave(move, grouped, raw):
            move(
                grouped.rearrange("p (c i j) -> p c j i", i=4, j=J),
                raw.rearrange("p j (c i) -> p c j i", i=4),
            )

        def load_bytes(unit, halves):
            g, pair = divmod(unit, 2)
            k0 = halves[0] * HALF
            k1 = k0 + len(halves) * HALF
            row_bytes = work.tile([P, 2, k1 - k0], U8, name="row_bytes", bufs=5)
            nc.sync.dma_start(out=row_bytes[:], in_=bytes_view[g][:, 2 * pair : 2 * pair + 2, k0:k1])
            for row in range(2):
                for half in halves:
                    byte_rows[unit, half, row] = row_bytes[:, row, half * HALF - k0 : (half + 1) * HALF - k0]

        def load_first_bytes(b, row):
            row_bytes = once.tile([P, 512], U8, name="first_bytes%d_%d" % (b, row))
            nc.sync.dma_start(out=row_bytes[:], in_=bytes_view[0][:, row, 512 * b : 512 * (b + 1)])
            byte_rows["first", b, row] = row_bytes[:]

        def load_recon(g, first, last):
            raw = once.tile([P, J, last - first], BF16, name="recon_raw%d_%d" % (g, first))
            nc.sync.dma_start(out=raw[:], in_=recon_view[g][:, :, first:last])
            recon_raw[g, first // PIECE] = (raw, first)
            recon_raw[g, (last - 1) // PIECE] = (raw, first)

        def load_commands(g, half):
            raw = work.tile([P, J, COLS], BF16, name="com_raw", bufs=7)
            nc.sync.dma_start(out=raw[:], in_=commands_view[g][:, :, half * COLS : (half + 1) * COLS])
            com_raw[g, half] = raw

        def load_weight(g):
            nc.sync.dma_start(out=weight[g][:], in_=frame_weight[g * P * J : (g + 1) * P * J].partition_broadcast(P))

        def interleave_recon(g, first, last, move, name):
            raw, z0 = recon_raw[g, first // PIECE]
            grouped = once.tile([P, J * (last - first)], BF16, name=name, align_bytes=64)
            interleave(move, grouped[:], raw[:, :, first - z0 : last - z0])
            recon_grouped[g, first] = (grouped, last)

        def share_recon(g, part, first, last, move, name=None):
            raw, z0 = recon_raw[g, part]
            if name:
                recon_grouped[g, z0] = (once.tile([P, J * PIECE], BF16, name=name, align_bytes=64), z0 + PIECE)
            interleave(move, recon_grouped[g, z0][0][:, J * first : J * last], raw[:, :, first:last])

        def quantize_recon(g, first):
            grouped, last = recon_grouped[g, first]
            cols = slice(g * Z + first, g * Z + last)
            nc.vector.quantize_mx(out=recon_codes[:, cols].bitcast(E4M3X4), scales=recon_sbytes[:, cols], in_=grouped[:])

        def interleave_commands(g, half, first, last, move=scalar_move, name=None):
            if name:
                com_grouped[g, half] = once.tile([P, J * COLS], BF16, name=name, align_bytes=64)
            interleave(move, com_grouped[g, half][:, J * first : J * last], com_raw[g, half][:, :, first:last])

        def interleave_last_quarter(first, last, move, name=None):
            if name:
                com_grouped["last"] = once.tile([P, J * PIECE], BF16, name=name, align_bytes=64)
            interleave(move, com_grouped["last"][:, J * first : J * last], com_raw[3, 1][:, :, PIECE + first : PIECE + last])

        def quantize_commands(g, half, first=0, count=COLS):
            c0 = g * A + half * COLS + first
            if (g, half, first) == (3, 1, PIECE):
                grouped = com_grouped["last"][:]
            else:
                grouped = com_grouped[g, half][:, J * first : J * (first + count)]
            nc.vector.quantize_mx(
                out=com_codes[:, c0 : c0 + count].bitcast(E4M3X4),
                scales=com_sbytes[:, c0 : c0 + count],
                in_=grouped,
            )

        def widen(unit, half, row):
            wide = work.tile([P, HALF], BF16, name="wide", bufs=WIDE_BUFS)
            widened[unit, half, row] = wide
            nc.scalar.copy(out=wide[:], in_=byte_rows[unit, half, row].bitcast(E4M3))

        def casts(unit, half):
            widen(unit, half, 1)
            widen(unit, half, 0)

        def first_turn(b, row):
            wide = work.tile([P, 512], BF16, name="wide", bufs=WIDE_BUFS)
            nc.scalar.copy(out=wide[:], in_=byte_rows["first", b, row].bitcast(E4M3))
            bank = psum.tile([P, 2, P], F32, name=("turn%d", "h%d")[row] % b)
            turned["first", b, row] = bank
            words = wide[:].bitcast(F32)
            for w in range(2):
                nc.tensor.transpose(bank[:, w, :], words[:, w:256:2], ident[:])

        def turn_slopes(unit, g, slot=None):
            half, b = divmod(g, 2)
            bank = psum.tile([P, 2, UNIT], F32, name="turn%d" % (g if slot is None else slot))
            turned[unit, g] = bank
            for row in range(2):
                words = widened[unit, half, row][:].bitcast(F32)
                for w in range(2):
                    nc.tensor.transpose(bank[:, w, row * P : (row + 1) * P], words[:, 256 * b + w : 256 * (b + 1) : 2], ident[:])

        def scale_slopes(unit, g):
            half, b = divmod(g, 2)
            if half == 0 and (unit, half) not in slopes_grouped:
                slopes_grouped[unit, half] = once.tile([P, 2 * UNIT * J], BF16, name="held%d" % unit, align_bytes=64)
            if b == 0 and half == 1:
                slopes_grouped[unit, half] = work.tile([P, 2 * UNIT * J], BF16, name="second_half", bufs=2, align_bytes=64)
            grouped = slopes_grouped[unit, half][:, b * UNIT * J : (b + 1) * UNIT * J]
            if unit == 0 and half == 0:
                parts = [(turned["first", b, row], grouped[:, row * P * J : (row + 1) * P * J], P) for row in range(2)]
            else:
                parts = [(turned[unit, g], grouped, UNIT)]
            for bank, target, frames in parts:
                values = bank[:].rearrange("p w r -> p (w r)").bitcast(BF16)
                nc.vector.tensor_tensor(
                    out=target.rearrange("p (r w e) -> p r w e", w=2, e=2),
                    in0=values.rearrange("p (w r e) -> p r w e", w=2, e=2),
                    in1=scale[half][:, b, :].rearrange("p (w e) -> p w e", e=2).unsqueeze(1).to_broadcast([P, frames, 2, 2]),
                    op=MULT,
                )

        def scale_on_scalar(unit):
            slope_planes[unit] = work.tile([P, J, UNIT], BF16, name="slope_planes", bufs=1)
            for t in range(J):
                w, e = divmod(t, 2)
                nc.scalar.activation(
                    out=slope_planes[unit][:, t, :],
                    in_=turned[unit, 0][:, w, :].bitcast(BF16)[:, e : 2 * UNIT : 2],
                    func=COPY,
                    scale=scale[0][:, 0, t : t + 1],
                )

        def group_on_scalar(unit):
            slopes_grouped[unit, 0] = once.tile([P, 2 * UNIT * J], BF16, name="held%d" % unit, align_bytes=64)
            interleave(scalar_move, slopes_grouped[unit, 0][:, 0 : UNIT * J], slope_planes[unit][:])

        def quantize_slopes(unit, first, count):
            if first == 0:
                slope_codes[unit] = (
                    work.tile([P, PASSES * UNIT], U32, name="slope_codes", bufs=3, align_bytes=64),
                    work.tile([P, PASSES * UNIT], U8, name="slope_sbytes", bufs=3, align_bytes=64),
                )
            codes, sbytes = slope_codes[unit]
            half, b = divmod(first, 2)
            cols = slice(first * UNIT, (first + count) * UNIT)
            nc.vector.quantize_mx(
                out=codes[:, cols].bitcast(E4M3X4),
                scales=sbytes[:, cols],
                in_=slopes_grouped[unit, half][:, b * UNIT * J : (b + count) * UNIT * J],
            )

        def stage1(unit, pair, first, last, bank_name=None):
            if first == 0:
                acc[unit, pair] = psum.tile([P, 2, UNIT], F32, name=bank_name or "acc%d" % pair)
            codes, sbytes = slope_codes[unit]
            for n in range(first, last):
                g, i = divmod(n, 2)
                z0 = g * Z + (2 * pair + i) * P
                r0 = g * UNIT
                nc.tensor.matmul_mx(
                    out=acc[unit, pair][:, i, :],
                    lhsT=recon_codes[:, z0 : z0 + P].bitcast(E4M3X4),
                    lhsT_scale=recon_sbytes[:, z0 : z0 + P],
                    rhs=codes[:, r0 : r0 + UNIT].bitcast(E4M3X4),
                    rhs_scale=sbytes[:, r0 : r0 + UNIT],
                    start=(n == 0),
                    stop=(n == 2 * PASSES - 1),
                )

        def limit(unit, pair):
            if pair == 0:
                h_raw[unit] = work.tile([P, MODE_BLOCKS * UNIT], F32, name="h_raw", bufs=3)
            for i in range(2):
                mb = 2 * pair + i
                order = "p (e r) -> p r e" if unit < LAST - 1 else "p (r e) -> p r e"
                nc.scalar.activation(
                    out=h_raw[unit][:, mb * UNIT : (mb + 1) * UNIT].rearrange("p (r e) -> p r e", e=2),
                    in_=acc[unit, pair][:, i, :].rearrange(order, e=2),
                    func=TANH,
                    scale=gain_cols[:, mb : mb + 1],
                )

        def weigh(unit, first=0, count=MODE_BLOCKS):
            g, pair = divmod(unit, 2)
            words = work.tile([P, count * UNIT], BF16, name="h_words", bufs=3)
            for i in range(count):
                h_words[unit, first + i] = words[:].bitcast(F32)[:, i * P : (i + 1) * P]
            factors = weight[g][:].rearrange("p (r t) -> p r t", t=J)[:, :, 2 * pair : 2 * pair + 2]
            nc.gpsimd.tensor_tensor(
                out=words[:].rearrange("p (m r e) -> p m r e", m=count, e=2),
                in0=h_raw[unit][:, first * UNIT : (first + count) * UNIT].rearrange("p (m r e) -> p m r e", m=count, e=2),
                in1=factors.unsqueeze(1).to_broadcast([P, count, P, 2]),
                op=MULT,
            )

        def turn_h(unit, half):
            g, pair = divmod(unit, 2)
            if pair == 0:
                h_turned[g, half] = psum.tile([P, 2, PIECE], F32, name="h%d" % half)
            for i in range(2):
                nc.tensor.transpose(h_turned[g, half][:, pair, i * P : (i + 1) * P], h_words[unit, 2 * half + i], ident[:])

        def take_h(g, half):
            if half == 0:
                h_grouped[g] = once.tile([P, J * Z], BF16, name="h_grouped%d" % g, align_bytes=64)
            scalar_move(
                h_grouped[g][:, half * J * PIECE : (half + 1) * J * PIECE].bitcast(F32).rearrange("p (z w) -> p z w", w=2),
                h_turned[g, half][:].rearrange("p w z -> p z w"),
            )

        def raw_rows(unit, mb, row):
            return h_raw[unit][:, mb * UNIT + row * P : mb * UNIT + (row + 1) * P]

        def turn_half_planes(unit, bank_name):
            bank = psum.tile([P, 2, PIECE], F32, name=bank_name)
            for row in range(2):
                for i in range(2):
                    nc.tensor.transpose(bank[:, row, i * P : (i + 1) * P], raw_rows(unit, 2 + i, row), ident[:])
            h_turned["half", unit] = bank

        def weigh_half_planes(unit):
            for row in range(2):
                t = 2 * (unit % 2) + row
                nc.scalar.activation(
                    out=last_planes[:, t, :], in_=h_turned["half", unit][:, row, :], func=COPY, scale=last_weight32[:, t : t + 1]
                )

        def turn_block(unit, mb):
            if unit % 2 == 0:
                h_turned["block", mb] = psum.tile([P, J, P], F32, name=BLOCK_BANKS[mb])
            for row in range(2):
                nc.tensor.transpose(h_turned["block", mb][:, 2 * (unit % 2) + row, :], raw_rows(unit, mb, row), ident[:])

        def weigh_block(mb):
            g = PASSES - 1
            if mb == 0:
                h_grouped[g] = once.tile([P, J * Z], BF16, name="h_grouped%d" % g, align_bytes=64)
            nc.vector.tensor_tensor(
                out=h_grouped[g][:, mb * J * P : (mb + 1) * J * P].rearrange("p (z t) -> p z t", t=J),
                in0=h_turned["block", mb][:].rearrange("p t z -> p z t"),
                in1=last_weight[:].unsqueeze(1).to_broadcast([P, P, J]),
                op=MULT,
            )

        def interleave_last_half():
            interleave(scalar_move, h_grouped[PASSES - 1][:, J * PIECE :], last_planes[:])

        def quantize_h(g, first=0, count=MODE_BLOCKS):
            cols = slice(g * Z + first * P, g * Z + (first + count) * P)
            nc.vector.quantize_mx(
                out=h_codes[:, cols].bitcast(E4M3X4),
                scales=h_sbytes[:, cols],
                in_=h_grouped[g][:, first * J * P : (first + count) * J * P],
            )

        def stage2(mb, g, first=0, count=COLS):
            if g == 0 and first == 0:
                resp[mb] = psum.tile([P, COLS], F32, name=RESP_BANKS[mb])
            z0 = g * Z + mb * P
            a0 = g * A + first
            nc.tensor.matmul_mx(
                out=resp[mb][:, first : first + count],
                lhsT=h_codes[:, z0 : z0 + P].bitcast(E4M3X4),
                lhsT_scale=h_sbytes[:, z0 : z0 + P],
                rhs=com_codes[:, a0 : a0 + count].bitcast(E4M3X4),
                rhs_scale=com_sbytes[:, a0 : a0 + count],
                start=(g == 0 and first == 0),
                stop=(g == PASSES - 1 and first + count == COLS),
            )

        def quarter(blocks, part, groups, bank_name=None):
            if bank_name:
                resp[blocks, part] = psum.tile([P, len(blocks), PIECE], F32, name=bank_name)
            for g in groups:
                a0 = g * A + COLS + part * PIECE
                for i, mb in enumerate(blocks):
                    z0 = g * Z + mb * P
                    nc.tensor.matmul_mx(
                        out=resp[blocks, part][:, i, :],
                        lhsT=h_codes[:, z0 : z0 + P].bitcast(E4M3X4),
                        lhsT_scale=h_sbytes[:, z0 : z0 + P],
                        rhs=com_codes[:, a0 : a0 + PIECE].bitcast(E4M3X4),
                        rhs_scale=com_sbytes[:, a0 : a0 + PIECE],
                        start=(g == 0 and i == 0),
                        stop=(g == PASSES - 1 and i == len(blocks) - 1),
                    )

        def store_quarter(blocks, part, move):
            result = work.tile([P, len(blocks), PIECE], F32, name="wide", bufs=WIDE_BUFS)
            move(result[:], resp[blocks, part][:])
            a0 = COLS + part * PIECE
            rows = out.rearrange("(m p) a -> p m a", p=P)
            nc.sync.dma_start(out=rows[:, blocks[0] : blocks[-1] + 1, a0 : a0 + PIECE], in_=result[:])

        def store(mb):
            result = work.tile([P, COLS], F32, name="wide", bufs=WIDE_BUFS)
            nc.scalar.copy(out=result[:], in_=resp[mb][:])
            nc.sync.dma_start(out=out[mb * P : (mb + 1) * P, 0:COLS], in_=result[:])

        nc.vector.memset(ident[:], 0.0)
        nc.vector.memset(gain_rows32[:], 0.0)
        make_identity(nc, ident[:], nomemset=True)
        scale_view = slopes_scale.rearrange("o (g p j) -> p (o g) j", p=P, j=J)
        nc.sync.dma_start(out=scale[0][:], in_=scale_view[:, 0:2, :])
        nc.scalar.activation(out=gain_rows[:], in_=gain_rows32[:], func=COPY)
        load_first_bytes(0, 0)
        load_first_bytes(0, 1)
        load_recon(0, 0, PIECE)
        load_first_bytes(1, 0)
        load_first_bytes(1, 1)
        load_bytes(1, (0,))
        load_recon(0, PIECE, Z)
        load_bytes(0, (1,))
        load_recon(1, 0, Z)
        nc.sync.dma_start(out=scale[1][:], in_=scale_view[:, 2:4, :])
        nc.sync.dma_start(out=gain_rows[0:MODE_BLOCKS, :], in_=gain.rearrange("(c p) -> c p", p=P))
        load_bytes(1, (1,))
        load_recon(2, 0, Z)
        load_bytes(2, (0, 1))
        load_recon(3, 0, Z)
        load_bytes(3, (0, 1))
        load_commands(0, 0)
        load_bytes(4, (0, 1))
        load_weight(0)
        load_commands(2, 0)
        load_bytes(5, (0, 1))
        load_weight(1)
        load_commands(0, 1)

        for b in range(2):
            for row in range(2):
                first_turn(b, row)
        share_recon(0, 0, 0, P, vector_move, "early0")
        share_recon(0, 0, P, PIECE, scalar_move)
        share_recon(0, 1, 0, NARROW, gpsimd_move, "early1")
        scale_slopes(0, 0)
        scale_slopes(0, 1)
        widen(1, 0, 0)
        widen(1, 0, 1)
        turn_slopes(1, 0, 2)
        turn_slopes(1, 1, 3)
        share_recon(0, 1, NARROW, PIECE, scalar_move)
        widen(0, 1, 0)
        widen(0, 1, 1)
        interleave_recon(1, SHORT, Z, scalar_move, "early2")
        nc.scalar.copy(out=gain_rows32[:], in_=gain_rows[:])
        quantize_slopes(0, 0, 1)
        quantize_recon(0, 0)
        quantize_slopes(0, 1, 1)
        quantize_recon(0, PIECE)
        interleave_recon(1, 0, SHORT, gpsimd_move, "held0")
        turn_slopes(0, 2, 0)
        turn_slopes(0, 3, 1)
        gain_bank = psum.tile([P, P], F32, name="h1")
        nc.tensor.transpose(gain_bank[:], gain_rows32[:], ident[:])
        scale_slopes(1, 0)
        scale_slopes(1, 1)
        widen(1, 1, 0)
        widen(1, 1, 1)
        interleave_recon(2, SHORT, Z, scalar_move, "early0")
        quantize_recon(1, SHORT)
        quantize_recon(1, 0)
        quantize_slopes(1, 0, 2)

        interleave_recon(2, 0, SHORT, gpsimd_move, "held0")
        for first in (0, 2):
            stage1(0, 0, first, first + 2)
            stage1(0, 1, first, first + 2)
        casts(2, 0)
        nc.scalar.copy(out=gain_cols[:], in_=gain_bank[:, 0:MODE_BLOCKS])
        interleave_recon(3, SHORT, Z, scalar_move, "early1")
        casts(2, 1)
        casts(3, 0)
        casts(3, 1)
        turn_slopes(1, 2)
        stage1(1, 0, 0, 4, "h0")
        turn_slopes(1, 3)
        scale_slopes(0, 2)
        scale_slopes(0, 3)
        quantize_recon(2, SHORT)
        quantize_recon(2, 0)
        quantize_slopes(0, 2, 2)
        interleave_recon(3, 0, SHORT, gpsimd_move, "held0")
        scale_slopes(1, 2)
        scale_slopes(1, 3)
        turn_slopes(2, 0)
        scale_on_scalar(2)
        widen(4, 0, 1)
        group_on_scalar(2)
        stage1(1, 1, 0, 4, "h1")
        turn_slopes(2, 1)
        turn_slopes(2, 2)
        stage1(0, 0, 4, 6)
        stage1(0, 1, 4, 6)
        quantize_recon(3, SHORT)
        quantize_recon(3, 0)
        quantize_slopes(1, 2, 2)
        load_bytes(6, (0, 1))
        load_commands(3, 0)
        load_commands(1, 0)

        def window(unit, share):
            g, half = WINDOW_HALVES[unit - 2]
            interleave_commands(g, half, 0, share, gpsimd_move, "held0" if unit == 2 else "held%d" % (unit - 1))
            if unit == 2:
                weigh(0, 0, 2)
            else:
                if unit == 3:
                    weigh(0, 2, 2)
                weigh(unit - 2)
            for g in range(unit in SCALAR_UNITS, PASSES if unit < LAST else PASSES - 1):
                scale_slopes(unit, g)

        def ahead(unit):
            return 0 if unit in SCALAR_UNITS else AHEAD

        def first_run(unit):
            stage1(unit - 1, 0, 0, 8)
            if ahead(unit):
                stage1(unit - 1, 1, 0, ahead(unit))
            turn_h(unit - 3, 0)
            turn_slopes(unit + 1, 0)
            turn_slopes(unit + 1, 1)

        def second_run(unit):
            stage1(unit - 1, 1, ahead(unit), 8)
            turn_h(unit - 3, 1)
            turn_slopes(unit + 1, 2)
            turn_slopes(unit + 1, 3)

        def close(unit):
            quantize_slopes(unit, 0, 2)
            quantize_slopes(unit, 2, 2)

        stage1(0, 0, 6, 8)
        stage1(0, 1, 6, 8)
        limit(0, 0)
        widen(4, 0, 0)
        limit(0, 1)
        turn_slopes(2, 3)
        window(2, BROAD)
        turn_slopes(3, 0)
        stage1(1, 0, 4, 8)
        casts(4, 1)
        limit(1, 0)
        turn_slopes(3, 1)
        stage1(1, 1, 4, 8)
        limit(1, 1)
        interleave_commands(0, 0, BROAD, COLS)
        turn_slopes(3, 2)
        turn_slopes(3, 3)
        close(2)
        load_bytes(7, (0, 1))
        load_commands(2, 1)
        load_weight(2)
        load_commands(1, 1)
        load_commands(3, 1)
        nc.sync.dma_start(out=last_weight[:], in_=frame_weight.rearrange("(g p t) -> g p t", p=P, t=J)[PASSES - 1])

        window(3, REST)
        first_run(3)
        casts(5, 0)
        limit(2, 0)
        second_run(3)
        scale_on_scalar(4)
        limit(2, 1)
        group_on_scalar(4)
        casts(5, 1)
        close(3)

        window(4, NARROW)
        first_run(4)
        casts(6, 0)
        limit(3, 0)
        second_run(4)
        casts(6, 1)
        limit(3, 1)
        take_h(0, 0)
        take_h(0, 1)
        close(4)

        window(5, BROAD)
        first_run(5)
        interleave_commands(1, 0, 0, LATE, scalar_move, "held1")
        casts(LAST, 0)
        limit(4, 0)
        second_run(5)
        casts(LAST, 1)
        limit(4, 1)
        interleave_commands(1, 0, LATE, COLS)
        close(5)

        window(6, BROAD)
        first_run(6)
        interleave_commands(2, 0, REST, PIECE)
        limit(5, 0)
        second_run(6)
        take_h(1, 0)
        interleave_commands(0, 1, NARROW, PIECE)
        limit(5, 1)
        take_h(1, 1)
        interleave_commands(2, 0, PIECE, COLS)
        nc.scalar.copy(out=last_weight32[:], in_=last_weight[:])
        close(6)

        window(LAST, NARROW)
        quantize_slopes(LAST, 0, 2)
        quantize_slopes(LAST, 2, 1)
        interleave_commands(3, 1, 0, P, gpsimd_move, "held7")
        scale_slopes(LAST, 3)
        quantize_h(0, 0, 2)
        quantize_slopes(LAST, 3, 1)
        stage1(LAST - 1, 0, 0, 8)
        limit(LAST - 1, 0)
        turn_h(LAST - 3, 0)
        turn_h(LAST - 3, 1)
        stage1(LAST - 1, 1, 0, 8)
        interleave_commands(3, 0, BROAD, COLS)
        limit(LAST - 1, 1)
        turn_block(LAST - 1, 0)
        turn_h(LAST - 2, 0)
        turn_h(LAST - 2, 1)
        turn_block(LAST - 1, 1)
        take_h(2, 0)
        take_h(2, 1)
        stage1(LAST, 0, 0, 4, "turn0")
        stage1(LAST, 1, 0, 4, "turn1")
        turn_half_planes(LAST - 1, "acc1")
        interleave_commands(1, 1, NARROW, LATE)
        interleave_commands(3, 1, P, PIECE)
        weigh_half_planes(LAST - 1)
        for first in (4, 6):
            stage1(LAST, 0, first, first + 2)
            stage1(LAST, 1, first, first + 2)
        limit(LAST, 0)
        limit(LAST, 1)
        interleave_commands(0, 1, PIECE, COLS)

        quantize_commands(0, 0, 0, PIECE)
        quantize_commands(0, 0, PIECE, PIECE)
        quantize_h(0, 2, 2)
        quantize_h(1)
        quantize_commands(1, 0)
        stage2(0, 0, 0, PIECE)
        stage2(0, 0, PIECE, PIECE)
        for mb in (2, 3, 1):
            stage2(mb, 0)
        turn_block(LAST, 0)
        turn_block(LAST, 1)
        turn_half_planes(LAST, "turn0")
        weigh_half_planes(LAST)
        interleave_commands(2, 1, BROAD, BROAD + REST)
        quantize_h(2)
        quantize_commands(2, 0)
        interleave_last_quarter(0, P, gpsimd_move, "h_grouped2")
        weigh_block(0)
        interleave_last_half()
        interleave_commands(2, 1, BROAD + REST, COLS)
        weigh_block(1)
        quantize_commands(3, 0)
        quantize_h(3, 0, 2)
        quantize_commands(0, 1)
        interleave_commands(1, 1, LATE, PIECE, vector_move)
        quantize_h(3, 2, 2)
        quantize_commands(2, 1, 0, PIECE)
        quantize_commands(1, 1, 0, PIECE)
        quantize_commands(3, 1, 0, PIECE)
        for g in (1, 2):
            for mb in range(MODE_BLOCKS):
                stage2(mb, g)
        for mb in range(2):
            stage2(mb, 3)
            store(mb)
        quarter((0, 1), 0, (0,), "turn1")
        quarter((2, 3), 0, (0,), "acc0")
        for mb in (2, 3):
            stage2(mb, 3)
            store(mb)
        quarter((0,), 1, (0,), "turn2")
        quarter((1,), 1, (0,), "turn0")
        interleave_commands(1, 1, PIECE, COLS, vector_move)
        interleave_last_quarter(P, PIECE, vector_move)
        for g in (2, 1, 3):
            quantize_commands(g, 1, PIECE, PIECE)
        quarter((0, 1), 0, (2, 1, 3))
        store_quarter((0, 1), 0, scalar_move)
        quarter((2, 3), 0, (2, 1, 3))
        store_quarter((2, 3), 0, vector_move)
        for mb in range(2):
            quarter((mb,), 1, (2, 1, 3))
            store_quarter((mb,), 1, (scalar_move, vector_move)[mb])
        for mb in (2, 3):
            quarter((mb,), 1, (0, 1, 2, 3), ("h1", "h0")[mb - 2])
            store_quarter((mb,), 1, (scalar_move, vector_move)[mb - 2])
